import numpy as np
import ml_dtypes


def mxq(x, axis, fmt="e4m3"):
    dtype, down = {"e4m3": (ml_dtypes.float8_e4m3fn, 7), "e5m2": (ml_dtypes.float8_e5m2, 14)}[fmt]
    v = np.moveaxis(np.asarray(x, np.float32).astype(ml_dtypes.bfloat16).astype(np.float64), axis, -1)
    blocks = v.reshape(v.shape[:-1] + (-1, 32))
    amax = np.abs(blocks).max(-1, keepdims=True)
    byte = np.maximum(np.where(amax > 0, np.frexp(amax)[1] - 1 + 127, 0) - down, 1)
    scale = np.exp2(byte - 127.0)
    codes = (blocks / scale).astype(np.float32).astype(dtype).astype(np.float64)
    return np.moveaxis((codes * scale).reshape(v.shape), -1, axis)


WIDE = False


def mx_kscale(k):
    if not WIDE:
        return np.ones(k)
    levels = np.array([10, -10, 5, -5, 0])
    if k % 512:
        return np.exp2(np.random.permutation(np.resize(levels, k // 32))).repeat(32)
    a = np.empty((k // 512, 16))
    for p in range(k // 512):
        a[p, :8] = np.random.permutation(np.resize(levels, 8))
        for g in range(8):
            far = levels[np.abs(levels - a[p, g]) >= 10]
            a[p, g + 8] = far[np.random.randint(len(far))]
    return np.exp2(a.ravel()).repeat(32)


def f64(x):
    return np.asarray(x).astype(np.float64)


def striped(idx):
    return np.tile(idx.reshape(-1, 16).T, (8, 1)).astype(np.uint16)


def unstriped(offs):
    return offs[:16].T.reshape(-1).astype(np.int64)


E2M1 = np.array([0.0, 0.5, 1.0, 1.5, 2.0, 3.0, 4.0, 6.0, -0.0, -0.5, -1.0, -1.5, -2.0, -3.0, -4.0, -6.0])


def pack_weight(w, fmt):
    k, n = w.shape
    w = f64(np.asarray(w, np.float32).astype(ml_dtypes.bfloat16)).reshape(k // 32, 32, n)
    amax = np.abs(w).max(1)
    if fmt == "e4m3":
        byte = np.frexp(amax)[1] - 1 + 127 - 7
    else:
        mant, ex = np.frexp(amax / 6.0)
        byte = np.where(mant > 0.5, ex, ex - 1) + 127
    byte = np.clip(np.where(amax > 0, byte, 1), 1, 254)
    scaled = (w * np.exp2(127.0 - byte)[:, None, :]).reshape(k, n).astype(np.float32)
    by_word = np.ascontiguousarray(scaled.reshape(k // 512, 128, 4, n).transpose(0, 1, 3, 2))
    if fmt == "e4m3":
        words = by_word.astype(ml_dtypes.float8_e4m3fn).view(np.uint8)
    else:
        c = by_word.astype(ml_dtypes.float4_e2m1fn).view(np.uint8) & 0xF
        words = (c[..., 0::2] | (c[..., 1::2] << 4)).reshape(k // 512, 128, 2 * n)
    return np.ascontiguousarray(words), np.ascontiguousarray(byte.astype(np.uint8).reshape(k // 512, 16, n))


def unpack_weight(words, scales, fmt):
    g, _, n = scales.shape
    words = np.ascontiguousarray(words).reshape(g, 128, n, -1)
    if fmt == "e4m3":
        vals = words.view(ml_dtypes.float8_e4m3fn).astype(np.float64)
    else:
        nib = np.empty((g, 128, n, 4), np.uint8)
        nib[..., 0::2] = words & 0xF
        nib[..., 1::2] = words >> 4
        vals = E2M1[nib]
    vals = vals * np.repeat(np.exp2(scales.astype(np.float64) - 127.0), 8, axis=1)[..., None]
    return vals.transpose(0, 1, 3, 2).reshape(g * 512, n)


def gelu(v):
    return 0.5 * v * (1.0 + np.tanh(np.sqrt(2.0 / np.pi) * (v + 0.044715 * v**3)))


K, H, T, T2, S, P = 512, 1024, 2048, 2048, 1024, 1024

def setup_inputs():
    n = np.random.standard_normal
    s = mx_kscale(K)[:, None]
    u = mx_kscale(H)[:, None]
    tab_words, tab_scales = pack_weight(n((K, T)) * s, "e4m3")
    wc = 0.5 * n((K, H)) / np.sqrt(K) / s / u.T
    wc_words, wc_scales = pack_weight(wc, "e2m1")
    return {
        "tab_words": tab_words, "tab_scales": tab_scales,
        "offs": striped(np.random.permutation(T)[:P]),
        "offs2": striped(np.random.permutation(T2)[:S]),
        "offs3": striped(np.random.permutation(T2)[:P]),
        "xs": (np.round(16 * n((K, S))) / 16 * s).astype(np.float32),
        "base": (n((K, T2)) * s).astype(np.float32),
        "w": (n((K, H)) / np.sqrt(K) / s / u.T).astype(np.float32),
        "wc_words": wc_words, "wc_scales": wc_scales,
        "prec": (0.6 * np.exp(0.3 * n(H)) * u[:, 0] * u[:, 0]).astype(np.float32),
    }

def reference(tab_words, tab_scales, offs, offs2, offs3, xs, base, w, wc_words, wc_scales, prec):
    v = unpack_weight(tab_words, tab_scales, "e4m3")[:, unstriped(offs)]
    page = f64(base).copy()
    page[:, unstriped(offs2)] = f64(xs)
    wk = mxq(f64(w), 0, "e4m3")
    wr = mxq(f64(w).T, 0, "e4m3")
    wc = unpack_weight(wc_words, wc_scales, "e2m1")
    a = wk.T @ mxq(page, 0, "e4m3")
    b = wk.T @ v + wc.T @ v
    e = a[:, unstriped(offs3)] - b
    f = f64(prec)[:, None] * e
    d = 1.0 + f * e
    g = f / (d * d)
    out = wr.T @ mxq(g, 0, "e4m3")
    return out

@@ -1,0 +1,382 @@
+from contextlib import ExitStack
+
+import concourse.mybir as mybir
+from concourse.masks import make_identity
+
+K, H, T, S, NP = 512, 1024, 2048, 1024, 1024
+FLOPS = 2 * K * H * T + 2 * 2 * K * H * NP + 2 * H * K * NP
+
+F32 = mybir.dt.float32
+BF16 = mybir.dt.bfloat16
+I32 = mybir.dt.int32
+U32 = mybir.dt.uint32
+U16 = mybir.dt.uint16
+U8 = mybir.dt.uint8
+FP8X4 = mybir.dt.float8_e4m3fn_x4
+FP4X4 = mybir.dt.float4_e2m1fn_x4
+ACT = mybir.ActivationFunctionType
+ALU = mybir.AluOpType
+
+P = 128
+PACK = 4
+BANK = 512
+R_PASSES = H // (P * PACK)
+CHUNKS = T // BANK
+PER_COL = 16
+ALIGN = 64
+
+
+def tile_list_submap_robust_gradient_kernel(
+    tc, tab_words, tab_scales, offs, offs2, offs3, xs, base, w, wc_words, wc_scales, prec, out
+):
+    nc = tc.nc
+    with ExitStack() as ctx:
+        keep = ctx.enter_context(tc.tile_pool(name="keep", bufs=1))
+        ring = ctx.enter_context(tc.tile_pool(name="ring", bufs=1))
+        psum = ctx.enter_context(tc.psum_pool(name="psum", bufs=1))
+
+        def held(shape, dtype, name):
+            return keep.tile(shape, dtype, name=name, align_bytes=ALIGN)
+
+        def ringed(shape, dtype, tag, bufs):
+            return ring.tile(shape, dtype, name=tag, tag=tag, bufs=bufs, align_bytes=ALIGN)
+
+        def wide_tile():
+            return ringed([P, T], F32, "wide", 4)
+
+        def bf16_tile(shape):
+            return ringed(shape, BF16, "rounded", 5)
+
+        def acc_bank(shape):
+            return psum.tile(shape, F32, name="acc", tag="acc", bufs=4)
+
+        def out_bank(shape):
+            return psum.tile(shape, F32, name="fin", tag="fin", bufs=4)
+
+        list_tab = held([P, NP // PER_COL], U16, "list_tab")
+        list_page = held([P, S // PER_COL], U16, "list_page")
+        list_pair = held([P, NP // PER_COL], U16, "list_pair")
+
+        tab_s = held([P, T], U8, "tab_s")
+        wc_s_raw = held([P, H], U8, "wc_s_raw")
+        prec_rows = held([P, P], F32, "prec_rows")
+        ident = held([P, P], F32, "ident")
+        warm = held([P, 2], F32, "warm")
+        nc.vector.memset(tab_s[:].bitcast(I32), 0)
+        nc.gpsimd.memset(warm[:, 0:1], 1.0)
+        nc.gpsimd.memset(wc_s_raw[:].bitcast(I32), 0)
+        nc.gpsimd.memset(prec_rows[:], 0.0)
+        make_identity(nc, ident[:])
+
+        base_v = base.rearrange("(p j) t -> p j t", j=PACK)
+        xs_v = xs.rearrange("(p j) m -> p j m", j=PACK)
+        w_v = w.rearrange("(p j) r -> p j r", j=PACK)
+        out_v = out.rearrange("(p j) c -> p j c", j=PACK)
+
+        page = []
+        scan = []
+        w_flat = ringed([P, PACK * H], F32, "w_then_pairs", 1)
+        w_raw = [
+            w_flat[:, b * PACK * BANK : (b + 1) * PACK * BANK].rearrange("p (j r) -> p j r", j=PACK)
+            for b in range(R_PASSES)
+        ]
+
+        def load_plane(j):
+            page.append(wide_tile())
+            if j + 1 < PACK:
+                scan.append(ringed([P, S], F32, "mid", 4))
+            else:
+                scan.append(ringed([P, S], F32, "scan_then_wr", 1))
+            nc.sync.dma_start(page[j][:], base_v[:, j, :])
+            nc.sync.dma_start(scan[j][:], xs_v[:, j, :])
+
+        def load_w(b):
+            nc.sync.dma_start(w_raw[b], w_v[:, :, b * BANK : (b + 1) * BANK])
+
+        tab_w = ringed([P, T], I32, "stage", 2)
+        wc_w_raw = held([P, 2 * H // 4], I32, "wc_w_raw")
+
+        nc.sync.dma_start(list_tab[:], offs)
+        for q in range(4):
+            nc.scalar.dma_start(tab_s[32 * q : 32 * q + 4, :].bitcast(I32), tab_scales[0, 4 * q : 4 * q + 4, :].bitcast(I32))
+        nc.scalar.activation(warm[:, 1:2], warm[:, 0:1], ACT.Abs_reciprocal_sqrt)
+        nc.sync.dma_start(list_page[:], offs2)
+        load_plane(0)
+        load_w(0)
+        load_w(1)
+        nc.sync.dma_start(tab_w[:], tab_words[0].rearrange("p t i -> p (t i)").bitcast(I32))
+        nc.sync.dma_start(wc_w_raw[:], wc_words[0].bitcast(I32))
+        for q in range(4):
+            nc.sync.dma_start(wc_s_raw[32 * q : 32 * q + 4, :].bitcast(I32), wc_scales[0, 4 * q : 4 * q + 4, :].bitcast(I32))
+        load_plane(1)
+        load_plane(2)
+        load_plane(3)
+        for b in range(R_PASSES):
+            nc.sync.dma_start(
+                prec_rows[PACK * b : PACK * (b + 1), :].rearrange("t (g i) -> t g i", i=8),
+                prec[b * BANK : (b + 1) * BANK].rearrange("(g t i) -> t g i", t=PACK, i=8),
+            )
+        nc.sync.dma_start(list_pair[:], offs3)
+
+
+        def scatter(j):
+            nc.vector.tensor_copy(page[j][:].indirect(list_page[:]), scan[j][:])
+
+        def round_plane(j):
+            for c in range(CHUNKS):
+                slots = pairs[c].rearrange("p (u n e) -> p u n e", u=2, e=2)
+                nc.scalar.copy(slots[:, j // 2, :, j % 2], page[j][:, c * BANK : (c + 1) * BANK])
+
+        wk_bf = []
+        wk_c = [held([P, BANK], U32, f"wk_c{b}") for b in range(R_PASSES)]
+        wk_s = [held([P, BANK], U8, f"wk_s{b}") for b in range(R_PASSES)]
+        wr_s = [held([P, BANK], U8, f"wr_s{b}") for b in range(R_PASSES)]
+
+        def round_w(b):
+            wk_bf.append(bf16_tile([P, BANK * PACK]))
+            nc.scalar.copy(
+                wk_bf[b][:].rearrange("p (t g i j) -> p g t j i", t=PACK, i=8, j=PACK),
+                w_raw[b].rearrange("p j (g t i) -> p g t j i", t=PACK, i=8),
+            )
+
+        def quantize(codes, scales, rounded):
+            nc.vector.quantize_mx(out=codes.bitcast(FP8X4), scales=scales, in_=rounded)
+
+        wr_bf = []
+
+        def turn_w(b):
+            wr_bf.append(bf16_tile([P, BANK * PACK]))
+            words = wk_bf[b][:].bitcast(F32)
+            for u in range(2):
+                bank = acc_bank([P, BANK])
+                for t in range(PACK):
+                    nc.tensor.transpose(
+                        bank[:, t * P : (t + 1) * P], words[:, 2 * P * t + u : 2 * P * (t + 1) : 2], ident[:]
+                    )
+                nc.scalar.copy(
+                    wr_bf[b][:, u * 2 * BANK : (u + 1) * 2 * BANK].rearrange("m (e p t) -> m e p t", e=2, t=PACK),
+                    bank[:].bitcast(BF16).rearrange("m (t p e) -> m e p t", t=PACK, e=2),
+                )
+
+        v_c = held([P, NP], U32, "v_c")
+        v_s = held([P, NP], U8, "v_s")
+        wc_w = held([P, 2 * H // 4], I32, "wc_w")
+        wc_s = held([P, H], U8, "wc_s")
+        b_sb = [held([P, NP], F32, f"b_sb{i}") for i in range(R_PASSES * PACK)]
+
+        nc.vector.tensor_copy(v_s[:], tab_s[:].indirect(list_tab[:]))
+        scatter(0)
+        round_w(0)
+        round_w(1)
+        pairs_flat = ringed([P, T * PACK], BF16, "w_then_pairs", 1)
+        pairs = [pairs_flat[:, c * BANK * PACK : (c + 1) * BANK * PACK] for c in range(CHUNKS)]
+        round_plane(0)
+        quantize(wk_c[0][:], wk_s[0][:], wk_bf[0][:])
+        nc.vector.tensor_copy(v_c[:], tab_w[:].bitcast(U32).indirect(list_tab[:]))
+        quantize(wk_c[1][:], wk_s[1][:], wk_bf[1][:])
+        nc.vector.tensor_copy(
+            wc_w[:].rearrange("p (b t g x) -> p b t g x", b=R_PASSES, t=PACK, x=4),
+            wc_w_raw[:].rearrange("p (b g t x) -> p b t g x", b=R_PASSES, t=PACK, x=4),
+        )
+        nc.vector.tensor_copy(
+            wc_s[:].bitcast(I32).rearrange("p (b t g x) -> p b t g x", b=R_PASSES, t=PACK, x=2),
+            wc_s_raw[:].bitcast(I32).rearrange("p (b g t x) -> p b t g x", b=R_PASSES, t=PACK, x=2),
+        )
+        turn_w(0)
+        turn_w(1)
+        scatter(1)
+        scatter(2)
+
+        wc_bytes = wc_w[:].bitcast(U8)
+        for i in range(R_PASSES * PACK):
+            b, t = divmod(i, PACK)
+            for h in range(NP // BANK):
+                cols = slice(h * BANK, (h + 1) * BANK)
+                bank = acc_bank([P, BANK])
+                nc.tensor.matmul_mx(
+                    out=bank[:],
+                    lhsT=wk_c[b][:, t * P : (t + 1) * P].bitcast(FP8X4),
+                    lhsT_scale=wk_s[b][:, t * P : (t + 1) * P],
+                    rhs=v_c[:, cols].bitcast(FP8X4),
+                    rhs_scale=v_s[:, cols],
+                    start=True,
+                    stop=False,
+                )
+                nc.tensor.matmul_mx(
+                    out=bank[:],
+                    lhsT=wc_bytes[:, 2 * P * i : 2 * P * (i + 1)].bitcast(FP4X4),
+                    lhsT_scale=wc_s[:, P * i : P * (i + 1)],
+                    rhs=v_c[:, cols].bitcast(FP8X4),
+                    rhs_scale=v_s[:, cols],
+                    start=False,
+                    stop=True,
+                )
+                nc.scalar.copy(b_sb[i][:, cols], bank[:])
+
+
+        prec_col = held([P, R_PASSES * PACK], F32, "prec_col")
+        prec_inv = held([P, R_PASSES * PACK], F32, "prec_inv")
+        bank = acc_bank([P, BANK])
+        nc.tensor.transpose(bank[:, 0:P], prec_rows[:], ident[:])
+        nc.scalar.copy(prec_col[:], bank[:, 0 : R_PASSES * PACK])
+        nc.vector.reciprocal(prec_inv[:], prec_col[:])
+
+        round_plane(1)
+        round_plane(2)
+        scatter(3)
+        round_plane(3)
+
+        page_c = [held([P, BANK], U32, f"page_c{c}") for c in range(CHUNKS)]
+        page_s = [held([P, BANK], U8, f"page_s{c}") for c in range(CHUNKS)]
+        woven = []
+
+        def weave(c):
+            woven.append(bf16_tile([P, BANK * PACK]))
+            nc.vector.tensor_copy(
+                woven[c][:].bitcast(F32).rearrange("p (n u) -> p n u", u=2),
+                pairs[c].bitcast(F32).rearrange("p (u n) -> p n u", u=2),
+            )
+
+        weave(0)
+        for c in range(CHUNKS):
+            if c + 1 < CHUNKS:
+                weave(c + 1)
+            quantize(page_c[c][:], page_s[c][:], woven[c][:])
+
+        wr_flat = ringed([P, R_PASSES * BANK], U32, "scan_then_wr", 1)
+        wr_c = [wr_flat[:, b * BANK : (b + 1) * BANK] for b in range(R_PASSES)]
+        for b in range(R_PASSES):
+            quantize(wr_c[b], wr_s[b][:], wr_bf[b][:])
+
+        a_sb = {}
+
+        def project(i, c):
+            b, t = divmod(i, PACK)
+            if i not in a_sb:
+                a_sb[i] = wide_tile()
+            bank = acc_bank([P, BANK])
+            nc.tensor.matmul_mx(
+                out=bank[:],
+                lhsT=wk_c[b][:, t * P : (t + 1) * P].bitcast(FP8X4),
+                lhsT_scale=wk_s[b][:, t * P : (t + 1) * P],
+                rhs=page_c[c][:].bitcast(FP8X4),
+                rhs_scale=page_s[c][:],
+                start=True,
+                stop=True,
+            )
+            dst = a_sb[i][:, c * BANK : (c + 1) * BANK]
+            if c == 0:
+                nc.vector.tensor_copy(dst, bank[:])
+            else:
+                nc.scalar.copy(dst, bank[:])
+
+        resid = {}
+        weight = {}
+        g_c = {}
+        g_s = {}
+
+        def residual(unit, t):
+            b, lo, n = unit
+            i = b * PACK + t
+            if unit not in resid:
+                resid[unit] = ringed([P, PACK, n], F32, "resid", 4)
+                weight[unit] = ringed([P, PACK, n], F32, "mid", 4)
+            e = resid[unit][:, t, :]
+            z = weight[unit][:, t, :]
+            nc.vector.tensor_tensor(
+                e, a_sb[i][:].indirect(list_pair[:, lo // PER_COL : (lo + n) // PER_COL]), b_sb[i][:, lo : lo + n], ALU.subtract
+            )
+            return e, z, i
+
+        def square(e, z):
+            nc.vector.tensor_tensor(z, e, e, ALU.mult)
+
+        def weigh(z, i):
+            nc.scalar.activation(z, z, ACT.Square, bias=1.0, scale=prec_col[:, i : i + 1])
+            nc.scalar.activation(z, z, ACT.Abs_reciprocal_sqrt, scale=prec_inv[:, i : i + 1])
+            nc.scalar.activation(z, z, ACT.Square)
+
+        def finish(unit):
+            b, lo, n = unit
+            g_bf = bf16_tile([P, n * PACK])
+            nc.vector.tensor_tensor(
+                g_bf[:].rearrange("p (c i t) -> p c t i", i=4, t=PACK),
+                resid[unit][:].rearrange("p t (c i) -> p c t i", i=4),
+                weight[unit][:].rearrange("p t (c i) -> p c t i", i=4),
+                ALU.mult,
+            )
+            g_c[unit] = held([P, n], U32, f"g_c{b}_{lo}")
+            g_s[unit] = held([P, n], U8, f"g_s{b}_{lo}")
+            quantize(g_c[unit][:], g_s[unit][:], g_bf[:])
+
+        def back_pass(banks, unit, lo, n):
+            b = unit[0]
+            cols = slice(lo - unit[1], lo - unit[1] + n)
+            for j in range(PACK):
+                nc.tensor.matmul_mx(
+                    out=banks[j][:, 0:n],
+                    lhsT=wr_c[b][:, j * P : (j + 1) * P].bitcast(FP8X4),
+                    lhsT_scale=wr_s[b][:, j * P : (j + 1) * P],
+                    rhs=g_c[unit][:, cols].bitcast(FP8X4),
+                    rhs_scale=g_s[unit][:, cols],
+                    start=(b == 0),
+                    stop=(b == R_PASSES - 1),
+                )
+
+        def store(banks, lo, n):
+            staged = ringed([P, PACK, n], F32, "stage", 2)
+            for j in range(PACK):
+                if j % 2 == 0:
+                    nc.scalar.copy(staged[:, j, :], banks[j][:, 0:n])
+                else:
+                    nc.vector.tensor_copy(staged[:, j, :], banks[j][:, 0:n])
+                    nc.sync.dma_start(out_v[:, j - 1 : j + 1, lo : lo + n], staged[:, j - 1 : j + 1, :])
+
+        first = [(0, 0, BANK), (0, BANK, BANK)]
+        second = [(1, 0, BANK), (1, BANK, BANK // 2), (1, BANK + BANK // 2, BANK // 2)]
+
+        for c in range(CHUNKS):
+            project(0, c)
+            project(1, c)
+        for t in range(PACK):
+            steps = [residual(unit, t) for unit in first]
+            for e, z, i in steps:
+                square(e, z)
+            for c in range(CHUNKS):
+                project(t + 2, c)
+            for e, z, i in steps:
+                weigh(z, i)
+        for t in range(PACK):
+            e, z, i = residual(second[0], t)
+            if t < 2:
+                finish(first[t])
+            square(e, z)
+            if t < 2:
+                for c in range(CHUNKS):
+                    project(PACK + t + 2, c)
+            weigh(z, i)
+        banks0 = [out_bank([P, BANK]) for j in range(PACK)]
+        back_pass(banks0, first[0], 0, BANK)
+        for t in range(PACK):
+            e, z, i = residual(second[1], t)
+            if t == 1:
+                finish(second[0])
+                back_pass(banks0, second[0], 0, BANK)
+            square(e, z)
+            weigh(z, i)
+        banks1 = [acc_bank([P, BANK]) for j in range(PACK)]
+        back_pass(banks1, first[1], BANK, BANK // 2)
+        store(banks0, 0, BANK)
+        for t in range(PACK):
+            e, z, i = residual(second[2], t)
+            if t == 1:
+                finish(second[1])
+                back_pass(banks1, second[1], BANK, BANK // 2)
+            square(e, z)
+            weigh(z, i)
+        banks2 = [out_bank([P, BANK]) for j in range(PACK)]
+        back_pass(banks2, first[1], BANK + BANK // 2, BANK // 2)
+        store(banks1, BANK, BANK // 2)
+        finish(second[2])
+        back_pass(banks2, second[2], BANK + BANK // 2, BANK // 2)
+        store(banks2, BANK + BANK // 2, BANK // 2)

@@ -42,10 +42,10 @@ def tile_list_submap_robust_gradient_kernel(
             return ring.tile(shape, dtype, name=tag, tag=tag, bufs=bufs, align_bytes=ALIGN)
 
         def wide_tile():
-            return ringed([P, T], F32, "wide", 4)
+            return ringed([P, T], F32, "wide", 6)
 
         def bf16_tile(shape):
-            return ringed(shape, BF16, "rounded", 5)
+            return ringed(shape, BF16, "rounded", 4)
 
         def acc_bank(shape):
             return psum.tile(shape, F32, name="acc", tag="acc", bufs=4)
@@ -62,7 +62,7 @@ def tile_list_submap_robust_gradient_kernel(
         prec_rows = held([P, P], F32, "prec_rows")
         ident = held([P, P], F32, "ident")
         warm = held([P, 2], F32, "warm")
-        nc.vector.memset(tab_s[:].bitcast(I32), 0)
+        nc.gpsimd.memset(tab_s[:].bitcast(I32), 0)
         nc.gpsimd.memset(warm[:, 0:1], 1.0)
         nc.gpsimd.memset(wc_s_raw[:].bitcast(I32), 0)
         nc.gpsimd.memset(prec_rows[:], 0.0)
@@ -83,10 +83,7 @@ def tile_list_submap_robust_gradient_kernel(
 
         def load_plane(j):
             page.append(wide_tile())
-            if j + 1 < PACK:
-                scan.append(ringed([P, S], F32, "mid", 4))
-            else:
-                scan.append(ringed([P, S], F32, "scan_then_wr", 1))
+            scan.append(ringed([P, S], F32, "scan", 4))
             nc.sync.dma_start(page[j][:], base_v[:, j, :])
             nc.sync.dma_start(scan[j][:], xs_v[:, j, :])
 
@@ -98,7 +95,7 @@ def tile_list_submap_robust_gradient_kernel(
 
         nc.sync.dma_start(list_tab[:], offs)
         for q in range(4):
-            nc.scalar.dma_start(tab_s[32 * q : 32 * q + 4, :].bitcast(I32), tab_scales[0, 4 * q : 4 * q + 4, :].bitcast(I32))
+            nc.sync.dma_start(tab_s[32 * q : 32 * q + 4, :].bitcast(I32), tab_scales[0, 4 * q : 4 * q + 4, :].bitcast(I32))
         nc.scalar.activation(warm[:, 1:2], warm[:, 0:1], ACT.Abs_reciprocal_sqrt)
         nc.sync.dma_start(list_page[:], offs2)
         load_plane(0)
@@ -145,15 +142,19 @@ def tile_list_submap_robust_gradient_kernel(
         wr_bf = []
 
         def turn_w(b):
-            wr_bf.append(bf16_tile([P, BANK * PACK]))
+            if b == 0:
+                wr_bf.append(bf16_tile([P, BANK * PACK]))
+            else:
+                wr_bf.append(ringed([P, BANK * PACK], BF16, "woven_then_wr", 1))
+            copy = nc.scalar.copy if b == 0 else nc.vector.tensor_copy
             words = wk_bf[b][:].bitcast(F32)
             for u in range(2):
-                bank = acc_bank([P, BANK])
+                bank = out_bank([P, BANK])
                 for t in range(PACK):
                     nc.tensor.transpose(
                         bank[:, t * P : (t + 1) * P], words[:, 2 * P * t + u : 2 * P * (t + 1) : 2], ident[:]
                     )
-                nc.scalar.copy(
+                copy(
                     wr_bf[b][:, u * 2 * BANK : (u + 1) * 2 * BANK].rearrange("m (e p t) -> m e p t", e=2, t=PACK),
                     bank[:].bitcast(BF16).rearrange("m (t p e) -> m e p t", t=PACK, e=2),
                 )
@@ -183,7 +184,6 @@ def tile_list_submap_robust_gradient_kernel(
             wc_s_raw[:].bitcast(I32).rearrange("p (b g t x) -> p b t g x", b=R_PASSES, t=PACK, x=2),
         )
         turn_w(0)
-        turn_w(1)
         scatter(1)
         scatter(2)
 
@@ -231,7 +231,12 @@ def tile_list_submap_robust_gradient_kernel(
         woven = []
 
         def weave(c):
-            woven.append(bf16_tile([P, BANK * PACK]))
+            if c == CHUNKS - 1:
+                woven.append(ringed([P, BANK * PACK], BF16, "woven_then_wr", 1))
+            elif c == CHUNKS - 2:
+                woven.append(ringed([P, BANK * PACK], BF16, "woven_then_codes", 1))
+            else:
+                woven.append(bf16_tile([P, BANK * PACK]))
             nc.vector.tensor_copy(
                 woven[c][:].bitcast(F32).rearrange("p (n u) -> p n u", u=2),
                 pairs[c].bitcast(F32).rearrange("p (u n) -> p n u", u=2),
@@ -243,14 +248,15 @@ def tile_list_submap_robust_gradient_kernel(
                 weave(c + 1)
             quantize(page_c[c][:], page_s[c][:], woven[c][:])
 
-        wr_flat = ringed([P, R_PASSES * BANK], U32, "scan_then_wr", 1)
+        turn_w(1)
+        wr_flat = ringed([P, R_PASSES * BANK], U32, "woven_then_codes", 1)
         wr_c = [wr_flat[:, b * BANK : (b + 1) * BANK] for b in range(R_PASSES)]
         for b in range(R_PASSES):
             quantize(wr_c[b], wr_s[b][:], wr_bf[b][:])
 
         a_sb = {}
 
-        def project(i, c):
+        def project(i, c, on_vector):
             b, t = divmod(i, PACK)
             if i not in a_sb:
                 a_sb[i] = wide_tile()
@@ -265,7 +271,7 @@ def tile_list_submap_robust_gradient_kernel(
                 stop=True,
             )
             dst = a_sb[i][:, c * BANK : (c + 1) * BANK]
-            if c == 0:
+            if on_vector:
                 nc.vector.tensor_copy(dst, bank[:])
             else:
                 nc.scalar.copy(dst, bank[:])
@@ -279,8 +285,8 @@ def tile_list_submap_robust_gradient_kernel(
             b, lo, n = unit
             i = b * PACK + t
             if unit not in resid:
-                resid[unit] = ringed([P, PACK, n], F32, "resid", 4)
-                weight[unit] = ringed([P, PACK, n], F32, "mid", 4)
+                resid[unit] = ringed([P, PACK, n], F32, "resid", 2)
+                weight[unit] = ringed([P, PACK, n], F32, "weight", 2)
             e = resid[unit][:, t, :]
             z = weight[unit][:, t, :]
             nc.vector.tensor_tensor(
@@ -288,15 +294,24 @@ def tile_list_submap_robust_gradient_kernel(
             )
             return e, z, i
 
-        def square(e, z):
-            nc.vector.tensor_tensor(z, e, e, ALU.mult)
+        def square(e, z, on_vector):
+            if on_vector:
+                nc.vector.tensor_tensor(z, e, e, ALU.mult)
+            else:
+                nc.scalar.activation(z, e, ACT.Square)
 
-        def weigh(z, i):
+        def denominator(z, i):
             nc.scalar.activation(z, z, ACT.Square, bias=1.0, scale=prec_col[:, i : i + 1])
+
+        def invert(z, i):
             nc.scalar.activation(z, z, ACT.Abs_reciprocal_sqrt, scale=prec_inv[:, i : i + 1])
+
+        def resquare(z):
             nc.scalar.activation(z, z, ACT.Square)
 
-        def finish(unit):
+        g_round = {}
+
+        def weigh(unit):
             b, lo, n = unit
             g_bf = bf16_tile([P, n * PACK])
             nc.vector.tensor_tensor(
@@ -305,6 +320,11 @@ def tile_list_submap_robust_gradient_kernel(
                 weight[unit][:].rearrange("p t (c i) -> p c t i", i=4),
                 ALU.mult,
             )
+            g_round[unit] = g_bf
+
+        def finish(unit):
+            b, lo, n = unit
+            g_bf = g_round[unit]
             g_c[unit] = held([P, n], U32, f"g_c{b}_{lo}")
             g_s[unit] = held([P, n], U8, f"g_s{b}_{lo}")
             quantize(g_c[unit][:], g_s[unit][:], g_bf[:])
@@ -323,60 +343,66 @@ def tile_list_submap_robust_gradient_kernel(
                     stop=(b == R_PASSES - 1),
                 )
 
-        def store(banks, lo, n):
+        def store(banks, lo, n, shared):
             staged = ringed([P, PACK, n], F32, "stage", 2)
             for j in range(PACK):
-                if j % 2 == 0:
-                    nc.scalar.copy(staged[:, j, :], banks[j][:, 0:n])
-                else:
+                if shared and j % 2 == 1:
                     nc.vector.tensor_copy(staged[:, j, :], banks[j][:, 0:n])
+                else:
+                    nc.scalar.copy(staged[:, j, :], banks[j][:, 0:n])
+                if j % 2 == 1:
                     nc.sync.dma_start(out_v[:, j - 1 : j + 1, lo : lo + n], staged[:, j - 1 : j + 1, :])
 
-        first = [(0, 0, BANK), (0, BANK, BANK)]
-        second = [(1, 0, BANK), (1, BANK, BANK // 2), (1, BANK + BANK // 2, BANK // 2)]
-
+        half = BANK // 2
+        units = [(0, 0, BANK), (0, BANK, BANK), (1, 0, BANK), (1, BANK, half), (1, BANK + half, half)]
+        ahead = 2
         for c in range(CHUNKS):
-            project(0, c)
-            project(1, c)
-        for t in range(PACK):
-            steps = [residual(unit, t) for unit in first]
-            for e, z, i in steps:
-                square(e, z)
-            for c in range(CHUNKS):
-                project(t + 2, c)
-            for e, z, i in steps:
-                weigh(z, i)
-        for t in range(PACK):
-            e, z, i = residual(second[0], t)
-            if t < 2:
-                finish(first[t])
-            square(e, z)
-            if t < 2:
-                for c in range(CHUNKS):
-                    project(PACK + t + 2, c)
-            weigh(z, i)
-        banks0 = [out_bank([P, BANK]) for j in range(PACK)]
-        back_pass(banks0, first[0], 0, BANK)
-        for t in range(PACK):
-            e, z, i = residual(second[1], t)
-            if t == 1:
-                finish(second[0])
-                back_pass(banks0, second[0], 0, BANK)
-            square(e, z)
-            weigh(z, i)
-        banks1 = [acc_bank([P, BANK]) for j in range(PACK)]
-        back_pass(banks1, first[1], BANK, BANK // 2)
-        store(banks0, 0, BANK)
-        for t in range(PACK):
-            e, z, i = residual(second[2], t)
-            if t == 1:
-                finish(second[1])
-                back_pass(banks1, second[1], BANK, BANK // 2)
-            square(e, z)
-            weigh(z, i)
-        banks2 = [out_bank([P, BANK]) for j in range(PACK)]
-        back_pass(banks2, first[1], BANK + BANK // 2, BANK // 2)
-        store(banks1, BANK, BANK // 2)
-        finish(second[2])
-        back_pass(banks2, second[2], BANK + BANK // 2, BANK // 2)
-        store(banks2, BANK + BANK // 2, BANK // 2)
+            for i in range(ahead):
+                project(i, c, False)
+        later = [(i, c) for i in range(ahead, R_PASSES * PACK) for c in range(CHUNKS)]
+        per_step = [4, 4, 2, 2, 2, 2, 2, 2, 2, 2]
+        on_vector = 6
+        emptied = 0
+        banks = {}
+        steps = [(k, t) for k in range(len(units)) for t in range(PACK)]
+        state = {}
+        for step in range(len(steps) + 2):
+            if step < len(steps):
+                k, t = steps[step]
+                state[step] = residual(units[k], t)
+                if k > 0:
+                    done = units[k - 1]
+                    if t == 2:
+                        weigh(done)
+                    if t == 3:
+                        finish(done)
+                        if k > 2:
+                            back_pass(banks[k - 1], done, done[1], done[2])
+                if k > 3 and t == 0:
+                    store(banks[k - 2], units[k - 2][1], units[k - 2][2], False)
+            if 1 <= step <= len(steps):
+                e, z, i = state[step - 1]
+                square(e, z, step - 1 != 9)
+            if step < len(per_step):
+                for i, c in later[emptied : emptied + per_step[step]]:
+                    project(i, c, (i, c) in later[2 * CHUNKS : 2 * CHUNKS + on_vector])
+                emptied = emptied + per_step[step]
+            if step >= 2:
+                e, z, i = state[step - 2]
+                invert(z, i)
+            if 1 <= step <= len(steps):
+                e, z, i = state[step - 1]
+                denominator(z, i)
+            if step >= 2:
+                resquare(state[step - 2][1])
+            if step < len(steps) and t == 3 and 0 < k < len(units) - 1:
+                follow = units[k + 1]
+                make = out_bank if k % 2 == 1 else acc_bank
+                banks[k + 1] = [make([P, BANK]) for j in range(PACK)]
+                back_pass(banks[k + 1], units[follow[1] // BANK], follow[1], follow[2])
+        last = units[-1]
+        weigh(last)
+        store(banks[len(units) - 2], units[-2][1], units[-2][2], False)
+        finish(last)
+        back_pass(banks[len(units) - 1], last, last[1], last[2])
+        store(banks[len(units) - 1], last[1], last[2], True)

@@ -83,14 +83,17 @@ def tile_list_submap_robust_gradient_kernel(
 
         def load_plane(j):
             page.append(wide_tile())
-            scan.append(ringed([P, S], F32, "scan", 4))
+            scan.append(ringed([P, S], F32, "weight", 3))
             nc.sync.dma_start(page[j][:], base_v[:, j, :])
-            nc.sync.dma_start(scan[j][:], xs_v[:, j, :])
+            parts = 2 if j < 2 else 1
+            for h in range(parts):
+                cols = slice(h * S // parts, (h + 1) * S // parts)
+                nc.sync.dma_start(scan[j][:, cols], xs_v[:, j, cols])
 
         def load_w(b):
             nc.sync.dma_start(w_raw[b], w_v[:, :, b * BANK : (b + 1) * BANK])
 
-        tab_w = ringed([P, T], I32, "stage", 2)
+        tab_w = ringed([P, T], I32, "stage", 3)
         wc_w_raw = held([P, 2 * H // 4], I32, "wc_w_raw")
 
         nc.sync.dma_start(list_tab[:], offs)
@@ -117,7 +120,10 @@ def tile_list_submap_robust_gradient_kernel(
 
 
         def scatter(j):
-            nc.vector.tensor_copy(page[j][:].indirect(list_page[:]), scan[j][:])
+            parts = 2 if j < 2 else 1
+            for h in range(parts):
+                lo, hi = h * S // parts, (h + 1) * S // parts
+                nc.vector.tensor_copy(page[j][:].indirect(list_page[:, lo // PER_COL : hi // PER_COL]), scan[j][:, lo:hi])
 
         def round_plane(j):
             for c in range(CHUNKS):
@@ -285,8 +291,8 @@ def tile_list_submap_robust_gradient_kernel(
             b, lo, n = unit
             i = b * PACK + t
             if unit not in resid:
-                resid[unit] = ringed([P, PACK, n], F32, "resid", 2)
-                weight[unit] = ringed([P, PACK, n], F32, "weight", 2)
+                resid[unit] = ringed([P, PACK, n], F32, "resid", 3)
+                weight[unit] = ringed([P, PACK, n], F32, "weight", 3)
             e = resid[unit][:, t, :]
             z = weight[unit][:, t, :]
             nc.vector.tensor_tensor(
@@ -329,29 +335,42 @@ def tile_list_submap_robust_gradient_kernel(
             g_s[unit] = held([P, n], U8, f"g_s{b}_{lo}")
             quantize(g_c[unit][:], g_s[unit][:], g_bf[:])
 
-        def back_pass(banks, unit, lo, n):
+        def back_pass(dst, j, unit, lo, n):
             b = unit[0]
             cols = slice(lo - unit[1], lo - unit[1] + n)
-            for j in range(PACK):
-                nc.tensor.matmul_mx(
-                    out=banks[j][:, 0:n],
-                    lhsT=wr_c[b][:, j * P : (j + 1) * P].bitcast(FP8X4),
-                    lhsT_scale=wr_s[b][:, j * P : (j + 1) * P],
-                    rhs=g_c[unit][:, cols].bitcast(FP8X4),
-                    rhs_scale=g_s[unit][:, cols],
-                    start=(b == 0),
-                    stop=(b == R_PASSES - 1),
-                )
+            nc.tensor.matmul_mx(
+                out=dst,
+                lhsT=wr_c[b][:, j * P : (j + 1) * P].bitcast(FP8X4),
+                lhsT_scale=wr_s[b][:, j * P : (j + 1) * P],
+                rhs=g_c[unit][:, cols].bitcast(FP8X4),
+                rhs_scale=g_s[unit][:, cols],
+                start=(b == 0),
+                stop=(b == R_PASSES - 1),
+            )
 
-        def store(banks, lo, n, shared):
-            staged = ringed([P, PACK, n], F32, "stage", 2)
+        def back_project(unit, make_bank):
+            b, lo, n = unit
+            per_bank = BANK // n
+            banks = [make_bank([P, BANK]) for x in range(PACK // per_bank)]
             for j in range(PACK):
-                if shared and j % 2 == 1:
-                    nc.vector.tensor_copy(staged[:, j, :], banks[j][:, 0:n])
+                dst = banks[j // per_bank][:, (j % per_bank) * n : (j % per_bank + 1) * n]
+                back_pass(dst, j, units[lo // BANK], lo, n)
+                back_pass(dst, j, unit, lo, n)
+            return banks
+
+        def store(banks, unit, engines):
+            b, lo, n = unit
+            per_bank = BANK // n
+            staged = ringed([P, PACK * n], F32, "stage", 3)
+            for x, bank in enumerate(banks):
+                part = staged[:, x * BANK : (x + 1) * BANK]
+                if engines[x] == "v":
+                    nc.vector.tensor_copy(part, bank[:])
                 else:
-                    nc.scalar.copy(staged[:, j, :], banks[j][:, 0:n])
-                if j % 2 == 1:
-                    nc.sync.dma_start(out_v[:, j - 1 : j + 1, lo : lo + n], staged[:, j - 1 : j + 1, :])
+                    nc.scalar.copy(part, bank[:])
+                nc.sync.dma_start(
+                    out_v[:, x * per_bank : (x + 1) * per_bank, lo : lo + n], part.rearrange("p (j c) -> p j c", c=n)
+                )
 
         half = BANK // 2
         units = [(0, 0, BANK), (0, BANK, BANK), (1, 0, BANK), (1, BANK, half), (1, BANK + half, half)]
@@ -361,7 +380,7 @@ def tile_list_submap_robust_gradient_kernel(
                 project(i, c, False)
         later = [(i, c) for i in range(ahead, R_PASSES * PACK) for c in range(CHUNKS)]
         per_step = [4, 4, 2, 2, 2, 2, 2, 2, 2, 2]
-        on_vector = 6
+        on_vector = 0
         emptied = 0
         banks = {}
         steps = [(k, t) for k in range(len(units)) for t in range(PACK)]
@@ -377,9 +396,9 @@ def tile_list_submap_robust_gradient_kernel(
                     if t == 3:
                         finish(done)
                         if k > 2:
-                            back_pass(banks[k - 1], done, done[1], done[2])
-                if k > 3 and t == 0:
-                    store(banks[k - 2], units[k - 2][1], units[k - 2][2], False)
+                            banks[k - 1] = back_project(done, out_bank if k == 3 else acc_bank)
+                if k == 4 and t == 0 and False:
+                    store(banks[2], units[2], "undefined")
             if 1 <= step <= len(steps):
                 e, z, i = state[step - 1]
                 square(e, z, step - 1 != 9)
@@ -395,14 +414,9 @@ def tile_list_submap_robust_gradient_kernel(
                 denominator(z, i)
             if step >= 2:
                 resquare(state[step - 2][1])
-            if step < len(steps) and t == 3 and 0 < k < len(units) - 1:
-                follow = units[k + 1]
-                make = out_bank if k % 2 == 1 else acc_bank
-                banks[k + 1] = [make([P, BANK]) for j in range(PACK)]
-                back_pass(banks[k + 1], units[follow[1] // BANK], follow[1], follow[2])
         last = units[-1]
         weigh(last)
-        store(banks[len(units) - 2], units[-2][1], units[-2][2], False)
         finish(last)
-        back_pass(banks[len(units) - 1], last, last[1], last[2])
-        store(banks[len(units) - 1], last[1], last[2], True)
+        banks[len(units) - 1] = back_project(last, acc_bank)
+        for k in range(2, len(units)):
+            store(banks[k], units[k], ["ssss","vv","sv"][k - 2])

@@ -19,11 +19,22 @@ ALU = mybir.AluOpType
 
 P = 128
 PACK = 4
+RUN = 8
+QUADRANT = 32
 BANK = 512
 R_PASSES = H // (P * PACK)
+ROW_TILES = R_PASSES * PACK
 CHUNKS = T // BANK
 PER_COL = 16
+LINE = 4
 ALIGN = 64
+
+WIDE_BUFS = 6
+ROUNDED_BUFS = 4
+UNIT_BUFS = 3
+STAGE_BUFS = 3
+HALF_PSUM = 4
+FIRST_TILES = 2
 
 
 def tile_list_submap_robust_gradient_kernel(
@@ -42,16 +53,26 @@ def tile_list_submap_robust_gradient_kernel(
             return ring.tile(shape, dtype, name=tag, tag=tag, bufs=bufs, align_bytes=ALIGN)
 
         def wide_tile():
-            return ringed([P, T], F32, "wide", 6)
+            return ringed([P, T], F32, "wide", WIDE_BUFS)
 
-        def bf16_tile(shape):
-            return ringed(shape, BF16, "rounded", 4)
+        def rounded_tile(columns):
+            return ringed([P, columns * PACK], BF16, "rounded", ROUNDED_BUFS)
 
-        def acc_bank(shape):
-            return psum.tile(shape, F32, name="acc", tag="acc", bufs=4)
+        def stream_bank():
+            return psum.tile([P, BANK], F32, name="stream", tag="stream", bufs=HALF_PSUM)
 
-        def out_bank(shape):
-            return psum.tile(shape, F32, name="fin", tag="fin", bufs=4)
+        def parked_bank():
+            return psum.tile([P, BANK], F32, name="parked", tag="parked", bufs=HALF_PSUM)
+
+        def quantize(codes, scales, rounded):
+            nc.vector.quantize_mx(out=codes.bitcast(FP8X4), scales=scales, in_=rounded)
+
+        def load_scale_rows(tile, rows):
+            for q in range(P // QUADRANT):
+                nc.sync.dma_start(
+                    tile[QUADRANT * q : QUADRANT * q + PACK, :].bitcast(I32),
+                    rows[PACK * q : PACK * (q + 1), :].bitcast(I32),
+                )
 
         list_tab = held([P, NP // PER_COL], U16, "list_tab")
         list_page = held([P, S // PER_COL], U16, "list_page")
@@ -81,53 +102,54 @@ def tile_list_submap_robust_gradient_kernel(
             for b in range(R_PASSES)
         ]
 
+        def scan_parts(j):
+            parts = 2 if j == 0 else 1
+            return [(h * S // parts, (h + 1) * S // parts) for h in range(parts)]
+
         def load_plane(j):
             page.append(wide_tile())
-            scan.append(ringed([P, S], F32, "weight", 3))
+            if j == PACK - 1:
+                scan.append(ringed([P, S], F32, "scan_then_wr", 1))
+            else:
+                scan.append(ringed([P, S], F32, "scan_then_weight", UNIT_BUFS))
             nc.sync.dma_start(page[j][:], base_v[:, j, :])
-            parts = 2 if j < 2 else 1
-            for h in range(parts):
-                cols = slice(h * S // parts, (h + 1) * S // parts)
-                nc.sync.dma_start(scan[j][:, cols], xs_v[:, j, cols])
+            for lo, hi in scan_parts(j):
+                nc.sync.dma_start(scan[j][:, lo:hi], xs_v[:, j, lo:hi])
 
         def load_w(b):
             nc.sync.dma_start(w_raw[b], w_v[:, :, b * BANK : (b + 1) * BANK])
 
-        tab_w = ringed([P, T], I32, "stage", 3)
-        wc_w_raw = held([P, 2 * H // 4], I32, "wc_w_raw")
+        tab_w = ringed([P, T], I32, "table_then_stage", STAGE_BUFS)
+        wc_w_raw = held([P, H // 2], I32, "wc_w_raw")
 
         nc.sync.dma_start(list_tab[:], offs)
-        for q in range(4):
-            nc.sync.dma_start(tab_s[32 * q : 32 * q + 4, :].bitcast(I32), tab_scales[0, 4 * q : 4 * q + 4, :].bitcast(I32))
+        load_scale_rows(tab_s, tab_scales[0])
         nc.scalar.activation(warm[:, 1:2], warm[:, 0:1], ACT.Abs_reciprocal_sqrt)
         nc.sync.dma_start(list_page[:], offs2)
         load_plane(0)
         load_w(0)
+        load_plane(1)
         load_w(1)
         nc.sync.dma_start(tab_w[:], tab_words[0].rearrange("p t i -> p (t i)").bitcast(I32))
         nc.sync.dma_start(wc_w_raw[:], wc_words[0].bitcast(I32))
-        for q in range(4):
-            nc.sync.dma_start(wc_s_raw[32 * q : 32 * q + 4, :].bitcast(I32), wc_scales[0, 4 * q : 4 * q + 4, :].bitcast(I32))
-        load_plane(1)
+        load_scale_rows(wc_s_raw, wc_scales[0])
         load_plane(2)
         load_plane(3)
         for b in range(R_PASSES):
             nc.sync.dma_start(
-                prec_rows[PACK * b : PACK * (b + 1), :].rearrange("t (g i) -> t g i", i=8),
-                prec[b * BANK : (b + 1) * BANK].rearrange("(g t i) -> t g i", t=PACK, i=8),
+                prec_rows[PACK * b : PACK * (b + 1), :].rearrange("t (s u) -> t s u", u=RUN),
+                prec[b * BANK : (b + 1) * BANK].rearrange("(s t u) -> t s u", t=PACK, u=RUN),
             )
         nc.sync.dma_start(list_pair[:], offs3)
 
-
         def scatter(j):
-            parts = 2 if j < 2 else 1
-            for h in range(parts):
-                lo, hi = h * S // parts, (h + 1) * S // parts
-                nc.vector.tensor_copy(page[j][:].indirect(list_page[:, lo // PER_COL : hi // PER_COL]), scan[j][:, lo:hi])
+            for lo, hi in scan_parts(j):
+                entries = list_page[:, lo // PER_COL : hi // PER_COL]
+                nc.vector.tensor_copy(page[j][:].indirect(entries), scan[j][:, lo:hi])
 
         def round_plane(j):
             for c in range(CHUNKS):
-                slots = pairs[c].rearrange("p (u n e) -> p u n e", u=2, e=2)
+                slots = pairs[c].rearrange("p (h n e) -> p h n e", h=2, e=2)
                 nc.scalar.copy(slots[:, j // 2, :, j % 2], page[j][:, c * BANK : (c + 1) * BANK])
 
         wk_bf = []
@@ -136,40 +158,30 @@ def tile_list_submap_robust_gradient_kernel(
         wr_s = [held([P, BANK], U8, f"wr_s{b}") for b in range(R_PASSES)]
 
         def round_w(b):
-            wk_bf.append(bf16_tile([P, BANK * PACK]))
+            wk_bf.append(rounded_tile(BANK))
             nc.scalar.copy(
-                wk_bf[b][:].rearrange("p (t g i j) -> p g t j i", t=PACK, i=8, j=PACK),
-                w_raw[b].rearrange("p j (g t i) -> p g t j i", t=PACK, i=8),
+                wk_bf[b][:].rearrange("p (t s u j) -> p s t j u", t=PACK, u=RUN, j=PACK),
+                w_raw[b].rearrange("p j (s t u) -> p s t j u", t=PACK, u=RUN),
             )
 
-        def quantize(codes, scales, rounded):
-            nc.vector.quantize_mx(out=codes.bitcast(FP8X4), scales=scales, in_=rounded)
-
-        wr_bf = []
-
-        def turn_w(b):
-            if b == 0:
-                wr_bf.append(bf16_tile([P, BANK * PACK]))
-            else:
-                wr_bf.append(ringed([P, BANK * PACK], BF16, "woven_then_wr", 1))
-            copy = nc.scalar.copy if b == 0 else nc.vector.tensor_copy
+        def turn_w(b, turned, copy):
             words = wk_bf[b][:].bitcast(F32)
-            for u in range(2):
-                bank = out_bank([P, BANK])
+            for h in range(2):
+                bank = parked_bank()
                 for t in range(PACK):
                     nc.tensor.transpose(
-                        bank[:, t * P : (t + 1) * P], words[:, 2 * P * t + u : 2 * P * (t + 1) : 2], ident[:]
+                        bank[:, t * P : (t + 1) * P], words[:, 2 * P * t + h : 2 * P * (t + 1) : 2], ident[:]
                     )
                 copy(
-                    wr_bf[b][:, u * 2 * BANK : (u + 1) * 2 * BANK].rearrange("m (e p t) -> m e p t", e=2, t=PACK),
+                    turned[:, h * 2 * BANK : (h + 1) * 2 * BANK].rearrange("m (e p t) -> m e p t", e=2, t=PACK),
                     bank[:].bitcast(BF16).rearrange("m (t p e) -> m e p t", t=PACK, e=2),
                 )
 
         v_c = held([P, NP], U32, "v_c")
         v_s = held([P, NP], U8, "v_s")
-        wc_w = held([P, 2 * H // 4], I32, "wc_w")
+        wc_w = held([P, H // 2], I32, "wc_w")
         wc_s = held([P, H], U8, "wc_s")
-        b_sb = [held([P, NP], F32, f"b_sb{i}") for i in range(R_PASSES * PACK)]
+        b_sb = [held([P, NP], F32, f"b_sb{i}") for i in range(ROW_TILES)]
 
         nc.vector.tensor_copy(v_s[:], tab_s[:].indirect(list_tab[:]))
         scatter(0)
@@ -179,26 +191,28 @@ def tile_list_submap_robust_gradient_kernel(
         pairs = [pairs_flat[:, c * BANK * PACK : (c + 1) * BANK * PACK] for c in range(CHUNKS)]
         round_plane(0)
         quantize(wk_c[0][:], wk_s[0][:], wk_bf[0][:])
+        scatter(1)
         nc.vector.tensor_copy(v_c[:], tab_w[:].bitcast(U32).indirect(list_tab[:]))
         quantize(wk_c[1][:], wk_s[1][:], wk_bf[1][:])
         nc.vector.tensor_copy(
-            wc_w[:].rearrange("p (b t g x) -> p b t g x", b=R_PASSES, t=PACK, x=4),
-            wc_w_raw[:].rearrange("p (b g t x) -> p b t g x", b=R_PASSES, t=PACK, x=4),
+            wc_w[:].rearrange("p (b t s x) -> p b t s x", b=R_PASSES, t=PACK, x=RUN // 2),
+            wc_w_raw[:].rearrange("p (b s t x) -> p b t s x", b=R_PASSES, t=PACK, x=RUN // 2),
         )
         nc.vector.tensor_copy(
-            wc_s[:].bitcast(I32).rearrange("p (b t g x) -> p b t g x", b=R_PASSES, t=PACK, x=2),
-            wc_s_raw[:].bitcast(I32).rearrange("p (b g t x) -> p b t g x", b=R_PASSES, t=PACK, x=2),
+            wc_s[:].bitcast(I32).rearrange("p (b t s x) -> p b t s x", b=R_PASSES, t=PACK, x=RUN // 4),
+            wc_s_raw[:].bitcast(I32).rearrange("p (b s t x) -> p b t s x", b=R_PASSES, t=PACK, x=RUN // 4),
         )
-        turn_w(0)
-        scatter(1)
+        wr_bf = [rounded_tile(BANK)]
+        turn_w(0, wr_bf[0], nc.scalar.copy)
+        round_plane(1)
         scatter(2)
 
-        wc_bytes = wc_w[:].bitcast(U8)
-        for i in range(R_PASSES * PACK):
+        wc_codes = wc_w[:].bitcast(U8)
+        for i in range(ROW_TILES):
             b, t = divmod(i, PACK)
-            for h in range(NP // BANK):
-                cols = slice(h * BANK, (h + 1) * BANK)
-                bank = acc_bank([P, BANK])
+            for lo in range(0, NP, BANK):
+                cols = slice(lo, lo + BANK)
+                bank = stream_bank()
                 nc.tensor.matmul_mx(
                     out=bank[:],
                     lhsT=wk_c[b][:, t * P : (t + 1) * P].bitcast(FP8X4),
@@ -210,7 +224,7 @@ def tile_list_submap_robust_gradient_kernel(
                 )
                 nc.tensor.matmul_mx(
                     out=bank[:],
-                    lhsT=wc_bytes[:, 2 * P * i : 2 * P * (i + 1)].bitcast(FP4X4),
+                    lhsT=wc_codes[:, 2 * P * i : 2 * P * (i + 1)].bitcast(FP4X4),
                     lhsT_scale=wc_s[:, P * i : P * (i + 1)],
                     rhs=v_c[:, cols].bitcast(FP8X4),
                     rhs_scale=v_s[:, cols],
@@ -219,15 +233,13 @@ def tile_list_submap_robust_gradient_kernel(
                 )
                 nc.scalar.copy(b_sb[i][:, cols], bank[:])
 
-
-        prec_col = held([P, R_PASSES * PACK], F32, "prec_col")
-        prec_inv = held([P, R_PASSES * PACK], F32, "prec_inv")
-        bank = acc_bank([P, BANK])
-        nc.tensor.transpose(bank[:, 0:P], prec_rows[:], ident[:])
-        nc.scalar.copy(prec_col[:], bank[:, 0 : R_PASSES * PACK])
+        prec_col = held([P, ROW_TILES], F32, "prec_col")
+        prec_inv = held([P, ROW_TILES], F32, "prec_inv")
+        prec_bank = stream_bank()
+        nc.tensor.transpose(prec_bank[:, 0:P], prec_rows[:], ident[:])
+        nc.scalar.copy(prec_col[:], prec_bank[:, 0:ROW_TILES])
         nc.vector.reciprocal(prec_inv[:], prec_col[:])
 
-        round_plane(1)
         round_plane(2)
         scatter(3)
         round_plane(3)
@@ -239,13 +251,11 @@ def tile_list_submap_robust_gradient_kernel(
         def weave(c):
             if c == CHUNKS - 1:
                 woven.append(ringed([P, BANK * PACK], BF16, "woven_then_wr", 1))
-            elif c == CHUNKS - 2:
-                woven.append(ringed([P, BANK * PACK], BF16, "woven_then_codes", 1))
             else:
-                woven.append(bf16_tile([P, BANK * PACK]))
+                woven.append(rounded_tile(BANK))
             nc.vector.tensor_copy(
-                woven[c][:].bitcast(F32).rearrange("p (n u) -> p n u", u=2),
-                pairs[c].bitcast(F32).rearrange("p (u n) -> p n u", u=2),
+                woven[c][:].bitcast(F32).rearrange("p (n h) -> p n h", h=2),
+                pairs[c].bitcast(F32).rearrange("p (h n) -> p n h", h=2),
             )
 
         weave(0)
@@ -254,19 +264,27 @@ def tile_list_submap_robust_gradient_kernel(
                 weave(c + 1)
             quantize(page_c[c][:], page_s[c][:], woven[c][:])
 
-        turn_w(1)
-        wr_flat = ringed([P, R_PASSES * BANK], U32, "woven_then_codes", 1)
-        wr_c = [wr_flat[:, b * BANK : (b + 1) * BANK] for b in range(R_PASSES)]
+        wr_bf.append(ringed([P, BANK * PACK], BF16, "woven_then_wr", 1))
+        turn_w(1, wr_bf[1], nc.vector.tensor_copy)
+        wr_c = [ringed([P, BANK], U32, "scan_then_wr", 1), held([P, BANK], U32, "wr_c1")]
         for b in range(R_PASSES):
-            quantize(wr_c[b], wr_s[b][:], wr_bf[b][:])
+            quantize(wr_c[b][:], wr_s[b][:], wr_bf[b][:])
 
+        half = BANK // 2
+        units = [(0, 0, BANK), (0, BANK, BANK), (1, 0, BANK), (1, BANK, half), (1, BANK + half, half)]
+        steps = [(unit, t) for unit in units for t in range(PACK)]
         a_sb = {}
+        resid = {}
+        weight = {}
+        g_bf = {}
+        g_c = {}
+        g_s = {}
 
-        def project(i, c, on_vector):
+        def project(i, c):
             b, t = divmod(i, PACK)
             if i not in a_sb:
                 a_sb[i] = wide_tile()
-            bank = acc_bank([P, BANK])
+            bank = stream_bank()
             nc.tensor.matmul_mx(
                 out=bank[:],
                 lhsT=wk_c[b][:, t * P : (t + 1) * P].bitcast(FP8X4),
@@ -276,95 +294,87 @@ def tile_list_submap_robust_gradient_kernel(
                 start=True,
                 stop=True,
             )
-            dst = a_sb[i][:, c * BANK : (c + 1) * BANK]
-            if on_vector:
-                nc.vector.tensor_copy(dst, bank[:])
-            else:
-                nc.scalar.copy(dst, bank[:])
-
-        resid = {}
-        weight = {}
-        g_c = {}
-        g_s = {}
+            nc.scalar.copy(a_sb[i][:, c * BANK : (c + 1) * BANK], bank[:])
 
         def residual(unit, t):
             b, lo, n = unit
             i = b * PACK + t
             if unit not in resid:
-                resid[unit] = ringed([P, PACK, n], F32, "resid", 3)
-                weight[unit] = ringed([P, PACK, n], F32, "weight", 3)
-            e = resid[unit][:, t, :]
-            z = weight[unit][:, t, :]
+                resid[unit] = ringed([P, PACK, n], F32, "resid", UNIT_BUFS)
+                weight[unit] = ringed([P, PACK, n], F32, "scan_then_weight", UNIT_BUFS)
+            entries = list_pair[:, lo // PER_COL : (lo + n) // PER_COL]
             nc.vector.tensor_tensor(
-                e, a_sb[i][:].indirect(list_pair[:, lo // PER_COL : (lo + n) // PER_COL]), b_sb[i][:, lo : lo + n], ALU.subtract
+                resid[unit][:, t, :], a_sb[i][:].indirect(entries), b_sb[i][:, lo : lo + n], ALU.subtract
             )
-            return e, z, i
 
-        def square(e, z, on_vector):
-            if on_vector:
-                nc.vector.tensor_tensor(z, e, e, ALU.mult)
-            else:
-                nc.scalar.activation(z, e, ACT.Square)
+        def square(unit, t):
+            nc.vector.tensor_tensor(weight[unit][:, t, :], resid[unit][:, t, :], resid[unit][:, t, :], ALU.mult)
 
-        def denominator(z, i):
+        def denominator(unit, t):
+            i = unit[0] * PACK + t
+            z = weight[unit][:, t, :]
             nc.scalar.activation(z, z, ACT.Square, bias=1.0, scale=prec_col[:, i : i + 1])
 
-        def invert(z, i):
+        def invert(unit, t):
+            i = unit[0] * PACK + t
+            z = weight[unit][:, t, :]
             nc.scalar.activation(z, z, ACT.Abs_reciprocal_sqrt, scale=prec_inv[:, i : i + 1])
 
-        def resquare(z):
-            nc.scalar.activation(z, z, ACT.Square)
+        def resquare(unit, t):
+            z = weight[unit][:, t, :]
+            if unit == units[-1]:
+                nc.vector.tensor_tensor(z, z, z, ALU.mult)
+            else:
+                nc.scalar.activation(z, z, ACT.Square)
 
-        g_round = {}
+        def halves(unit):
+            n = unit[2]
+            return [(0, n // 2), (n // 2, n)]
 
         def weigh(unit):
-            b, lo, n = unit
-            g_bf = bf16_tile([P, n * PACK])
-            nc.vector.tensor_tensor(
-                g_bf[:].rearrange("p (c i t) -> p c t i", i=4, t=PACK),
-                resid[unit][:].rearrange("p t (c i) -> p c t i", i=4),
-                weight[unit][:].rearrange("p t (c i) -> p c t i", i=4),
-                ALU.mult,
-            )
-            g_round[unit] = g_bf
+            g_bf[unit] = rounded_tile(unit[2])
+            for lo, hi in halves(unit):
+                nc.vector.tensor_tensor(
+                    g_bf[unit][:, lo * PACK : hi * PACK].rearrange("p (c i t) -> p c t i", i=LINE, t=PACK),
+                    resid[unit][:, :, lo:hi].rearrange("p t (c i) -> p c t i", i=LINE),
+                    weight[unit][:, :, lo:hi].rearrange("p t (c i) -> p c t i", i=LINE),
+                    ALU.mult,
+                )
 
-        def finish(unit):
+        def quantize_g(unit):
             b, lo, n = unit
-            g_bf = g_round[unit]
             g_c[unit] = held([P, n], U32, f"g_c{b}_{lo}")
             g_s[unit] = held([P, n], U8, f"g_s{b}_{lo}")
-            quantize(g_c[unit][:], g_s[unit][:], g_bf[:])
+            for first, last in halves(unit):
+                quantize(g_c[unit][:, first:last], g_s[unit][:, first:last], g_bf[unit][:, first * PACK : last * PACK])
 
-        def back_pass(dst, j, unit, lo, n):
-            b = unit[0]
-            cols = slice(lo - unit[1], lo - unit[1] + n)
-            nc.tensor.matmul_mx(
-                out=dst,
-                lhsT=wr_c[b][:, j * P : (j + 1) * P].bitcast(FP8X4),
-                lhsT_scale=wr_s[b][:, j * P : (j + 1) * P],
-                rhs=g_c[unit][:, cols].bitcast(FP8X4),
-                rhs_scale=g_s[unit][:, cols],
-                start=(b == 0),
-                stop=(b == R_PASSES - 1),
-            )
-
-        def back_project(unit, make_bank):
+        def back_project(unit, new_bank):
             b, lo, n = unit
             per_bank = BANK // n
-            banks = [make_bank([P, BANK]) for x in range(PACK // per_bank)]
+            banks = [new_bank() for x in range(PACK // per_bank)]
             for j in range(PACK):
                 dst = banks[j // per_bank][:, (j % per_bank) * n : (j % per_bank + 1) * n]
-                back_pass(dst, j, units[lo // BANK], lo, n)
-                back_pass(dst, j, unit, lo, n)
+                for source in (units[lo // BANK], unit):
+                    r_pass = source[0]
+                    cols = slice(lo - source[1], lo - source[1] + n)
+                    nc.tensor.matmul_mx(
+                        out=dst,
+                        lhsT=wr_c[r_pass][:, j * P : (j + 1) * P].bitcast(FP8X4),
+                        lhsT_scale=wr_s[r_pass][:, j * P : (j + 1) * P],
+                        rhs=g_c[source][:, cols].bitcast(FP8X4),
+                        rhs_scale=g_s[source][:, cols],
+                        start=(r_pass == 0),
+                        stop=(r_pass == R_PASSES - 1),
+                    )
             return banks
 
-        def store(banks, unit, engines):
+        def store(unit, banks):
             b, lo, n = unit
             per_bank = BANK // n
-            staged = ringed([P, PACK * n], F32, "stage", 3)
+            staged = ringed([P, PACK * n], F32, "table_then_stage", STAGE_BUFS)
             for x, bank in enumerate(banks):
                 part = staged[:, x * BANK : (x + 1) * BANK]
-                if engines[x] == "v":
+                if unit == units[-1] and x == len(banks) - 1:
                     nc.vector.tensor_copy(part, bank[:])
                 else:
                     nc.scalar.copy(part, bank[:])
@@ -372,51 +382,43 @@ def tile_list_submap_robust_gradient_kernel(
                     out_v[:, x * per_bank : (x + 1) * per_bank, lo : lo + n], part.rearrange("p (j c) -> p j c", c=n)
                 )
 
-        half = BANK // 2
-        units = [(0, 0, BANK), (0, BANK, BANK), (1, 0, BANK), (1, BANK, half), (1, BANK + half, half)]
-        ahead = 2
         for c in range(CHUNKS):
-            for i in range(ahead):
-                project(i, c, False)
-        later = [(i, c) for i in range(ahead, R_PASSES * PACK) for c in range(CHUNKS)]
-        per_step = [4, 4, 2, 2, 2, 2, 2, 2, 2, 2]
-        on_vector = 0
-        emptied = 0
-        banks = {}
-        steps = [(k, t) for k in range(len(units)) for t in range(PACK)]
-        state = {}
+            for i in range(FIRST_TILES):
+                project(i, c)
+
+        urgent = [[(i, c) for c in range(CHUNKS)] for i in range(FIRST_TILES, PACK)]
+        spread = [
+            [(i, c) for c in range(first, first + CHUNKS // 2)]
+            for i in range(PACK, ROW_TILES)
+            for first in (0, CHUNKS // 2)
+        ]
+        projections = urgent + spread
+
+        out_banks = {}
         for step in range(len(steps) + 2):
             if step < len(steps):
-                k, t = steps[step]
-                state[step] = residual(units[k], t)
-                if k > 0:
-                    done = units[k - 1]
-                    if t == 2:
-                        weigh(done)
-                    if t == 3:
-                        finish(done)
-                        if k > 2:
-                            banks[k - 1] = back_project(done, out_bank if k == 3 else acc_bank)
-                if k == 4 and t == 0 and False:
-                    store(banks[2], units[2], "undefined")
+                unit, t = steps[step]
+                residual(unit, t)
+                if step >= PACK and t == PACK - 2:
+                    weigh(steps[step - PACK][0])
+                if step >= PACK and t == PACK - 1:
+                    done = steps[step - PACK][0]
+                    quantize_g(done)
+                    if done[0] == R_PASSES - 1:
+                        out_banks[done] = back_project(done, parked_bank if done[2] == BANK else stream_bank)
             if 1 <= step <= len(steps):
-                e, z, i = state[step - 1]
-                square(e, z, step - 1 != 9)
-            if step < len(per_step):
-                for i, c in later[emptied : emptied + per_step[step]]:
-                    project(i, c, (i, c) in later[2 * CHUNKS : 2 * CHUNKS + on_vector])
-                emptied = emptied + per_step[step]
+                square(*steps[step - 1])
+            if step < len(projections):
+                for i, c in projections[step]:
+                    project(i, c)
             if step >= 2:
-                e, z, i = state[step - 2]
-                invert(z, i)
+                invert(*steps[step - 2])
             if 1 <= step <= len(steps):
-                e, z, i = state[step - 1]
-                denominator(z, i)
+                denominator(*steps[step - 1])
             if step >= 2:
-                resquare(state[step - 2][1])
-        last = units[-1]
-        weigh(last)
-        finish(last)
-        banks[len(units) - 1] = back_project(last, acc_bank)
-        for k in range(2, len(units)):
-            store(banks[k], units[k], ["ssss","vv","sv"][k - 2])
+                resquare(*steps[step - 2])
+        weigh(units[-1])
+        quantize_g(units[-1])
+        out_banks[units[-1]] = back_project(units[-1], stream_bank)
+        for unit in units[R_PASSES:]:
+            store(unit, out_banks[unit])

@@ -30,11 +30,12 @@ LINE = 4
 ALIGN = 64
 
 WIDE_BUFS = 6
-ROUNDED_BUFS = 4
-UNIT_BUFS = 3
+ROUNDED_BUFS = 5
+SCAN_BUFS = 3
 STAGE_BUFS = 3
 HALF_PSUM = 4
-FIRST_TILES = 2
+LATE_B = 2
+LAST_WIDTHS = (512, 256, 256)
 
 
 def tile_list_submap_robust_gradient_kernel(
@@ -94,30 +95,24 @@ def tile_list_submap_robust_gradient_kernel(
         w_v = w.rearrange("(p j) r -> p j r", j=PACK)
         out_v = out.rearrange("(p j) c -> p j c", j=PACK)
 
-        page = []
-        scan = []
-        w_flat = ringed([P, PACK * H], F32, "w_then_pairs", 1)
-        w_raw = [
-            w_flat[:, b * PACK * BANK : (b + 1) * PACK * BANK].rearrange("p (j r) -> p j r", j=PACK)
-            for b in range(R_PASSES)
-        ]
+        page = [wide_tile() for j in range(PACK)]
+        scan = [ringed([P, S], F32, "scan", SCAN_BUFS) for j in range(PACK - 1)]
+        scan.append(ringed([P, S], F32, "scan_then_wr", 1))
+        w_raw = [ringed([P, PACK, BANK], F32, tag, 1) for tag in ("w_then_resid", "w_then_pairs")]
 
         def scan_parts(j):
             parts = 2 if j == 0 else 1
             return [(h * S // parts, (h + 1) * S // parts) for h in range(parts)]
 
         def load_plane(j):
-            page.append(wide_tile())
-            if j == PACK - 1:
-                scan.append(ringed([P, S], F32, "scan_then_wr", 1))
-            else:
-                scan.append(ringed([P, S], F32, "scan_then_weight", UNIT_BUFS))
             nc.sync.dma_start(page[j][:], base_v[:, j, :])
-            for lo, hi in scan_parts(j):
-                nc.sync.dma_start(scan[j][:, lo:hi], xs_v[:, j, lo:hi])
+
+        def load_scan(j, part):
+            lo, hi = scan_parts(j)[part]
+            nc.sync.dma_start(scan[j][:, lo:hi], xs_v[:, j, lo:hi])
 
         def load_w(b):
-            nc.sync.dma_start(w_raw[b], w_v[:, :, b * BANK : (b + 1) * BANK])
+            nc.sync.dma_start(w_raw[b][:], w_v[:, :, b * BANK : (b + 1) * BANK])
 
         tab_w = ringed([P, T], I32, "table_then_stage", STAGE_BUFS)
         wc_w_raw = held([P, H // 2], I32, "wc_w_raw")
@@ -127,14 +122,18 @@ def tile_list_submap_robust_gradient_kernel(
         nc.scalar.activation(warm[:, 1:2], warm[:, 0:1], ACT.Abs_reciprocal_sqrt)
         nc.sync.dma_start(list_page[:], offs2)
         load_plane(0)
+        load_scan(0, 0)
         load_w(0)
+        load_scan(0, 1)
         load_plane(1)
+        load_scan(1, 0)
         load_w(1)
         nc.sync.dma_start(tab_w[:], tab_words[0].rearrange("p t i -> p (t i)").bitcast(I32))
-        nc.sync.dma_start(wc_w_raw[:], wc_words[0].bitcast(I32))
         load_scale_rows(wc_s_raw, wc_scales[0])
-        load_plane(2)
-        load_plane(3)
+        nc.sync.dma_start(wc_w_raw[:], wc_words[0].bitcast(I32))
+        for j in range(2, PACK):
+            load_plane(j)
+            load_scan(j, 0)
         for b in range(R_PASSES):
             nc.sync.dma_start(
                 prec_rows[PACK * b : PACK * (b + 1), :].rearrange("t (s u) -> t s u", u=RUN),
@@ -147,24 +146,28 @@ def tile_list_submap_robust_gradient_kernel(
                 entries = list_page[:, lo // PER_COL : hi // PER_COL]
                 nc.vector.tensor_copy(page[j][:].indirect(entries), scan[j][:, lo:hi])
 
-        def round_plane(j):
-            for c in range(CHUNKS):
-                slots = pairs[c].rearrange("p (h n e) -> p h n e", h=2, e=2)
-                nc.scalar.copy(slots[:, j // 2, :, j % 2], page[j][:, c * BANK : (c + 1) * BANK])
+        def round_plane(j, first, last):
+            slots = pairs[:].rearrange("p (c h n e) -> p c h n e", c=CHUNKS, h=2, e=2)
+            nc.scalar.copy(
+                slots[:, first:last, j // 2, :, j % 2],
+                page[j][:, first * BANK : last * BANK].rearrange("p (c n) -> p c n", n=BANK),
+            )
 
         wk_bf = []
+        wr_bf = []
         wk_c = [held([P, BANK], U32, f"wk_c{b}") for b in range(R_PASSES)]
         wk_s = [held([P, BANK], U8, f"wk_s{b}") for b in range(R_PASSES)]
-        wr_s = [held([P, BANK], U8, f"wr_s{b}") for b in range(R_PASSES)]
 
         def round_w(b):
             wk_bf.append(rounded_tile(BANK))
             nc.scalar.copy(
                 wk_bf[b][:].rearrange("p (t s u j) -> p s t j u", t=PACK, u=RUN, j=PACK),
-                w_raw[b].rearrange("p j (s t u) -> p s t j u", t=PACK, u=RUN),
+                w_raw[b][:].rearrange("p j (s t u) -> p s t j u", t=PACK, u=RUN),
             )
 
-        def turn_w(b, turned, copy):
+        def turn_w(b):
+            turned = rounded_tile(BANK)
+            wr_bf.append(turned)
             words = wk_bf[b][:].bitcast(F32)
             for h in range(2):
                 bank = parked_bank()
@@ -172,7 +175,7 @@ def tile_list_submap_robust_gradient_kernel(
                     nc.tensor.transpose(
                         bank[:, t * P : (t + 1) * P], words[:, 2 * P * t + h : 2 * P * (t + 1) : 2], ident[:]
                     )
-                copy(
+                nc.scalar.copy(
                     turned[:, h * 2 * BANK : (h + 1) * 2 * BANK].rearrange("m (e p t) -> m e p t", e=2, t=PACK),
                     bank[:].bitcast(BF16).rearrange("m (t p e) -> m e p t", t=PACK, e=2),
                 )
@@ -181,34 +184,10 @@ def tile_list_submap_robust_gradient_kernel(
         v_s = held([P, NP], U8, "v_s")
         wc_w = held([P, H // 2], I32, "wc_w")
         wc_s = held([P, H], U8, "wc_s")
-        b_sb = [held([P, NP], F32, f"b_sb{i}") for i in range(ROW_TILES)]
-
-        nc.vector.tensor_copy(v_s[:], tab_s[:].indirect(list_tab[:]))
-        scatter(0)
-        round_w(0)
-        round_w(1)
-        pairs_flat = ringed([P, T * PACK], BF16, "w_then_pairs", 1)
-        pairs = [pairs_flat[:, c * BANK * PACK : (c + 1) * BANK * PACK] for c in range(CHUNKS)]
-        round_plane(0)
-        quantize(wk_c[0][:], wk_s[0][:], wk_bf[0][:])
-        scatter(1)
-        nc.vector.tensor_copy(v_c[:], tab_w[:].bitcast(U32).indirect(list_tab[:]))
-        quantize(wk_c[1][:], wk_s[1][:], wk_bf[1][:])
-        nc.vector.tensor_copy(
-            wc_w[:].rearrange("p (b t s x) -> p b t s x", b=R_PASSES, t=PACK, x=RUN // 2),
-            wc_w_raw[:].rearrange("p (b s t x) -> p b t s x", b=R_PASSES, t=PACK, x=RUN // 2),
-        )
-        nc.vector.tensor_copy(
-            wc_s[:].bitcast(I32).rearrange("p (b t s x) -> p b t s x", b=R_PASSES, t=PACK, x=RUN // 4),
-            wc_s_raw[:].bitcast(I32).rearrange("p (b s t x) -> p b t s x", b=R_PASSES, t=PACK, x=RUN // 4),
-        )
-        wr_bf = [rounded_tile(BANK)]
-        turn_w(0, wr_bf[0], nc.scalar.copy)
-        round_plane(1)
-        scatter(2)
-
         wc_codes = wc_w[:].bitcast(U8)
-        for i in range(ROW_TILES):
+        chain = [held([P, PACK, NP], F32, f"chain{b}") for b in range(R_PASSES)]
+
+        def map_side(i):
             b, t = divmod(i, PACK)
             for lo in range(0, NP, BANK):
                 cols = slice(lo, lo + BANK)
@@ -231,31 +210,60 @@ def tile_list_submap_robust_gradient_kernel(
                     start=False,
                     stop=True,
                 )
-                nc.scalar.copy(b_sb[i][:, cols], bank[:])
+                nc.scalar.copy(chain[b][:, t, cols], bank[:])
 
+        nc.vector.tensor_copy(v_s[:], tab_s[:].indirect(list_tab[:]))
+        scatter(0)
+        round_w(0)
+        turn_w(0)
+        quantize(wk_c[0][:], wk_s[0][:], wk_bf[0][:])
+        scatter(1)
+        round_w(1)
+        turn_w(1)
+        quantize(wk_c[1][:], wk_s[1][:], wk_bf[1][:])
+        nc.vector.tensor_copy(v_c[:], tab_w[:].bitcast(U32).indirect(list_tab[:]))
+        nc.vector.tensor_copy(
+            wc_w[:].rearrange("p (b t s x) -> p b t s x", b=R_PASSES, t=PACK, x=RUN // 2),
+            wc_w_raw[:].rearrange("p (b s t x) -> p b t s x", b=R_PASSES, t=PACK, x=RUN // 2),
+        )
+        nc.vector.tensor_copy(
+            wc_s[:].bitcast(I32).rearrange("p (b t s x) -> p b t s x", b=R_PASSES, t=PACK, x=RUN // 4),
+            wc_s_raw[:].bitcast(I32).rearrange("p (b s t x) -> p b t s x", b=R_PASSES, t=PACK, x=RUN // 4),
+        )
+        pairs = ringed([P, T * PACK], BF16, "w_then_pairs", 1)
+        round_plane(0, 0, CHUNKS)
+        round_plane(1, 0, CHUNKS)
+        scatter(2)
+        for i in range(ROW_TILES - LATE_B):
+            map_side(i)
         prec_col = held([P, ROW_TILES], F32, "prec_col")
         prec_inv = held([P, ROW_TILES], F32, "prec_inv")
         prec_bank = stream_bank()
         nc.tensor.transpose(prec_bank[:, 0:P], prec_rows[:], ident[:])
         nc.scalar.copy(prec_col[:], prec_bank[:, 0:ROW_TILES])
         nc.vector.reciprocal(prec_inv[:], prec_col[:])
-
-        round_plane(2)
+        round_plane(2, 0, CHUNKS)
         scatter(3)
-        round_plane(3)
+        for c in range(CHUNKS):
+            round_plane(3, c, c + 1)
+        for i in range(ROW_TILES - LATE_B, ROW_TILES):
+            map_side(i)
+
+        wr_c = ringed([P, R_PASSES * BANK], U32, "scan_then_wr", 1)
+        wr_s = held([P, R_PASSES * BANK], U8, "wr_s")
+        for b in range(R_PASSES):
+            cols = slice(b * BANK, (b + 1) * BANK)
+            quantize(wr_c[:, cols], wr_s[:, cols], wr_bf[b][:])
 
         page_c = [held([P, BANK], U32, f"page_c{c}") for c in range(CHUNKS)]
         page_s = [held([P, BANK], U8, f"page_s{c}") for c in range(CHUNKS)]
         woven = []
 
         def weave(c):
-            if c == CHUNKS - 1:
-                woven.append(ringed([P, BANK * PACK], BF16, "woven_then_wr", 1))
-            else:
-                woven.append(rounded_tile(BANK))
+            woven.append(rounded_tile(BANK))
             nc.vector.tensor_copy(
                 woven[c][:].bitcast(F32).rearrange("p (n h) -> p n h", h=2),
-                pairs[c].bitcast(F32).rearrange("p (h n) -> p n h", h=2),
+                pairs[:, c * BANK * PACK : (c + 1) * BANK * PACK].bitcast(F32).rearrange("p (h n) -> p n h", h=2),
             )
 
         weave(0)
@@ -264,27 +272,16 @@ def tile_list_submap_robust_gradient_kernel(
                 weave(c + 1)
             quantize(page_c[c][:], page_s[c][:], woven[c][:])
 
-        wr_bf.append(ringed([P, BANK * PACK], BF16, "woven_then_wr", 1))
-        turn_w(1, wr_bf[1], nc.vector.tensor_copy)
-        wr_c = [ringed([P, BANK], U32, "scan_then_wr", 1), held([P, BANK], U32, "wr_c1")]
-        for b in range(R_PASSES):
-            quantize(wr_c[b][:], wr_s[b][:], wr_bf[b][:])
-
-        half = BANK // 2
-        units = [(0, 0, BANK), (0, BANK, BANK), (1, 0, BANK), (1, BANK, half), (1, BANK + half, half)]
-        steps = [(unit, t) for unit in units for t in range(PACK)]
         a_sb = {}
-        resid = {}
-        weight = {}
-        g_bf = {}
-        g_c = {}
-        g_s = {}
+        resid = [ringed([P, PACK, NP], F32, "w_then_resid", 1), held([P, PACK, NP], F32, "resid1")]
+        g_c = [held([P, NP], U32, f"g_c{b}") for b in range(R_PASSES)]
+        g_s = [held([P, NP], U8, f"g_s{b}") for b in range(R_PASSES)]
 
-        def project(i, c):
+        def project(i, c, on_vector):
             b, t = divmod(i, PACK)
             if i not in a_sb:
                 a_sb[i] = wide_tile()
-            bank = stream_bank()
+            bank = parked_bank() if on_vector else stream_bank()
             nc.tensor.matmul_mx(
                 out=bank[:],
                 lhsT=wk_c[b][:, t * P : (t + 1) * P].bitcast(FP8X4),
@@ -294,131 +291,124 @@ def tile_list_submap_robust_gradient_kernel(
                 start=True,
                 stop=True,
             )
-            nc.scalar.copy(a_sb[i][:, c * BANK : (c + 1) * BANK], bank[:])
+            copy = nc.vector.tensor_copy if on_vector else nc.scalar.copy
+            copy(a_sb[i][:, c * BANK : (c + 1) * BANK], bank[:])
 
-        def residual(unit, t):
-            b, lo, n = unit
-            i = b * PACK + t
-            if unit not in resid:
-                resid[unit] = ringed([P, PACK, n], F32, "resid", UNIT_BUFS)
-                weight[unit] = ringed([P, PACK, n], F32, "scan_then_weight", UNIT_BUFS)
+        def residual(i, lo, n):
+            b, t = divmod(i, PACK)
             entries = list_pair[:, lo // PER_COL : (lo + n) // PER_COL]
             nc.vector.tensor_tensor(
-                resid[unit][:, t, :], a_sb[i][:].indirect(entries), b_sb[i][:, lo : lo + n], ALU.subtract
+                resid[b][:, t, lo : lo + n], a_sb[i][:].indirect(entries), chain[b][:, t, lo : lo + n], ALU.subtract
             )
 
-        def square(unit, t):
-            nc.vector.tensor_tensor(weight[unit][:, t, :], resid[unit][:, t, :], resid[unit][:, t, :], ALU.mult)
+        def square(i, lo, n):
+            b, t = divmod(i, PACK)
+            nc.scalar.activation(chain[b][:, t, lo : lo + n], resid[b][:, t, lo : lo + n], ACT.Square)
 
-        def denominator(unit, t):
-            i = unit[0] * PACK + t
-            z = weight[unit][:, t, :]
+        def denominator(i, lo, n):
+            b, t = divmod(i, PACK)
+            z = chain[b][:, t, lo : lo + n]
             nc.scalar.activation(z, z, ACT.Square, bias=1.0, scale=prec_col[:, i : i + 1])
 
-        def invert(unit, t):
-            i = unit[0] * PACK + t
-            z = weight[unit][:, t, :]
+        def invert(i, lo, n):
+            b, t = divmod(i, PACK)
+            z = chain[b][:, t, lo : lo + n]
             nc.scalar.activation(z, z, ACT.Abs_reciprocal_sqrt, scale=prec_inv[:, i : i + 1])
 
-        def resquare(unit, t):
-            z = weight[unit][:, t, :]
-            if unit == units[-1]:
+        def resquare(i, lo, n, on_vector):
+            b, t = divmod(i, PACK)
+            z = chain[b][:, t, lo : lo + n]
+            if on_vector:
                 nc.vector.tensor_tensor(z, z, z, ALU.mult)
             else:
                 nc.scalar.activation(z, z, ACT.Square)
 
-        def halves(unit):
-            n = unit[2]
-            return [(0, n // 2), (n // 2, n)]
-
-        def weigh(unit):
-            g_bf[unit] = rounded_tile(unit[2])
-            for lo, hi in halves(unit):
+        def weigh(b, lo, n):
+            g_bf = rounded_tile(n)
+            halves = [(0, n // 2), (n // 2, n)]
+            for first, last in halves:
                 nc.vector.tensor_tensor(
-                    g_bf[unit][:, lo * PACK : hi * PACK].rearrange("p (c i t) -> p c t i", i=LINE, t=PACK),
-                    resid[unit][:, :, lo:hi].rearrange("p t (c i) -> p c t i", i=LINE),
-                    weight[unit][:, :, lo:hi].rearrange("p t (c i) -> p c t i", i=LINE),
+                    g_bf[:, first * PACK : last * PACK].rearrange("p (c i t) -> p c t i", i=LINE, t=PACK),
+                    resid[b][:, :, lo + first : lo + last].rearrange("p t (c i) -> p c t i", i=LINE),
+                    chain[b][:, :, lo + first : lo + last].rearrange("p t (c i) -> p c t i", i=LINE),
                     ALU.mult,
                 )
+            for first, last in halves:
+                cols = slice(lo + first, lo + last)
+                quantize(g_c[b][:, cols], g_s[b][:, cols], g_bf[:, first * PACK : last * PACK])
 
-        def quantize_g(unit):
-            b, lo, n = unit
-            g_c[unit] = held([P, n], U32, f"g_c{b}_{lo}")
-            g_s[unit] = held([P, n], U8, f"g_s{b}_{lo}")
-            for first, last in halves(unit):
-                quantize(g_c[unit][:, first:last], g_s[unit][:, first:last], g_bf[unit][:, first * PACK : last * PACK])
-
-        def back_project(unit, new_bank):
-            b, lo, n = unit
+        def back_project(lo, n, new_bank):
             per_bank = BANK // n
             banks = [new_bank() for x in range(PACK // per_bank)]
+            cols = slice(lo, lo + n)
             for j in range(PACK):
                 dst = banks[j // per_bank][:, (j % per_bank) * n : (j % per_bank + 1) * n]
-                for source in (units[lo // BANK], unit):
-                    r_pass = source[0]
-                    cols = slice(lo - source[1], lo - source[1] + n)
+                for b in range(R_PASSES):
+                    rows = slice(b * BANK + j * P, b * BANK + (j + 1) * P)
                     nc.tensor.matmul_mx(
                         out=dst,
-                        lhsT=wr_c[r_pass][:, j * P : (j + 1) * P].bitcast(FP8X4),
-                        lhsT_scale=wr_s[r_pass][:, j * P : (j + 1) * P],
-                        rhs=g_c[source][:, cols].bitcast(FP8X4),
-                        rhs_scale=g_s[source][:, cols],
-                        start=(r_pass == 0),
-                        stop=(r_pass == R_PASSES - 1),
+                        lhsT=wr_c[:, rows].bitcast(FP8X4),
+                        lhsT_scale=wr_s[:, rows],
+                        rhs=g_c[b][:, cols].bitcast(FP8X4),
+                        rhs_scale=g_s[b][:, cols],
+                        start=(b == 0),
+                        stop=(b == R_PASSES - 1),
                     )
             return banks
 
-        def store(unit, banks):
-            b, lo, n = unit
+        def store(lo, n, banks, vector_banks):
             per_bank = BANK // n
             staged = ringed([P, PACK * n], F32, "table_then_stage", STAGE_BUFS)
             for x, bank in enumerate(banks):
                 part = staged[:, x * BANK : (x + 1) * BANK]
-                if unit == units[-1] and x == len(banks) - 1:
-                    nc.vector.tensor_copy(part, bank[:])
-                else:
-                    nc.scalar.copy(part, bank[:])
+                copy = nc.vector.tensor_copy if x >= len(banks) - vector_banks else nc.scalar.copy
+                copy(part, bank[:])
                 nc.sync.dma_start(
                     out_v[:, x * per_bank : (x + 1) * per_bank, lo : lo + n], part.rearrange("p (j c) -> p j c", c=n)
                 )
 
+        half = CHUNKS // 2
         for c in range(CHUNKS):
-            for i in range(FIRST_TILES):
-                project(i, c)
+            project(0, c, False)
+        for c in range(CHUNKS):
+            project(1, c, c < half)
+        banks_of_a = [(i, c) for i in range(2, ROW_TILES) for c in range(CHUNKS)]
+        on_scalar = [(2, 0), (3, 1), (3, 2), (3, 3)]
+        on_vector = [bank for bank in banks_of_a if bank not in on_scalar]
 
-        urgent = [[(i, c) for c in range(CHUNKS)] for i in range(FIRST_TILES, PACK)]
-        spread = [
-            [(i, c) for c in range(first, first + CHUNKS // 2)]
-            for i in range(PACK, ROW_TILES)
-            for first in (0, CHUNKS // 2)
-        ]
-        projections = urgent + spread
+        ranges = []
+        lo = 0
+        for n in LAST_WIDTHS:
+            ranges.append((lo, n))
+            lo = lo + n
+        steps = [(i, 0, NP) for i in range(PACK)]
+        steps = steps + [(i, lo, n) for lo, n in ranges for i in range(PACK, ROW_TILES)]
+        gathers = steps[: 2 * PACK] + [(i, BANK, BANK) for i in range(PACK, ROW_TILES)]
 
-        out_banks = {}
-        for step in range(len(steps) + 2):
+        for c in range(3):
+            project(*on_scalar.pop(0), False)
+        for step in range(len(steps) + 1):
+            if step < len(gathers):
+                i = gathers[step][0]
+                residual(*gathers[step])
+                while len(on_vector) > 0 and on_vector[0] <= (i + 2, 0):
+                    project(*on_vector.pop(0), True)
             if step < len(steps):
-                unit, t = steps[step]
-                residual(unit, t)
-                if step >= PACK and t == PACK - 2:
-                    weigh(steps[step - PACK][0])
-                if step >= PACK and t == PACK - 1:
-                    done = steps[step - PACK][0]
-                    quantize_g(done)
-                    if done[0] == R_PASSES - 1:
-                        out_banks[done] = back_project(done, parked_bank if done[2] == BANK else stream_bank)
-            if 1 <= step <= len(steps):
-                square(*steps[step - 1])
-            if step < len(projections):
-                for i, c in projections[step]:
-                    project(i, c)
-            if step >= 2:
-                invert(*steps[step - 2])
-            if 1 <= step <= len(steps):
-                denominator(*steps[step - 1])
-            if step >= 2:
-                resquare(*steps[step - 2])
-        weigh(units[-1])
-        quantize_g(units[-1])
-        out_banks[units[-1]] = back_project(units[-1], stream_bank)
-        for unit in units[R_PASSES:]:
-            store(unit, out_banks[unit])
+                square(*steps[step])
+            if step > 0:
+                invert(*steps[step - 1])
+            if step in (0,) and len(on_scalar) > 0:
+                project(*on_scalar.pop(0), False)
+            if step < len(steps):
+                denominator(*steps[step])
+            if step in (0,) and len(on_scalar) > 0:
+                project(*on_scalar.pop(0), False)
+            if step > 0:
+                resquare(*steps[step - 1], False)
+
+        for lo, n in ranges:
+            if lo % BANK == 0:
+                weigh(0, lo, BANK)
+            weigh(1, lo, n)
+            banks = back_project(lo, n, parked_bank if n == BANK else stream_bank)
+            store(lo, n, banks, {0: 0, 512: 0, 768: 1}[lo])

@@ -32,10 +32,9 @@ ALIGN = 64
 WIDE_BUFS = 6
 ROUNDED_BUFS = 5
 SCAN_BUFS = 3
-STAGE_BUFS = 3
 HALF_PSUM = 4
-LATE_B = 2
-LAST_WIDTHS = (512, 256, 256)
+LATE_B = 0
+LAST_WIDTHS = (512, 256, 128, 128)
 
 
 def tile_list_submap_robust_gradient_kernel(
@@ -114,7 +113,7 @@ def tile_list_submap_robust_gradient_kernel(
         def load_w(b):
             nc.sync.dma_start(w_raw[b][:], w_v[:, :, b * BANK : (b + 1) * BANK])
 
-        tab_w = ringed([P, T], I32, "table_then_stage", STAGE_BUFS)
+        tab_w = ringed([P, T], I32, "table_then_stage", 1)
         wc_w_raw = held([P, H // 2], I32, "wc_w_raw")
 
         nc.sync.dma_start(list_tab[:], offs)
@@ -125,13 +124,13 @@ def tile_list_submap_robust_gradient_kernel(
         load_scan(0, 0)
         load_w(0)
         load_scan(0, 1)
-        load_plane(1)
-        load_scan(1, 0)
+        load_plane(2)
+        load_scan(2, 0)
         load_w(1)
         nc.sync.dma_start(tab_w[:], tab_words[0].rearrange("p t i -> p (t i)").bitcast(I32))
         load_scale_rows(wc_s_raw, wc_scales[0])
         nc.sync.dma_start(wc_w_raw[:], wc_words[0].bitcast(I32))
-        for j in range(2, PACK):
+        for j in (1, 3):
             load_plane(j)
             load_scan(j, 0)
         for b in range(R_PASSES):
@@ -147,11 +146,12 @@ def tile_list_submap_robust_gradient_kernel(
                 nc.vector.tensor_copy(page[j][:].indirect(entries), scan[j][:, lo:hi])
 
         def round_plane(j, first, last):
-            slots = pairs[:].rearrange("p (c h n e) -> p c h n e", c=CHUNKS, h=2, e=2)
-            nc.scalar.copy(
-                slots[:, first:last, j // 2, :, j % 2],
-                page[j][:, first * BANK : last * BANK].rearrange("p (c n) -> p c n", n=BANK),
-            )
+            slots = pairs[:].rearrange("p (c h n e) -> p c h n e", c=CHUNKS, h=2, e=2)[:, first:last, j // 2, :, j % 2]
+            values = page[j][:, first * BANK : last * BANK].rearrange("p (c n) -> p c n", n=BANK)
+            if j < 2:
+                nc.gpsimd.tensor_scalar(slots, values, 1.0, 0.0, ALU.mult, ALU.add)
+            else:
+                nc.scalar.copy(slots, values)
 
         wk_bf = []
         wr_bf = []
@@ -217,7 +217,7 @@ def tile_list_submap_robust_gradient_kernel(
         round_w(0)
         turn_w(0)
         quantize(wk_c[0][:], wk_s[0][:], wk_bf[0][:])
-        scatter(1)
+        scatter(2)
         round_w(1)
         turn_w(1)
         quantize(wk_c[1][:], wk_s[1][:], wk_bf[1][:])
@@ -232,8 +232,9 @@ def tile_list_submap_robust_gradient_kernel(
         )
         pairs = ringed([P, T * PACK], BF16, "w_then_pairs", 1)
         round_plane(0, 0, CHUNKS)
+        round_plane(2, 0, CHUNKS)
+        scatter(1)
         round_plane(1, 0, CHUNKS)
-        scatter(2)
         for i in range(ROW_TILES - LATE_B):
             map_side(i)
         prec_col = held([P, ROW_TILES], F32, "prec_col")
@@ -242,7 +243,6 @@ def tile_list_submap_robust_gradient_kernel(
         nc.tensor.transpose(prec_bank[:, 0:P], prec_rows[:], ident[:])
         nc.scalar.copy(prec_col[:], prec_bank[:, 0:ROW_TILES])
         nc.vector.reciprocal(prec_inv[:], prec_col[:])
-        round_plane(2, 0, CHUNKS)
         scatter(3)
         for c in range(CHUNKS):
             round_plane(3, c, c + 1)
@@ -301,9 +301,10 @@ def tile_list_submap_robust_gradient_kernel(
                 resid[b][:, t, lo : lo + n], a_sb[i][:].indirect(entries), chain[b][:, t, lo : lo + n], ALU.subtract
             )
 
-        def square(i, lo, n):
+        def square(i, lo, n, tiles=1):
             b, t = divmod(i, PACK)
-            nc.scalar.activation(chain[b][:, t, lo : lo + n], resid[b][:, t, lo : lo + n], ACT.Square)
+            part = (slice(None), slice(t, t + tiles), slice(lo, lo + n))
+            nc.scalar.activation(chain[b][part], resid[b][part], ACT.Square)
 
         def denominator(i, lo, n):
             b, t = divmod(i, PACK)
@@ -315,9 +316,9 @@ def tile_list_submap_robust_gradient_kernel(
             z = chain[b][:, t, lo : lo + n]
             nc.scalar.activation(z, z, ACT.Abs_reciprocal_sqrt, scale=prec_inv[:, i : i + 1])
 
-        def resquare(i, lo, n, on_vector):
+        def resquare(i, lo, n, on_vector, tiles=1):
             b, t = divmod(i, PACK)
-            z = chain[b][:, t, lo : lo + n]
+            z = chain[b][:, t : t + tiles, lo : lo + n]
             if on_vector:
                 nc.vector.tensor_tensor(z, z, z, ALU.mult)
             else:
@@ -338,77 +339,95 @@ def tile_list_submap_robust_gradient_kernel(
                 quantize(g_c[b][:, cols], g_s[b][:, cols], g_bf[:, first * PACK : last * PACK])
 
         def back_project(lo, n, new_bank):
-            per_bank = BANK // n
+            per_bank = min(BANK // n, 2)
             banks = [new_bank() for x in range(PACK // per_bank)]
             cols = slice(lo, lo + n)
-            for j in range(PACK):
-                dst = banks[j // per_bank][:, (j % per_bank) * n : (j % per_bank + 1) * n]
-                for b in range(R_PASSES):
+            for b in range(R_PASSES):
+                for j in range(PACK):
+                    place = j % per_bank
                     rows = slice(b * BANK + j * P, b * BANK + (j + 1) * P)
                     nc.tensor.matmul_mx(
-                        out=dst,
+                        out=banks[j // per_bank][:, place * n : (place + 1) * n],
                         lhsT=wr_c[:, rows].bitcast(FP8X4),
                         lhsT_scale=wr_s[:, rows],
                         rhs=g_c[b][:, cols].bitcast(FP8X4),
                         rhs_scale=g_s[b][:, cols],
-                        start=(b == 0),
-                        stop=(b == R_PASSES - 1),
+                        start=(b == 0 and place == 0),
+                        stop=(b == R_PASSES - 1 and place == per_bank - 1),
                     )
             return banks
 
-        def store(lo, n, banks, vector_banks):
-            per_bank = BANK // n
-            staged = ringed([P, PACK * n], F32, "table_then_stage", STAGE_BUFS)
-            for x, bank in enumerate(banks):
-                part = staged[:, x * BANK : (x + 1) * BANK]
-                copy = nc.vector.tensor_copy if x >= len(banks) - vector_banks else nc.scalar.copy
-                copy(part, bank[:])
+        def store(lo, n, banks, which, copy):
+            per_bank = PACK // len(banks)
+            for x in which:
+                part = staged[lo][:, x * per_bank * n : (x + 1) * per_bank * n]
+                copy(part, banks[x][:, 0 : per_bank * n])
                 nc.sync.dma_start(
                     out_v[:, x * per_bank : (x + 1) * per_bank, lo : lo + n], part.rearrange("p (j c) -> p j c", c=n)
                 )
 
-        half = CHUNKS // 2
-        for c in range(CHUNKS):
-            project(0, c, False)
-        for c in range(CHUNKS):
-            project(1, c, c < half)
-        banks_of_a = [(i, c) for i in range(2, ROW_TILES) for c in range(CHUNKS)]
-        on_scalar = [(2, 0), (3, 1), (3, 2), (3, 3)]
-        on_vector = [bank for bank in banks_of_a if bank not in on_scalar]
+        banks_of_a = [(i, c) for i in range(ROW_TILES) for c in range(CHUNKS)]
+        first_scalar = [(0, 0), (1, 0), (0, 1), (1, 1), (0, 2), (0, 3), (1, 2), (1, 3), (3, 1), (3, 2), (3, 3)]
+        first_vector = [(2, 0), (2, 1), (2, 2)]
+        on_scalar = [(4, 1)]
+        on_vector = [bank for bank in banks_of_a if bank not in first_scalar + first_vector + on_scalar]
+        for i, c in first_scalar[: 2 * CHUNKS]:
+            project(i, c, False)
+        for i, c in first_vector:
+            project(i, c, True)
+        for i, c in first_scalar[2 * CHUNKS :]:
+            project(i, c, False)
 
         ranges = []
         lo = 0
         for n in LAST_WIDTHS:
             ranges.append((lo, n))
             lo = lo + n
-        steps = [(i, 0, NP) for i in range(PACK)]
-        steps = steps + [(i, lo, n) for lo, n in ranges for i in range(PACK, ROW_TILES)]
-        gathers = steps[: 2 * PACK] + [(i, BANK, BANK) for i in range(PACK, ROW_TILES)]
+        steps = [(i, 0, NP) for i in range(PACK)] + [(i, 0, BANK) for i in range(PACK, ROW_TILES)]
+        gathers = steps + [(i, BANK, BANK) for i in range(PACK, ROW_TILES)]
 
-        for c in range(3):
-            project(*on_scalar.pop(0), False)
-        for step in range(len(steps) + 1):
-            if step < len(gathers):
-                i = gathers[step][0]
-                residual(*gathers[step])
-                while len(on_vector) > 0 and on_vector[0] <= (i + 2, 0):
-                    project(*on_vector.pop(0), True)
+        for step, (i, lo, n) in enumerate(gathers):
+            residual(i, lo, n)
+            while len(on_vector) > 0 and on_vector[0] <= (i + 2, 0):
+                project(*on_vector.pop(0), True)
             if step < len(steps):
-                square(*steps[step])
-            if step > 0:
-                invert(*steps[step - 1])
-            if step in (0,) and len(on_scalar) > 0:
-                project(*on_scalar.pop(0), False)
-            if step < len(steps):
-                denominator(*steps[step])
-            if step in (0,) and len(on_scalar) > 0:
-                project(*on_scalar.pop(0), False)
-            if step > 0:
-                resquare(*steps[step - 1], False)
+                square(i, lo, n)
+                if step > 0:
+                    invert(*steps[step - 1])
+                if step == 0:
+                    for bank in on_scalar:
+                        project(*bank, False)
+                denominator(i, lo, n)
+                if step > 0:
+                    resquare(*steps[step - 1], False)
 
-        for lo, n in ranges:
-            if lo % BANK == 0:
-                weigh(0, lo, BANK)
-            weigh(1, lo, n)
-            banks = back_project(lo, n, parked_bank if n == BANK else stream_bank)
-            store(lo, n, banks, {0: 0, 512: 0, 768: 1}[lo])
+        staged = {0: ringed([P, PACK * BANK], F32, "table_then_stage", 1)}
+        for lo, n in ranges[1:]:
+            staged[lo] = held([P, PACK * n], F32, f"staged{lo}")
+
+        def narrow_chain(lo, n, behind):
+            square(PACK, lo, n, PACK)
+            resquare(*behind)
+            for link in (denominator, invert):
+                for i in range(PACK, ROW_TILES):
+                    link(i, lo, n)
+
+        wide, middle, narrow, last = ranges
+        invert(*steps[-1])
+        narrow_chain(*middle, steps[-1] + (False, 1))
+        weigh(0, 0, BANK)
+        weigh(1, *wide)
+        banks = back_project(*wide, parked_bank)
+        store(*wide, banks, range(2), nc.vector.tensor_copy)
+        narrow_chain(*narrow, (PACK, *middle, False, PACK))
+        store(*wide, banks, range(2, PACK), nc.scalar.copy)
+        narrow_chain(*last, (PACK, *narrow, False, PACK))
+        weigh(0, BANK, BANK)
+        for part in (middle, narrow):
+            weigh(1, *part)
+            store(*part, back_project(*part, stream_bank), range(2), nc.scalar.copy)
+        resquare(PACK, *last, True, PACK)
+        weigh(1, *last)
+        banks = back_project(*last, parked_bank)
+        store(*last, banks, [0], nc.vector.tensor_copy)
+        store(*last, banks, [1], nc.scalar.copy)

@@ -33,7 +33,7 @@ WIDE_BUFS = 6
 ROUNDED_BUFS = 5
 SCAN_BUFS = 3
 HALF_PSUM = 4
-LATE_B = 0
+LATE_B = 2
 LAST_WIDTHS = (512, 256, 128, 128)
 
 
@@ -122,15 +122,15 @@ def tile_list_submap_robust_gradient_kernel(
         nc.sync.dma_start(list_page[:], offs2)
         load_plane(0)
         load_scan(0, 0)
-        load_w(0)
         load_scan(0, 1)
-        load_plane(2)
-        load_scan(2, 0)
+        load_w(0)
+        load_plane(1)
+        load_scan(1, 0)
         load_w(1)
-        nc.sync.dma_start(tab_w[:], tab_words[0].rearrange("p t i -> p (t i)").bitcast(I32))
         load_scale_rows(wc_s_raw, wc_scales[0])
         nc.sync.dma_start(wc_w_raw[:], wc_words[0].bitcast(I32))
-        for j in (1, 3):
+        nc.sync.dma_start(tab_w[:], tab_words[0].rearrange("p t i -> p (t i)").bitcast(I32))
+        for j in range(2, PACK):
             load_plane(j)
             load_scan(j, 0)
         for b in range(R_PASSES):
@@ -148,10 +148,7 @@ def tile_list_submap_robust_gradient_kernel(
         def round_plane(j, first, last):
             slots = pairs[:].rearrange("p (c h n e) -> p c h n e", c=CHUNKS, h=2, e=2)[:, first:last, j // 2, :, j % 2]
             values = page[j][:, first * BANK : last * BANK].rearrange("p (c n) -> p c n", n=BANK)
-            if j < 2:
-                nc.gpsimd.tensor_scalar(slots, values, 1.0, 0.0, ALU.mult, ALU.add)
-            else:
-                nc.scalar.copy(slots, values)
+            nc.scalar.copy(slots, values)
 
         wk_bf = []
         wr_bf = []
@@ -217,24 +214,23 @@ def tile_list_submap_robust_gradient_kernel(
         round_w(0)
         turn_w(0)
         quantize(wk_c[0][:], wk_s[0][:], wk_bf[0][:])
-        scatter(2)
+        scatter(1)
         round_w(1)
         turn_w(1)
         quantize(wk_c[1][:], wk_s[1][:], wk_bf[1][:])
         nc.vector.tensor_copy(v_c[:], tab_w[:].bitcast(U32).indirect(list_tab[:]))
-        nc.vector.tensor_copy(
+        nc.gpsimd.tensor_copy(
             wc_w[:].rearrange("p (b t s x) -> p b t s x", b=R_PASSES, t=PACK, x=RUN // 2),
             wc_w_raw[:].rearrange("p (b s t x) -> p b t s x", b=R_PASSES, t=PACK, x=RUN // 2),
         )
-        nc.vector.tensor_copy(
+        nc.gpsimd.tensor_copy(
             wc_s[:].bitcast(I32).rearrange("p (b t s x) -> p b t s x", b=R_PASSES, t=PACK, x=RUN // 4),
             wc_s_raw[:].bitcast(I32).rearrange("p (b s t x) -> p b t s x", b=R_PASSES, t=PACK, x=RUN // 4),
         )
         pairs = ringed([P, T * PACK], BF16, "w_then_pairs", 1)
         round_plane(0, 0, CHUNKS)
-        round_plane(2, 0, CHUNKS)
-        scatter(1)
         round_plane(1, 0, CHUNKS)
+        scatter(2)
         for i in range(ROW_TILES - LATE_B):
             map_side(i)
         prec_col = held([P, ROW_TILES], F32, "prec_col")
@@ -243,6 +239,7 @@ def tile_list_submap_robust_gradient_kernel(
         nc.tensor.transpose(prec_bank[:, 0:P], prec_rows[:], ident[:])
         nc.scalar.copy(prec_col[:], prec_bank[:, 0:ROW_TILES])
         nc.vector.reciprocal(prec_inv[:], prec_col[:])
+        round_plane(2, 0, CHUNKS)
         scatter(3)
         for c in range(CHUNKS):
             round_plane(3, c, c + 1)
@@ -367,15 +364,15 @@ def tile_list_submap_robust_gradient_kernel(
                 )
 
         banks_of_a = [(i, c) for i in range(ROW_TILES) for c in range(CHUNKS)]
-        first_scalar = [(0, 0), (1, 0), (0, 1), (1, 1), (0, 2), (0, 3), (1, 2), (1, 3), (3, 1), (3, 2), (3, 3)]
-        first_vector = [(2, 0), (2, 1), (2, 2)]
+        first_scalar = [(0, 0), (0, 1), (0, 2), (0, 3), (1, 3), (2, 0), (3, 1), (3, 2), (3, 3)]
+        first_vector = [(1, 0), (1, 1), (1, 2)]
         on_scalar = [(4, 1)]
         on_vector = [bank for bank in banks_of_a if bank not in first_scalar + first_vector + on_scalar]
-        for i, c in first_scalar[: 2 * CHUNKS]:
+        for i, c in first_scalar[: CHUNKS]:
             project(i, c, False)
         for i, c in first_vector:
             project(i, c, True)
-        for i, c in first_scalar[2 * CHUNKS :]:
+        for i, c in first_scalar[CHUNKS :]:
             project(i, c, False)
 
         ranges = []
@@ -418,9 +415,9 @@ def tile_list_submap_robust_gradient_kernel(
         weigh(0, 0, BANK)
         weigh(1, *wide)
         banks = back_project(*wide, parked_bank)
-        store(*wide, banks, range(2), nc.vector.tensor_copy)
+        store(*wide, banks, range(1), nc.vector.tensor_copy)
         narrow_chain(*narrow, (PACK, *middle, False, PACK))
-        store(*wide, banks, range(2, PACK), nc.scalar.copy)
+        store(*wide, banks, range(1, PACK), nc.scalar.copy)
         narrow_chain(*last, (PACK, *narrow, False, PACK))
         weigh(0, BANK, BANK)
         for part in (middle, narrow):

@@ -34,7 +34,7 @@ ROUNDED_BUFS = 5
 SCAN_BUFS = 3
 HALF_PSUM = 4
 LATE_B = 2
-LAST_WIDTHS = (512, 256, 128, 128)
+LAST_WIDTHS = (256, 256, 256, 128, 128)
 
 
 def tile_list_submap_robust_gradient_kernel(
@@ -118,7 +118,7 @@ def tile_list_submap_robust_gradient_kernel(
 
         nc.sync.dma_start(list_tab[:], offs)
         load_scale_rows(tab_s, tab_scales[0])
-        nc.scalar.activation(warm[:, 1:2], warm[:, 0:1], ACT.Abs_reciprocal_sqrt)
+        nc.scalar.activation(warm[:, 1:2], warm[:, 0:1], ACT.Ln)
         nc.sync.dma_start(list_page[:], offs2)
         load_plane(0)
         load_scan(0, 0)
@@ -162,7 +162,7 @@ def tile_list_submap_robust_gradient_kernel(
                 w_raw[b][:].rearrange("p j (s t u) -> p s t j u", t=PACK, u=RUN),
             )
 
-        def turn_w(b):
+        def turn_w(b, copy):
             turned = rounded_tile(BANK)
             wr_bf.append(turned)
             words = wk_bf[b][:].bitcast(F32)
@@ -172,7 +172,7 @@ def tile_list_submap_robust_gradient_kernel(
                     nc.tensor.transpose(
                         bank[:, t * P : (t + 1) * P], words[:, 2 * P * t + h : 2 * P * (t + 1) : 2], ident[:]
                     )
-                nc.scalar.copy(
+                copy(
                     turned[:, h * 2 * BANK : (h + 1) * 2 * BANK].rearrange("m (e p t) -> m e p t", e=2, t=PACK),
                     bank[:].bitcast(BF16).rearrange("m (t p e) -> m e p t", t=PACK, e=2),
                 )
@@ -212,11 +212,11 @@ def tile_list_submap_robust_gradient_kernel(
         nc.vector.tensor_copy(v_s[:], tab_s[:].indirect(list_tab[:]))
         scatter(0)
         round_w(0)
-        turn_w(0)
+        turn_w(0, nc.scalar.copy)
         quantize(wk_c[0][:], wk_s[0][:], wk_bf[0][:])
         scatter(1)
         round_w(1)
-        turn_w(1)
+        turn_w(1, nc.scalar.copy)
         quantize(wk_c[1][:], wk_s[1][:], wk_bf[1][:])
         nc.vector.tensor_copy(v_c[:], tab_w[:].bitcast(U32).indirect(list_tab[:]))
         nc.gpsimd.tensor_copy(
@@ -234,11 +234,11 @@ def tile_list_submap_robust_gradient_kernel(
         for i in range(ROW_TILES - LATE_B):
             map_side(i)
         prec_col = held([P, ROW_TILES], F32, "prec_col")
-        prec_inv = held([P, ROW_TILES], F32, "prec_inv")
+        prec_log = held([P, ROW_TILES], F32, "prec_log")
         prec_bank = stream_bank()
         nc.tensor.transpose(prec_bank[:, 0:P], prec_rows[:], ident[:])
         nc.scalar.copy(prec_col[:], prec_bank[:, 0:ROW_TILES])
-        nc.vector.reciprocal(prec_inv[:], prec_col[:])
+        nc.scalar.activation(prec_log[:], prec_bank[:, 0:ROW_TILES], ACT.Ln)
         round_plane(2, 0, CHUNKS)
         scatter(3)
         for c in range(CHUNKS):
@@ -298,37 +298,34 @@ def tile_list_submap_robust_gradient_kernel(
                 resid[b][:, t, lo : lo + n], a_sb[i][:].indirect(entries), chain[b][:, t, lo : lo + n], ALU.subtract
             )
 
-        def square(i, lo, n, tiles=1):
+        def square(i, lo, n):
             b, t = divmod(i, PACK)
-            part = (slice(None), slice(t, t + tiles), slice(lo, lo + n))
-            nc.scalar.activation(chain[b][part], resid[b][part], ACT.Square)
-
-        def denominator(i, lo, n):
-            b, t = divmod(i, PACK)
-            z = chain[b][:, t, lo : lo + n]
-            nc.scalar.activation(z, z, ACT.Square, bias=1.0, scale=prec_col[:, i : i + 1])
-
-        def invert(i, lo, n):
-            b, t = divmod(i, PACK)
-            z = chain[b][:, t, lo : lo + n]
-            nc.scalar.activation(z, z, ACT.Abs_reciprocal_sqrt, scale=prec_inv[:, i : i + 1])
-
-        def resquare(i, lo, n, on_vector, tiles=1):
-            b, t = divmod(i, PACK)
-            z = chain[b][:, t : t + tiles, lo : lo + n]
-            if on_vector:
-                nc.vector.tensor_tensor(z, z, z, ALU.mult)
+            e = resid[b][:, t, lo : lo + n]
+            if i in (7,):
+                nc.vector.tensor_tensor(chain[b][:, t, lo : lo + n], e, e, ALU.mult)
             else:
-                nc.scalar.activation(z, z, ACT.Square)
+                nc.scalar.activation(chain[b][:, t, lo : lo + n], e, ACT.Square)
 
-        def weigh(b, lo, n):
+        def log_denominator(i, lo, n):
+            b, t = divmod(i, PACK)
+            z = chain[b][:, t, lo : lo + n]
+            nc.scalar.activation(z, z, ACT.Ln, bias=1.0, scale=prec_col[:, i : i + 1])
+
+        def weight(b, lo, n, dst):
+            for t in range(PACK):
+                i = b * PACK + t
+                nc.scalar.activation(
+                    dst[:, t, :], chain[b][:, t, lo : lo + n], ACT.Exp, bias=prec_log[:, i : i + 1], scale=-2.0
+                )
+
+        def weigh(b, lo, n, weights):
             g_bf = rounded_tile(n)
             halves = [(0, n // 2), (n // 2, n)]
             for first, last in halves:
                 nc.vector.tensor_tensor(
                     g_bf[:, first * PACK : last * PACK].rearrange("p (c i t) -> p c t i", i=LINE, t=PACK),
                     resid[b][:, :, lo + first : lo + last].rearrange("p t (c i) -> p c t i", i=LINE),
-                    chain[b][:, :, lo + first : lo + last].rearrange("p t (c i) -> p c t i", i=LINE),
+                    weights[:, :, first:last].rearrange("p t (c i) -> p c t i", i=LINE),
                     ALU.mult,
                 )
             for first, last in halves:
@@ -364,67 +361,64 @@ def tile_list_submap_robust_gradient_kernel(
                 )
 
         banks_of_a = [(i, c) for i in range(ROW_TILES) for c in range(CHUNKS)]
-        first_scalar = [(0, 0), (0, 1), (0, 2), (0, 3), (1, 3), (2, 0), (3, 1), (3, 2), (3, 3)]
-        first_vector = [(1, 0), (1, 1), (1, 2)]
-        on_scalar = [(4, 1)]
-        on_vector = [bank for bank in banks_of_a if bank not in first_scalar + first_vector + on_scalar]
-        for i, c in first_scalar[: CHUNKS]:
+        first_scalar = [(0, 0), (0, 1), (0, 2), (0, 3), (1, 3), (2, 0), (2, 1), (2, 2), (2, 3)]
+        first_vector = [(1, 0), (1, 1), (1, 2), (3, 0)]
+        on_scalar = [[(3, 2), (3, 3)], [(4, 3)], [(5, 3)], [(6, 3)]]
+        taken = first_scalar + first_vector + [bank for banks in on_scalar for bank in banks]
+        on_vector = [bank for bank in banks_of_a if bank not in taken]
+        for i, c in first_scalar[:CHUNKS]:
             project(i, c, False)
         for i, c in first_vector:
             project(i, c, True)
-        for i, c in first_scalar[CHUNKS :]:
+        for i, c in first_scalar[CHUNKS:]:
             project(i, c, False)
 
-        ranges = []
-        lo = 0
-        for n in LAST_WIDTHS:
-            ranges.append((lo, n))
-            lo = lo + n
-        steps = [(i, 0, NP) for i in range(PACK)] + [(i, 0, BANK) for i in range(PACK, ROW_TILES)]
-        gathers = steps + [(i, BANK, BANK) for i in range(PACK, ROW_TILES)]
-
-        for step, (i, lo, n) in enumerate(gathers):
-            residual(i, lo, n)
+        for i in range(ROW_TILES):
+            for lo in range(0, NP, BANK if i in (7,) else NP):
+                residual(i, lo, BANK if i in (7,) else NP)
             while len(on_vector) > 0 and on_vector[0] <= (i + 2, 0):
                 project(*on_vector.pop(0), True)
-            if step < len(steps):
-                square(i, lo, n)
-                if step > 0:
-                    invert(*steps[step - 1])
-                if step == 0:
-                    for bank in on_scalar:
-                        project(*bank, False)
-                denominator(i, lo, n)
-                if step > 0:
-                    resquare(*steps[step - 1], False)
+            if i < PACK:
+                square(i, 0, NP)
+                for bank in on_scalar[i]:
+                    project(*bank, False)
+                log_denominator(i, 0, NP)
+            if i == PACK - 1:
+                weight(0, 0, NP, chain[0][:])
+        for i in range(PACK, ROW_TILES + 1):
+            if i < ROW_TILES:
+                for lo in range(0, NP, BANK if i in (7,) else NP):
+                    square(i, lo, BANK if i in (7,) else NP)
+            if i >= PACK + 1:
+                log_denominator(i - 1, 0, NP)
+        weigh(0, 0, BANK, chain[0][:, :, 0:BANK])
+        weigh(0, BANK, 768 - BANK, chain[0][:, :, BANK:768])
 
-        staged = {0: ringed([P, PACK * BANK], F32, "table_then_stage", 1)}
-        for lo, n in ranges[1:]:
-            staged[lo] = held([P, PACK * n], F32, f"staged{lo}")
+        spare = [wide_tile() for x in range(2)]
+        weights = {}
+        lo = 0
+        for n in LAST_WIDTHS:
+            first = PACK * (lo % BANK)
+            weights[lo] = spare[lo // BANK][:, first : first + PACK * n].rearrange("p (t n) -> p t n", t=PACK)
+            weight(1, lo, n, weights[lo])
+            lo = lo + n
 
-        def narrow_chain(lo, n, behind):
-            square(PACK, lo, n, PACK)
-            resquare(*behind)
-            for link in (denominator, invert):
-                for i in range(PACK, ROW_TILES):
-                    link(i, lo, n)
-
-        wide, middle, narrow, last = ranges
-        invert(*steps[-1])
-        narrow_chain(*middle, steps[-1] + (False, 1))
-        weigh(0, 0, BANK)
-        weigh(1, *wide)
-        banks = back_project(*wide, parked_bank)
-        store(*wide, banks, range(1), nc.vector.tensor_copy)
-        narrow_chain(*narrow, (PACK, *middle, False, PACK))
-        store(*wide, banks, range(1, PACK), nc.scalar.copy)
-        narrow_chain(*last, (PACK, *narrow, False, PACK))
-        weigh(0, BANK, BANK)
-        for part in (middle, narrow):
-            weigh(1, *part)
-            store(*part, back_project(*part, stream_bank), range(2), nc.scalar.copy)
-        resquare(PACK, *last, True, PACK)
-        weigh(1, *last)
-        banks = back_project(*last, parked_bank)
-        store(*last, banks, [0], nc.vector.tensor_copy)
-        store(*last, banks, [1], nc.scalar.copy)
+        lo = 0
+        waiting = []
+        staged = {}
+        for x, n in enumerate(LAST_WIDTHS):
+            if lo == 0:
+                staged[lo] = ringed([P, PACK * n], F32, "table_then_stage", 1)
+            else:
+                staged[lo] = held([P, PACK * n], F32, f"staged{lo}")
+            if lo == 768:
+                weigh(0, lo, NP - lo, chain[0][:, :, lo:])
+            weigh(1, lo, n, weights[lo])
+            for part in waiting:
+                k = [0, 0, 0, 0, 0][x - 1]
+                store(*part, range(k), nc.vector.tensor_copy)
+                store(*part, range(k, len(part[2])), nc.scalar.copy)
+            waiting = [(lo, n, back_project(lo, n, parked_bank if x % 2 == 0 else stream_bank))]
+            lo = lo + n
+        store(*waiting[0], [0], nc.vector.tensor_copy)
+        store(*waiting[0], [1], nc.scalar.copy)

@@ -29,7 +29,7 @@ PER_COL = 16
 LINE = 4
 ALIGN = 64
 
-WIDE_BUFS = 6
+WIDE_BUFS = 4
 ROUNDED_BUFS = 5
 SCAN_BUFS = 3
 HALF_PSUM = 4
@@ -277,7 +277,7 @@ def tile_list_submap_robust_gradient_kernel(
         def project(i, c, on_vector):
             b, t = divmod(i, PACK)
             if i not in a_sb:
-                a_sb[i] = wide_tile()
+                a_sb[i] = wide_tile() if i < PACK else ringed([P, T], F32, "late_a", 2)
             bank = parked_bank() if on_vector else stream_bank()
             nc.tensor.matmul_mx(
                 out=bank[:],
@@ -294,14 +294,19 @@ def tile_list_submap_robust_gradient_kernel(
         def residual(i, lo, n):
             b, t = divmod(i, PACK)
             entries = list_pair[:, lo // PER_COL : (lo + n) // PER_COL]
-            nc.vector.tensor_tensor(
-                resid[b][:, t, lo : lo + n], a_sb[i][:].indirect(entries), chain[b][:, t, lo : lo + n], ALU.subtract
-            )
+            e = resid[b][:, t, lo : lo + n]
+            if i in ():
+                nc.vector.tensor_copy(e, a_sb[i][:].indirect(entries))
+                nc.gpsimd.tensor_tensor(e, e, chain[b][:, t, lo : lo + n], ALU.subtract)
+            else:
+                nc.vector.tensor_tensor(e, a_sb[i][:].indirect(entries), chain[b][:, t, lo : lo + n], ALU.subtract)
 
         def square(i, lo, n):
             b, t = divmod(i, PACK)
             e = resid[b][:, t, lo : lo + n]
-            if i in (7,):
+            if i in (4, 5):
+                nc.gpsimd.tensor_tensor(chain[b][:, t, lo : lo + n], e, e, ALU.mult)
+            elif i in (7,):
                 nc.vector.tensor_tensor(chain[b][:, t, lo : lo + n], e, e, ALU.mult)
             else:
                 nc.scalar.activation(chain[b][:, t, lo : lo + n], e, ACT.Square)
@@ -363,7 +368,7 @@ def tile_list_submap_robust_gradient_kernel(
         banks_of_a = [(i, c) for i in range(ROW_TILES) for c in range(CHUNKS)]
         first_scalar = [(0, 0), (0, 1), (0, 2), (0, 3), (1, 3), (2, 0), (2, 1), (2, 2), (2, 3)]
         first_vector = [(1, 0), (1, 1), (1, 2), (3, 0)]
-        on_scalar = [[(3, 2), (3, 3)], [(4, 3)], [(5, 3)], [(6, 3)]]
+        on_scalar = [[(3, 2), (3, 3)], [(4, 1), (4, 2)], [(4, 3)], [(5, 3)]]
         taken = first_scalar + first_vector + [bank for banks in on_scalar for bank in banks]
         on_vector = [bank for bank in banks_of_a if bank not in taken]
         for i, c in first_scalar[:CHUNKS]:
@@ -376,7 +381,7 @@ def tile_list_submap_robust_gradient_kernel(
         for i in range(ROW_TILES):
             for lo in range(0, NP, BANK if i in (7,) else NP):
                 residual(i, lo, BANK if i in (7,) else NP)
-            while len(on_vector) > 0 and on_vector[0] <= (i + 2, 0):
+            while len(on_vector) > 0 and on_vector[0] <= [(2, 0), (3, 1), (4, 0), (5, 3), (6, 3), (9, 0), (9, 0), (9, 0)][i]:
                 project(*on_vector.pop(0), True)
             if i < PACK:
                 square(i, 0, NP)
@@ -392,7 +397,8 @@ def tile_list_submap_robust_gradient_kernel(
             if i >= PACK + 1:
                 log_denominator(i - 1, 0, NP)
         weigh(0, 0, BANK, chain[0][:, :, 0:BANK])
-        weigh(0, BANK, 768 - BANK, chain[0][:, :, BANK:768])
+        for lo, hi in ((BANK, 768), (768, 896)):
+            weigh(0, lo, hi - lo, chain[0][:, :, lo:hi])
 
         spare = [wide_tile() for x in range(2)]
         weights = {}
@@ -411,7 +417,7 @@ def tile_list_submap_robust_gradient_kernel(
                 staged[lo] = ringed([P, PACK * n], F32, "table_then_stage", 1)
             else:
                 staged[lo] = held([P, PACK * n], F32, f"staged{lo}")
-            if lo == 768:
+            if lo == 896:
                 weigh(0, lo, NP - lo, chain[0][:, :, lo:])
             weigh(1, lo, n, weights[lo])
             for part in waiting:

@@ -82,9 +82,7 @@ def tile_list_submap_robust_gradient_kernel(
         wc_s_raw = held([P, H], U8, "wc_s_raw")
         prec_rows = held([P, P], F32, "prec_rows")
         ident = held([P, P], F32, "ident")
-        warm = held([P, 2], F32, "warm")
         nc.gpsimd.memset(tab_s[:].bitcast(I32), 0)
-        nc.gpsimd.memset(warm[:, 0:1], 1.0)
         nc.gpsimd.memset(wc_s_raw[:].bitcast(I32), 0)
         nc.gpsimd.memset(prec_rows[:], 0.0)
         make_identity(nc, ident[:])
@@ -118,11 +116,15 @@ def tile_list_submap_robust_gradient_kernel(
 
         nc.sync.dma_start(list_tab[:], offs)
         load_scale_rows(tab_s, tab_scales[0])
-        nc.scalar.activation(warm[:, 1:2], warm[:, 0:1], ACT.Ln)
         nc.sync.dma_start(list_page[:], offs2)
         load_plane(0)
         load_scan(0, 0)
         load_scan(0, 1)
+        for b in range(R_PASSES):
+            nc.sync.dma_start(
+                prec_rows[PACK * b : PACK * (b + 1), :].rearrange("t (s u) -> t s u", u=RUN),
+                prec[b * BANK : (b + 1) * BANK].rearrange("(s t u) -> t s u", t=PACK, u=RUN),
+            )
         load_w(0)
         load_plane(1)
         load_scan(1, 0)
@@ -133,11 +135,6 @@ def tile_list_submap_robust_gradient_kernel(
         for j in range(2, PACK):
             load_plane(j)
             load_scan(j, 0)
-        for b in range(R_PASSES):
-            nc.sync.dma_start(
-                prec_rows[PACK * b : PACK * (b + 1), :].rearrange("t (s u) -> t s u", u=RUN),
-                prec[b * BANK : (b + 1) * BANK].rearrange("(s t u) -> t s u", t=PACK, u=RUN),
-            )
         nc.sync.dma_start(list_pair[:], offs3)
 
         def scatter(j):
@@ -209,6 +206,12 @@ def tile_list_submap_robust_gradient_kernel(
                 )
                 nc.scalar.copy(chain[b][:, t, cols], bank[:])
 
+        prec_col = held([P, ROW_TILES], F32, "prec_col")
+        prec_log = held([P, ROW_TILES], F32, "prec_log")
+        prec_bank = stream_bank()
+        nc.tensor.transpose(prec_bank[:, 0:P], prec_rows[:], ident[:])
+        nc.scalar.activation(prec_log[:], prec_bank[:, 0:ROW_TILES], ACT.Ln)
+        nc.scalar.copy(prec_col[:], prec_bank[:, 0:ROW_TILES])
         nc.vector.tensor_copy(v_s[:], tab_s[:].indirect(list_tab[:]))
         scatter(0)
         round_w(0)
@@ -233,12 +236,6 @@ def tile_list_submap_robust_gradient_kernel(
         scatter(2)
         for i in range(ROW_TILES - LATE_B):
             map_side(i)
-        prec_col = held([P, ROW_TILES], F32, "prec_col")
-        prec_log = held([P, ROW_TILES], F32, "prec_log")
-        prec_bank = stream_bank()
-        nc.tensor.transpose(prec_bank[:, 0:P], prec_rows[:], ident[:])
-        nc.scalar.copy(prec_col[:], prec_bank[:, 0:ROW_TILES])
-        nc.scalar.activation(prec_log[:], prec_bank[:, 0:ROW_TILES], ACT.Ln)
         round_plane(2, 0, CHUNKS)
         scatter(3)
         for c in range(CHUNKS):

@@ -31,10 +31,9 @@ ALIGN = 64
 
 WIDE_BUFS = 4
 ROUNDED_BUFS = 5
-SCAN_BUFS = 3
 HALF_PSUM = 4
 LATE_B = 2
-LAST_WIDTHS = (256, 256, 256, 128, 128)
+WIDTHS = (256, 256, 256, 128, 128)
 
 
 def tile_list_submap_robust_gradient_kernel(
@@ -93,7 +92,7 @@ def tile_list_submap_robust_gradient_kernel(
         out_v = out.rearrange("(p j) c -> p j c", j=PACK)
 
         page = [wide_tile() for j in range(PACK)]
-        scan = [ringed([P, S], F32, "scan", SCAN_BUFS) for j in range(PACK - 1)]
+        scan = [ringed([P, S], F32, "scan", PACK - 1) for j in range(PACK - 1)]
         scan.append(ringed([P, S], F32, "scan_then_wr", 1))
         w_raw = [ringed([P, PACK, BANK], F32, tag, 1) for tag in ("w_then_resid", "w_then_pairs")]
 
@@ -109,7 +108,10 @@ def tile_list_submap_robust_gradient_kernel(
             nc.sync.dma_start(scan[j][:, lo:hi], xs_v[:, j, lo:hi])
 
         def load_w(b):
-            nc.sync.dma_start(w_raw[b][:], w_v[:, :, b * BANK : (b + 1) * BANK])
+            for lo in range(0, BANK, BANK // 2):
+                nc.sync.dma_start(
+                    w_raw[b][:, :, lo : lo + BANK // 2], w_v[:, :, b * BANK + lo : b * BANK + lo + BANK // 2]
+                )
 
         tab_w = ringed([P, T], I32, "table_then_stage", 1)
         wc_w_raw = held([P, H // 2], I32, "wc_w_raw")
@@ -154,12 +156,12 @@ def tile_list_submap_robust_gradient_kernel(
 
         def round_w(b):
             wk_bf.append(rounded_tile(BANK))
-            nc.scalar.copy(
-                wk_bf[b][:].rearrange("p (t s u j) -> p s t j u", t=PACK, u=RUN, j=PACK),
-                w_raw[b][:].rearrange("p j (s t u) -> p s t j u", t=PACK, u=RUN),
-            )
+            rounded = wk_bf[b][:].rearrange("p (t s u j) -> p s t j u", t=PACK, u=RUN, j=PACK)
+            values = w_raw[b][:].rearrange("p j (s t u) -> p s t j u", t=PACK, u=RUN)
+            for first in range(0, 2 * RUN, RUN):
+                nc.scalar.copy(rounded[:, first : first + RUN], values[:, first : first + RUN])
 
-        def turn_w(b, copy):
+        def turn_w(b):
             turned = rounded_tile(BANK)
             wr_bf.append(turned)
             words = wk_bf[b][:].bitcast(F32)
@@ -169,7 +171,7 @@ def tile_list_submap_robust_gradient_kernel(
                     nc.tensor.transpose(
                         bank[:, t * P : (t + 1) * P], words[:, 2 * P * t + h : 2 * P * (t + 1) : 2], ident[:]
                     )
-                copy(
+                nc.scalar.copy(
                     turned[:, h * 2 * BANK : (h + 1) * 2 * BANK].rearrange("m (e p t) -> m e p t", e=2, t=PACK),
                     bank[:].bitcast(BF16).rearrange("m (t p e) -> m e p t", t=PACK, e=2),
                 )
@@ -215,11 +217,11 @@ def tile_list_submap_robust_gradient_kernel(
         nc.vector.tensor_copy(v_s[:], tab_s[:].indirect(list_tab[:]))
         scatter(0)
         round_w(0)
-        turn_w(0, nc.scalar.copy)
+        turn_w(0)
         quantize(wk_c[0][:], wk_s[0][:], wk_bf[0][:])
         scatter(1)
         round_w(1)
-        turn_w(1, nc.scalar.copy)
+        turn_w(1)
         quantize(wk_c[1][:], wk_s[1][:], wk_bf[1][:])
         nc.vector.tensor_copy(v_c[:], tab_w[:].bitcast(U32).indirect(list_tab[:]))
         nc.gpsimd.tensor_copy(
@@ -291,26 +293,21 @@ def tile_list_submap_robust_gradient_kernel(
         def residual(i, lo, n):
             b, t = divmod(i, PACK)
             entries = list_pair[:, lo // PER_COL : (lo + n) // PER_COL]
-            e = resid[b][:, t, lo : lo + n]
-            if i in ():
-                nc.vector.tensor_copy(e, a_sb[i][:].indirect(entries))
-                nc.gpsimd.tensor_tensor(e, e, chain[b][:, t, lo : lo + n], ALU.subtract)
-            else:
-                nc.vector.tensor_tensor(e, a_sb[i][:].indirect(entries), chain[b][:, t, lo : lo + n], ALU.subtract)
+            nc.vector.tensor_tensor(
+                resid[b][:, t, lo : lo + n], a_sb[i][:].indirect(entries), chain[b][:, t, lo : lo + n], ALU.subtract
+            )
 
-        def square(i, lo, n):
+        def square(i, lo, n, engine):
             b, t = divmod(i, PACK)
             e = resid[b][:, t, lo : lo + n]
-            if i in (4, 5):
-                nc.gpsimd.tensor_tensor(chain[b][:, t, lo : lo + n], e, e, ALU.mult)
-            elif i in (7,):
-                nc.vector.tensor_tensor(chain[b][:, t, lo : lo + n], e, e, ALU.mult)
-            else:
+            if engine == nc.scalar:
                 nc.scalar.activation(chain[b][:, t, lo : lo + n], e, ACT.Square)
+            else:
+                engine.tensor_tensor(chain[b][:, t, lo : lo + n], e, e, ALU.mult)
 
-        def log_denominator(i, lo, n):
+        def log_denominator(i):
             b, t = divmod(i, PACK)
-            z = chain[b][:, t, lo : lo + n]
+            z = chain[b][:, t, :]
             nc.scalar.activation(z, z, ACT.Ln, bias=1.0, scale=prec_col[:, i : i + 1])
 
         def weight(b, lo, n, dst):
@@ -362,66 +359,80 @@ def tile_list_submap_robust_gradient_kernel(
                     out_v[:, x * per_bank : (x + 1) * per_bank, lo : lo + n], part.rearrange("p (j c) -> p j c", c=n)
                 )
 
-        banks_of_a = [(i, c) for i in range(ROW_TILES) for c in range(CHUNKS)]
-        first_scalar = [(0, 0), (0, 1), (0, 2), (0, 3), (1, 3), (2, 0), (2, 1), (2, 2), (2, 3)]
-        first_vector = [(1, 0), (1, 1), (1, 2), (3, 0)]
-        on_scalar = [[(3, 2), (3, 3)], [(4, 1), (4, 2)], [(4, 3)], [(5, 3)]]
-        taken = first_scalar + first_vector + [bank for banks in on_scalar for bank in banks]
-        on_vector = [bank for bank in banks_of_a if bank not in taken]
-        for i, c in first_scalar[:CHUNKS]:
-            project(i, c, False)
-        for i, c in first_vector:
-            project(i, c, True)
-        for i, c in first_scalar[CHUNKS:]:
-            project(i, c, False)
+        def project_chunks(i, first, last, on_vector):
+            for c in range(first, last):
+                project(i, c, on_vector)
 
-        for i in range(ROW_TILES):
-            for lo in range(0, NP, BANK if i in (7,) else NP):
-                residual(i, lo, BANK if i in (7,) else NP)
-            while len(on_vector) > 0 and on_vector[0] <= [(2, 0), (3, 1), (4, 0), (5, 3), (6, 3), (9, 0), (9, 0), (9, 0)][i]:
-                project(*on_vector.pop(0), True)
-            if i < PACK:
-                square(i, 0, NP)
-                for bank in on_scalar[i]:
-                    project(*bank, False)
-                log_denominator(i, 0, NP)
-            if i == PACK - 1:
-                weight(0, 0, NP, chain[0][:])
-        for i in range(PACK, ROW_TILES + 1):
-            if i < ROW_TILES:
-                for lo in range(0, NP, BANK if i in (7,) else NP):
-                    square(i, lo, BANK if i in (7,) else NP)
-            if i >= PACK + 1:
-                log_denominator(i - 1, 0, NP)
-        weigh(0, 0, BANK, chain[0][:, :, 0:BANK])
-        for lo, hi in ((BANK, 768), (768, 896)):
-            weigh(0, lo, hi - lo, chain[0][:, :, lo:hi])
+        last = CHUNKS - 1
+        half = CHUNKS // 2
+        project_chunks(0, 0, CHUNKS, False)
+        project_chunks(1, 0, last, True)
+        project_chunks(3, 0, 1, True)
+        project_chunks(1, last, CHUNKS, False)
+        project_chunks(2, 0, CHUNKS, False)
 
-        spare = [wide_tile() for x in range(2)]
-        weights = {}
+        residual(0, 0, NP)
+        square(0, 0, NP, nc.scalar)
+        project_chunks(3, half, CHUNKS, False)
+        log_denominator(0)
+        residual(1, 0, NP)
+        project_chunks(3, 1, half, True)
+        square(1, 0, NP, nc.scalar)
+        project_chunks(4, 1, last, False)
+        log_denominator(1)
+        residual(2, 0, NP)
+        project_chunks(4, 0, 1, True)
+        square(2, 0, NP, nc.scalar)
+        project_chunks(4, last, CHUNKS, False)
+        log_denominator(2)
+        residual(3, 0, NP)
+        project_chunks(5, 0, last, True)
+        square(3, 0, NP, nc.scalar)
+        project_chunks(5, last, CHUNKS, False)
+        log_denominator(3)
+        weight(0, 0, NP, chain[0][:])
+
+        for i in (4, 5):
+            residual(i, 0, NP)
+            project_chunks(i + 2, 0, CHUNKS, True)
+        residual(6, 0, NP)
+        for lo in range(0, NP, BANK):
+            residual(7, lo, BANK)
+        square(4, 0, NP, nc.gpsimd)
+        square(5, 0, NP, nc.gpsimd)
+        log_denominator(4)
+        square(6, 0, NP, nc.scalar)
+        log_denominator(5)
+        for lo in range(0, NP, BANK):
+            square(7, lo, BANK, nc.vector)
+        log_denominator(6)
+        log_denominator(7)
+
+        ranges = []
         lo = 0
-        for n in LAST_WIDTHS:
+        for n in WIDTHS:
+            ranges.append((lo, n))
+            lo = lo + n
+        for lo, n in [(0, BANK)] + ranges[2:-1]:
+            weigh(0, lo, n, chain[0][:, :, lo : lo + n])
+
+        spare = [wide_tile() for x in range(NP // BANK)]
+        weights = {}
+        for lo, n in ranges:
             first = PACK * (lo % BANK)
             weights[lo] = spare[lo // BANK][:, first : first + PACK * n].rearrange("p (t n) -> p t n", t=PACK)
             weight(1, lo, n, weights[lo])
-            lo = lo + n
 
-        lo = 0
+        staged = {0: ringed([P, PACK * WIDTHS[0]], F32, "table_then_stage", 1)}
         waiting = []
-        staged = {}
-        for x, n in enumerate(LAST_WIDTHS):
-            if lo == 0:
-                staged[lo] = ringed([P, PACK * n], F32, "table_then_stage", 1)
-            else:
+        for x, (lo, n) in enumerate(ranges):
+            if x > 0:
                 staged[lo] = held([P, PACK * n], F32, f"staged{lo}")
-            if lo == 896:
-                weigh(0, lo, NP - lo, chain[0][:, :, lo:])
+            if x == len(ranges) - 1:
+                weigh(0, lo, n, chain[0][:, :, lo : lo + n])
             weigh(1, lo, n, weights[lo])
             for part in waiting:
-                k = [0, 0, 0, 0, 0][x - 1]
-                store(*part, range(k), nc.vector.tensor_copy)
-                store(*part, range(k, len(part[2])), nc.scalar.copy)
+                store(*part, range(2), nc.scalar.copy)
             waiting = [(lo, n, back_project(lo, n, parked_bank if x % 2 == 0 else stream_bank))]
-            lo = lo + n
         store(*waiting[0], [0], nc.vector.tensor_copy)
         store(*waiting[0], [1], nc.scalar.copy)

@@ -32,7 +32,8 @@ ALIGN = 64
 WIDE_BUFS = 4
 ROUNDED_BUFS = 5
 HALF_PSUM = 4
-LATE_B = 2
+LATE_B = 3
+AHEAD = 3
 WIDTHS = (256, 256, 256, 128, 128)
 
 
@@ -97,8 +98,7 @@ def tile_list_submap_robust_gradient_kernel(
         w_raw = [ringed([P, PACK, BANK], F32, tag, 1) for tag in ("w_then_resid", "w_then_pairs")]
 
         def scan_parts(j):
-            parts = 2 if j == 0 else 1
-            return [(h * S // parts, (h + 1) * S // parts) for h in range(parts)]
+            return [(0, S // 4), (S // 4, S)] if j == 0 else [(0, S)]
 
         def load_plane(j):
             nc.sync.dma_start(page[j][:], base_v[:, j, :])
@@ -183,9 +183,9 @@ def tile_list_submap_robust_gradient_kernel(
         wc_codes = wc_w[:].bitcast(U8)
         chain = [held([P, PACK, NP], F32, f"chain{b}") for b in range(R_PASSES)]
 
-        def map_side(i):
-            b, t = divmod(i, PACK)
-            for lo in range(0, NP, BANK):
+        def map_side(banks):
+            for i, lo in banks:
+                b, t = divmod(i, PACK)
                 cols = slice(lo, lo + BANK)
                 bank = stream_bank()
                 nc.tensor.matmul_mx(
@@ -236,14 +236,13 @@ def tile_list_submap_robust_gradient_kernel(
         round_plane(0, 0, CHUNKS)
         round_plane(1, 0, CHUNKS)
         scatter(2)
-        for i in range(ROW_TILES - LATE_B):
-            map_side(i)
+        banks_of_b = [(i, lo) for i in range(ROW_TILES) for lo in range(0, NP, BANK)]
+        map_side(banks_of_b[:-LATE_B])
         round_plane(2, 0, CHUNKS)
         scatter(3)
         for c in range(CHUNKS):
             round_plane(3, c, c + 1)
-        for i in range(ROW_TILES - LATE_B, ROW_TILES):
-            map_side(i)
+        map_side(banks_of_b[-LATE_B:])
 
         wr_c = ringed([P, R_PASSES * BANK], U32, "scan_then_wr", 1)
         wr_s = held([P, R_PASSES * BANK], U8, "wr_s")
@@ -370,10 +369,11 @@ def tile_list_submap_robust_gradient_kernel(
         project_chunks(3, 0, 1, True)
         project_chunks(1, last, CHUNKS, False)
         project_chunks(2, 0, CHUNKS, False)
+        project_chunks(3, half, last, False)
 
         residual(0, 0, NP)
         square(0, 0, NP, nc.scalar)
-        project_chunks(3, half, CHUNKS, False)
+        project_chunks(3, last, CHUNKS, False)
         log_denominator(0)
         residual(1, 0, NP)
         project_chunks(3, 1, half, True)
@@ -421,9 +421,10 @@ def tile_list_submap_robust_gradient_kernel(
         for lo, n in ranges:
             first = PACK * (lo % BANK)
             weights[lo] = spare[lo // BANK][:, first : first + PACK * n].rearrange("p (t n) -> p t n", t=PACK)
-            weight(1, lo, n, weights[lo])
 
         staged = {0: ringed([P, PACK * WIDTHS[0]], F32, "table_then_stage", 1)}
+        for lo, n in ranges[:AHEAD]:
+            weight(1, lo, n, weights[lo])
         waiting = []
         for x, (lo, n) in enumerate(ranges):
             if x > 0:
@@ -433,6 +434,9 @@ def tile_list_submap_robust_gradient_kernel(
             weigh(1, lo, n, weights[lo])
             for part in waiting:
                 store(*part, range(2), nc.scalar.copy)
+            if x == 1:
+                for later in ranges[AHEAD:]:
+                    weight(1, *later, weights[later[0]])
             waiting = [(lo, n, back_project(lo, n, parked_bank if x % 2 == 0 else stream_bank))]
         store(*waiting[0], [0], nc.vector.tensor_copy)
         store(*waiting[0], [1], nc.scalar.copy)

@@ -363,33 +363,25 @@ def tile_list_submap_robust_gradient_kernel(
                 project(i, c, on_vector)
 
         last = CHUNKS - 1
-        half = CHUNKS // 2
         project_chunks(0, 0, CHUNKS, False)
         project_chunks(1, 0, last, True)
         project_chunks(3, 0, 1, True)
-        project_chunks(1, last, CHUNKS, False)
+        project(1, last, False)
         project_chunks(2, 0, CHUNKS, False)
-        project_chunks(3, half, last, False)
+        project(3, last, False)
 
-        residual(0, 0, NP)
-        square(0, 0, NP, nc.scalar)
-        project_chunks(3, last, CHUNKS, False)
-        log_denominator(0)
-        residual(1, 0, NP)
-        project_chunks(3, 1, half, True)
-        square(1, 0, NP, nc.scalar)
-        project_chunks(4, 1, last, False)
-        log_denominator(1)
-        residual(2, 0, NP)
-        project_chunks(4, 0, 1, True)
-        square(2, 0, NP, nc.scalar)
-        project_chunks(4, last, CHUNKS, False)
-        log_denominator(2)
-        residual(3, 0, NP)
-        project_chunks(5, 0, last, True)
-        square(3, 0, NP, nc.scalar)
-        project_chunks(5, last, CHUNKS, False)
-        log_denominator(3)
+        remaining = [(4, c) for c in range(CHUNKS)] + [(5, last)]
+        for i in range(PACK):
+            residual(i, 0, NP)
+            if i == 1:
+                project_chunks(3, 1, last, True)
+            if i == PACK - 1:
+                project_chunks(5, 0, last, True)
+            square(i, 0, NP, nc.scalar)
+            if i == 0:
+                project(*remaining.pop(0), False)
+            project(*remaining.pop(0), False)
+            log_denominator(i)
         weight(0, 0, NP, chain[0][:])
 
         for i in (4, 5):

@@ -31,9 +31,9 @@ ALIGN = 64
 
 WIDE_BUFS = 4
 ROUNDED_BUFS = 5
-HALF_PSUM = 4
-LATE_B = 3
+BANKS = 8
 AHEAD = 3
+LAST = ROW_TILES - 1
 WIDTHS = (256, 256, 256, 128, 128)
 
 
@@ -52,17 +52,20 @@ def tile_list_submap_robust_gradient_kernel(
         def ringed(shape, dtype, tag, bufs):
             return ring.tile(shape, dtype, name=tag, tag=tag, bufs=bufs, align_bytes=ALIGN)
 
-        def wide_tile():
-            return ringed([P, T], F32, "wide", WIDE_BUFS)
+        def wide_tile(x):
+            return ringed([P, T], F32, f"wide{x}", 1)
 
         def rounded_tile(columns):
             return ringed([P, columns * PACK], BF16, "rounded", ROUNDED_BUFS)
 
-        def stream_bank():
-            return psum.tile([P, BANK], F32, name="stream", tag="stream", bufs=HALF_PSUM)
+        turn = [BANKS - 1]
 
-        def parked_bank():
-            return psum.tile([P, BANK], F32, name="parked", tag="parked", bufs=HALF_PSUM)
+        def bank_at(x):
+            return psum.tile([P, BANK], F32, name=f"bank{x}", tag=f"bank{x}", bufs=1)
+
+        def new_bank():
+            turn.append((turn[-1] + 1) % BANKS)
+            return bank_at(turn[-1])
 
         def quantize(codes, scales, rounded):
             nc.vector.quantize_mx(out=codes.bitcast(FP8X4), scales=scales, in_=rounded)
@@ -92,10 +95,14 @@ def tile_list_submap_robust_gradient_kernel(
         w_v = w.rearrange("(p j) r -> p j r", j=PACK)
         out_v = out.rearrange("(p j) c -> p j c", j=PACK)
 
-        page = [wide_tile() for j in range(PACK)]
+        page = [wide_tile(j) for j in range(PACK)]
         scan = [ringed([P, S], F32, "scan", PACK - 1) for j in range(PACK - 1)]
         scan.append(ringed([P, S], F32, "scan_then_wr", 1))
-        w_raw = [ringed([P, PACK, BANK], F32, tag, 1) for tag in ("w_then_resid", "w_then_pairs")]
+        pairs = ringed([P, T * PACK], BF16, "pairs_then_resid", 1)
+        first_w = ringed([P, PACK * BANK], F32, "w_then_resid", 1)
+        w_raw = [
+            values.rearrange("p (j r) -> p j r", j=PACK) for values in (first_w[:], pairs[:, 2 * T :].bitcast(F32))
+        ]
 
         def scan_parts(j):
             return [(0, S // 4), (S // 4, S)] if j == 0 else [(0, S)]
@@ -113,7 +120,7 @@ def tile_list_submap_robust_gradient_kernel(
                     w_raw[b][:, :, lo : lo + BANK // 2], w_v[:, :, b * BANK + lo : b * BANK + lo + BANK // 2]
                 )
 
-        tab_w = ringed([P, T], I32, "table_then_stage", 1)
+        tab_w = ringed([P, T], I32, "table_then_a", 1)
         wc_w_raw = held([P, H // 2], I32, "wc_w_raw")
 
         nc.sync.dma_start(list_tab[:], offs)
@@ -128,13 +135,13 @@ def tile_list_submap_robust_gradient_kernel(
                 prec[b * BANK : (b + 1) * BANK].rearrange("(s t u) -> t s u", t=PACK, u=RUN),
             )
         load_w(0)
-        load_plane(1)
-        load_scan(1, 0)
-        load_w(1)
+        load_plane(2)
+        load_scan(2, 0)
         load_scale_rows(wc_s_raw, wc_scales[0])
         nc.sync.dma_start(wc_w_raw[:], wc_words[0].bitcast(I32))
+        load_w(1)
         nc.sync.dma_start(tab_w[:], tab_words[0].rearrange("p t i -> p (t i)").bitcast(I32))
-        for j in range(2, PACK):
+        for j in (1, 3):
             load_plane(j)
             load_scan(j, 0)
         nc.sync.dma_start(list_pair[:], offs3)
@@ -144,54 +151,60 @@ def tile_list_submap_robust_gradient_kernel(
                 entries = list_page[:, lo // PER_COL : hi // PER_COL]
                 nc.vector.tensor_copy(page[j][:].indirect(entries), scan[j][:, lo:hi])
 
-        def round_plane(j, first, last):
-            slots = pairs[:].rearrange("p (c h n e) -> p c h n e", c=CHUNKS, h=2, e=2)[:, first:last, j // 2, :, j % 2]
-            values = page[j][:, first * BANK : last * BANK].rearrange("p (c n) -> p c n", n=BANK)
-            nc.scalar.copy(slots, values)
+        def round_plane(j, first, last, copy):
+            slots = pairs[:].rearrange("p (h n e) -> p h n e", h=2, e=2)[:, j // 2, first * BANK : last * BANK, j % 2]
+            copy(slots, page[j][:, first * BANK : last * BANK])
 
-        wk_bf = []
-        wr_bf = []
-        wk_c = [held([P, BANK], U32, f"wk_c{b}") for b in range(R_PASSES)]
-        wk_s = [held([P, BANK], U8, f"wk_s{b}") for b in range(R_PASSES)]
+        def round_on_gpsimd(rounded, values):
+            nc.gpsimd.tensor_scalar(rounded, values, 1.0, 0.0, ALU.mult, ALU.add)
+
+        wk_all = ringed([P, H * PACK], BF16, "w_then_wc", 1)
+        wk_bf = [wk_all[:, b * BANK * PACK : (b + 1) * BANK * PACK] for b in range(R_PASSES)]
+        wk_c = held([P, H], U32, "wk_c")
+        wk_s = held([P, H], U8, "wk_s")
 
         def round_w(b):
-            wk_bf.append(rounded_tile(BANK))
-            rounded = wk_bf[b][:].rearrange("p (t s u j) -> p s t j u", t=PACK, u=RUN, j=PACK)
-            values = w_raw[b][:].rearrange("p j (s t u) -> p s t j u", t=PACK, u=RUN)
+            rounded = wk_bf[b].rearrange("p (t s u j) -> p s t j u", t=PACK, u=RUN, j=PACK)
+            values = w_raw[b].rearrange("p j (s t u) -> p s t j u", t=PACK, u=RUN)
             for first in range(0, 2 * RUN, RUN):
                 nc.scalar.copy(rounded[:, first : first + RUN], values[:, first : first + RUN])
 
-        def turn_w(b):
-            turned = rounded_tile(BANK)
-            wr_bf.append(turned)
-            words = wk_bf[b][:].bitcast(F32)
+        def turn_w(b, turned, copy, banks):
+            words = wk_bf[b].bitcast(F32)
             for h in range(2):
-                bank = parked_bank()
+                bank = bank_at(banks[h])
                 for t in range(PACK):
                     nc.tensor.transpose(
                         bank[:, t * P : (t + 1) * P], words[:, 2 * P * t + h : 2 * P * (t + 1) : 2], ident[:]
                     )
-                nc.scalar.copy(
+                copy(
                     turned[:, h * 2 * BANK : (h + 1) * 2 * BANK].rearrange("m (e p t) -> m e p t", e=2, t=PACK),
                     bank[:].bitcast(BF16).rearrange("m (t p e) -> m e p t", t=PACK, e=2),
                 )
 
         v_c = held([P, NP], U32, "v_c")
         v_s = held([P, NP], U8, "v_s")
-        wc_w = held([P, H // 2], I32, "wc_w")
+        wc_w = ringed([P, H // 2], I32, "w_then_wc", 1)
         wc_s = held([P, H], U8, "wc_s")
         wc_codes = wc_w[:].bitcast(U8)
         chain = [held([P, PACK, NP], F32, f"chain{b}") for b in range(R_PASSES)]
 
-        def map_side(banks):
+        early_b = {i: ringed([P, BANK], F32, f"b{i}_then_a", 1) for i in (4, 5)}
+
+        def b_rows(i, lo, n):
+            if i in early_b and lo == 0:
+                return early_b[i][:]
+            return chain[i // PACK][:, i % PACK, lo : lo + n]
+
+        def map_side(banks, copy):
             for i, lo in banks:
                 b, t = divmod(i, PACK)
                 cols = slice(lo, lo + BANK)
-                bank = stream_bank()
+                bank = new_bank()
                 nc.tensor.matmul_mx(
                     out=bank[:],
-                    lhsT=wk_c[b][:, t * P : (t + 1) * P].bitcast(FP8X4),
-                    lhsT_scale=wk_s[b][:, t * P : (t + 1) * P],
+                    lhsT=wk_c[:, i * P : (i + 1) * P].bitcast(FP8X4),
+                    lhsT_scale=wk_s[:, i * P : (i + 1) * P],
                     rhs=v_c[:, cols].bitcast(FP8X4),
                     rhs_scale=v_s[:, cols],
                     start=True,
@@ -206,24 +219,30 @@ def tile_list_submap_robust_gradient_kernel(
                     start=False,
                     stop=True,
                 )
-                nc.scalar.copy(chain[b][:, t, cols], bank[:])
+                copy(b_rows(i, lo, BANK), bank[:])
+
+        def gather_words(lo):
+            entries = list_tab[:, lo // PER_COL : (lo + BANK) // PER_COL]
+            nc.vector.tensor_copy(v_c[:, lo : lo + BANK], tab_w[:].bitcast(U32).indirect(entries))
 
         prec_col = held([P, ROW_TILES], F32, "prec_col")
         prec_log = held([P, ROW_TILES], F32, "prec_log")
-        prec_bank = stream_bank()
+        prec_bank = bank_at(3)
         nc.tensor.transpose(prec_bank[:, 0:P], prec_rows[:], ident[:])
         nc.scalar.activation(prec_log[:], prec_bank[:, 0:ROW_TILES], ACT.Ln)
         nc.scalar.copy(prec_col[:], prec_bank[:, 0:ROW_TILES])
         nc.vector.tensor_copy(v_s[:], tab_s[:].indirect(list_tab[:]))
         scatter(0)
         round_w(0)
-        turn_w(0)
-        quantize(wk_c[0][:], wk_s[0][:], wk_bf[0][:])
-        scatter(1)
+        wr_bf = [rounded_tile(BANK)]
+        turn_w(0, wr_bf[0], nc.scalar.copy, (6, 7))
+        scatter(2)
         round_w(1)
-        turn_w(1)
-        quantize(wk_c[1][:], wk_s[1][:], wk_bf[1][:])
-        nc.vector.tensor_copy(v_c[:], tab_w[:].bitcast(U32).indirect(list_tab[:]))
+        wr_bf.append(rounded_tile(BANK))
+        turn_w(1, wr_bf[1], nc.scalar.copy, (4, 5))
+        quantize(wk_c[:], wk_s[:], wk_all[:])
+        gather_words(0)
+        gather_words(BANK)
         nc.gpsimd.tensor_copy(
             wc_w[:].rearrange("p (b t s x) -> p b t s x", b=R_PASSES, t=PACK, x=RUN // 2),
             wc_w_raw[:].rearrange("p (b s t x) -> p b t s x", b=R_PASSES, t=PACK, x=RUN // 2),
@@ -232,55 +251,59 @@ def tile_list_submap_robust_gradient_kernel(
             wc_s[:].bitcast(I32).rearrange("p (b t s x) -> p b t s x", b=R_PASSES, t=PACK, x=RUN // 4),
             wc_s_raw[:].bitcast(I32).rearrange("p (b s t x) -> p b t s x", b=R_PASSES, t=PACK, x=RUN // 4),
         )
-        pairs = ringed([P, T * PACK], BF16, "w_then_pairs", 1)
-        round_plane(0, 0, CHUNKS)
-        round_plane(1, 0, CHUNKS)
-        scatter(2)
-        banks_of_b = [(i, lo) for i in range(ROW_TILES) for lo in range(0, NP, BANK)]
-        map_side(banks_of_b[:-LATE_B])
-        round_plane(2, 0, CHUNKS)
+        round_plane(0, 0, CHUNKS, round_on_gpsimd)
+        round_plane(2, 0, CHUNKS, nc.scalar.copy)
+        scatter(1)
+        round_plane(1, 0, CHUNKS, round_on_gpsimd)
+        map_side([(i, lo) for lo in range(0, NP, BANK) for i in range(ROW_TILES)], nc.scalar.copy)
         scatter(3)
-        for c in range(CHUNKS):
-            round_plane(3, c, c + 1)
-        map_side(banks_of_b[-LATE_B:])
-
         wr_c = ringed([P, R_PASSES * BANK], U32, "scan_then_wr", 1)
         wr_s = held([P, R_PASSES * BANK], U8, "wr_s")
         for b in range(R_PASSES):
             cols = slice(b * BANK, (b + 1) * BANK)
             quantize(wr_c[:, cols], wr_s[:, cols], wr_bf[b][:])
+        for c in range(CHUNKS):
+            round_plane(3, c, c + 1, nc.scalar.copy)
 
         page_c = [held([P, BANK], U32, f"page_c{c}") for c in range(CHUNKS)]
         page_s = [held([P, BANK], U8, f"page_s{c}") for c in range(CHUNKS)]
         woven = []
 
-        def weave(c):
-            woven.append(rounded_tile(BANK))
-            nc.vector.tensor_copy(
+        def weave(c, copy):
+            last = c == CHUNKS - 1
+            woven.append(ringed([P, BANK * PACK], BF16, "woven_then_a", 1) if last else rounded_tile(BANK))
+            copy(
                 woven[c][:].bitcast(F32).rearrange("p (n h) -> p n h", h=2),
-                pairs[:, c * BANK * PACK : (c + 1) * BANK * PACK].bitcast(F32).rearrange("p (h n) -> p n h", h=2),
+                pairs[:].bitcast(F32).rearrange("p (h n) -> p n h", h=2)[:, c * BANK : (c + 1) * BANK],
             )
 
-        weave(0)
+        weave(0, nc.vector.tensor_copy)
         for c in range(CHUNKS):
             if c + 1 < CHUNKS:
-                weave(c + 1)
+                weave(c + 1, nc.vector.tensor_copy)
             quantize(page_c[c][:], page_s[c][:], woven[c][:])
 
         a_sb = {}
-        resid = [ringed([P, PACK, NP], F32, "w_then_resid", 1), held([P, PACK, NP], F32, "resid1")]
+        resid = [ringed([P, PACK, NP], F32, "w_then_resid", 1), ringed([P, PACK, NP], F32, "pairs_then_resid", 1)]
         g_c = [held([P, NP], U32, f"g_c{b}") for b in range(R_PASSES)]
         g_s = [held([P, NP], U8, f"g_s{b}") for b in range(R_PASSES)]
 
-        def project(i, c, on_vector):
+        def project(i, c, on_vector, x):
             b, t = divmod(i, PACK)
             if i not in a_sb:
-                a_sb[i] = wide_tile() if i < PACK else ringed([P, T], F32, "late_a", 2)
-            bank = parked_bank() if on_vector else stream_bank()
+                if i == 1:
+                    a_sb[i] = ringed([P, T], F32, "woven_then_a", 1)
+                elif i == 5:
+                    a_sb[i] = ringed([P, T], F32, "table_then_a", 1)
+                elif i - 2 in early_b:
+                    a_sb[i] = ringed([P, T], F32, f"b{i - 2}_then_a", 1)
+                else:
+                    a_sb[i] = wide_tile({0: 0, 2: 2, 3: 1, 4: 3}[i])
+            bank = bank_at(x)
             nc.tensor.matmul_mx(
                 out=bank[:],
-                lhsT=wk_c[b][:, t * P : (t + 1) * P].bitcast(FP8X4),
-                lhsT_scale=wk_s[b][:, t * P : (t + 1) * P],
+                lhsT=wk_c[:, i * P : (i + 1) * P].bitcast(FP8X4),
+                lhsT_scale=wk_s[:, i * P : (i + 1) * P],
                 rhs=page_c[c][:].bitcast(FP8X4),
                 rhs_scale=page_s[c][:],
                 start=True,
@@ -293,21 +316,29 @@ def tile_list_submap_robust_gradient_kernel(
             b, t = divmod(i, PACK)
             entries = list_pair[:, lo // PER_COL : (lo + n) // PER_COL]
             nc.vector.tensor_tensor(
-                resid[b][:, t, lo : lo + n], a_sb[i][:].indirect(entries), chain[b][:, t, lo : lo + n], ALU.subtract
+                resid[b][:, t, lo : lo + n], a_sb[i][:].indirect(entries), b_rows(i, lo, n), ALU.subtract
             )
+
+        def square_rows(i):
+            return chain[i // PACK][:, i % PACK, :]
 
         def square(i, lo, n, engine):
             b, t = divmod(i, PACK)
             e = resid[b][:, t, lo : lo + n]
             if engine == nc.scalar:
-                nc.scalar.activation(chain[b][:, t, lo : lo + n], e, ACT.Square)
+                nc.scalar.activation(square_rows(i)[:, lo : lo + n], e, ACT.Square)
             else:
-                engine.tensor_tensor(chain[b][:, t, lo : lo + n], e, e, ALU.mult)
+                engine.tensor_tensor(square_rows(i)[:, lo : lo + n], e, e, ALU.mult)
 
-        def log_denominator(i):
+        def log_denominator(i, lo, n):
             b, t = divmod(i, PACK)
-            z = chain[b][:, t, :]
-            nc.scalar.activation(z, z, ACT.Ln, bias=1.0, scale=prec_col[:, i : i + 1])
+            nc.scalar.activation(
+                chain[b][:, t, lo : lo + n],
+                square_rows(i)[:, lo : lo + n],
+                ACT.Ln,
+                bias=1.0,
+                scale=prec_col[:, i : i + 1],
+            )
 
         def weight(b, lo, n, dst):
             for t in range(PACK):
@@ -318,21 +349,16 @@ def tile_list_submap_robust_gradient_kernel(
 
         def weigh(b, lo, n, weights):
             g_bf = rounded_tile(n)
-            halves = [(0, n // 2), (n // 2, n)]
-            for first, last in halves:
-                nc.vector.tensor_tensor(
-                    g_bf[:, first * PACK : last * PACK].rearrange("p (c i t) -> p c t i", i=LINE, t=PACK),
-                    resid[b][:, :, lo + first : lo + last].rearrange("p t (c i) -> p c t i", i=LINE),
-                    weights[:, :, first:last].rearrange("p t (c i) -> p c t i", i=LINE),
-                    ALU.mult,
-                )
-            for first, last in halves:
-                cols = slice(lo + first, lo + last)
-                quantize(g_c[b][:, cols], g_s[b][:, cols], g_bf[:, first * PACK : last * PACK])
+            nc.vector.tensor_tensor(
+                g_bf[:].rearrange("p (c i t) -> p c t i", i=LINE, t=PACK),
+                resid[b][:, :, lo : lo + n].rearrange("p t (c i) -> p c t i", i=LINE),
+                weights.rearrange("p t (c i) -> p c t i", i=LINE),
+                ALU.mult,
+            )
+            return g_c[b][:, lo : lo + n], g_s[b][:, lo : lo + n], g_bf[:]
 
-        def back_project(lo, n, new_bank):
-            per_bank = min(BANK // n, 2)
-            banks = [new_bank() for x in range(PACK // per_bank)]
+        def back_project(lo, n, per_bank):
+            banks = [bank_at(out_banks.pop(0)) for x in range(PACK // per_bank)]
             cols = slice(lo, lo + n)
             for b in range(R_PASSES):
                 for j in range(PACK):
@@ -349,86 +375,102 @@ def tile_list_submap_robust_gradient_kernel(
                     )
             return banks
 
-        def store(lo, n, banks, which, copy):
-            per_bank = PACK // len(banks)
-            for x in which:
-                part = staged[lo][:, x * per_bank * n : (x + 1) * per_bank * n]
-                copy(part, banks[x][:, 0 : per_bank * n])
-                nc.sync.dma_start(
-                    out_v[:, x * per_bank : (x + 1) * per_bank, lo : lo + n], part.rearrange("p (j c) -> p j c", c=n)
-                )
+        def project_chunks(i, on_vector, banks):
+            for c in range(CHUNKS - len(banks), CHUNKS):
+                project(i, c, on_vector, banks[c - CHUNKS])
 
-        def project_chunks(i, first, last, on_vector):
-            for c in range(first, last):
-                project(i, c, on_vector)
-
-        last = CHUNKS - 1
-        project_chunks(0, 0, CHUNKS, False)
-        project_chunks(1, 0, last, True)
-        project_chunks(3, 0, 1, True)
-        project(1, last, False)
-        project_chunks(2, 0, CHUNKS, False)
-        project(3, last, False)
-
-        remaining = [(4, c) for c in range(CHUNKS)] + [(5, last)]
-        for i in range(PACK):
-            residual(i, 0, NP)
-            if i == 1:
-                project_chunks(3, 1, last, True)
-            if i == PACK - 1:
-                project_chunks(5, 0, last, True)
-            square(i, 0, NP, nc.scalar)
-            if i == 0:
-                project(*remaining.pop(0), False)
-            project(*remaining.pop(0), False)
-            log_denominator(i)
+        half = NP // 2
+        project(0, 0, False, 0)
+        project(2, 0, False, 1)
+        project(0, 1, False, 2)
+        project(1, 0, True, 3)
+        project(1, 1, True, 4)
+        project(0, 2, False, 0)
+        project(1, 2, True, 5)
+        project(0, 3, False, 1)
+        residual(0, 0, NP)
+        for i, c, x in ((1, 3, 2), (2, 3, 6), (2, 1, 0), (2, 2, 3)):
+            project(i, c, False, x)
+        square(0, 0, NP, nc.scalar)
+        residual(1, 0, NP)
+        for c, x in ((3, 7), (0, 4), (1, 1), (2, 5)):
+            project(3, c, False, x)
+        log_denominator(0, 0, NP)
+        residual(2, 0, NP)
+        project_chunks(4, False, (2, 6, 0, 3))
+        square(1, 0, NP, nc.scalar)
+        square(2, 0, NP, nc.scalar)
+        residual(3, 0, NP)
+        square(3, 0, NP, nc.gpsimd)
+        project_chunks(5, True, (5, 2, 6, 0))
+        for i in (1, 2, 3):
+            log_denominator(i, 0, NP)
         weight(0, 0, NP, chain[0][:])
-
         for i in (4, 5):
-            residual(i, 0, NP)
-            project_chunks(i + 2, 0, CHUNKS, True)
+            residual(i, 0, half)
+            residual(i, half, half)
+            square(i, 0, NP, nc.gpsimd)
+            project_chunks(i + 2, True, (7, 4, 1, 3))
         residual(6, 0, NP)
-        for lo in range(0, NP, BANK):
-            residual(7, lo, BANK)
-        square(4, 0, NP, nc.gpsimd)
-        square(5, 0, NP, nc.gpsimd)
-        log_denominator(4)
+        residual(7, 0, half)
+        residual(7, half, half)
+        log_denominator(4, 0, NP)
         square(6, 0, NP, nc.scalar)
-        log_denominator(5)
-        for lo in range(0, NP, BANK):
-            square(7, lo, BANK, nc.vector)
-        log_denominator(6)
-        log_denominator(7)
+        log_denominator(5, 0, NP)
+        square(7, 0, half, nc.vector)
+        square(7, half, half, nc.vector)
+        log_denominator(6, 0, NP)
+        log_denominator(7, 0, NP)
 
         ranges = []
         lo = 0
         for n in WIDTHS:
             ranges.append((lo, n))
             lo = lo + n
-        for lo, n in [(0, BANK)] + ranges[2:-1]:
-            weigh(0, lo, n, chain[0][:, :, lo : lo + n])
 
-        spare = [wide_tile() for x in range(NP // BANK)]
+        spare = [wide_tile(x) for x in (0, 2)]
         weights = {}
         for lo, n in ranges:
             first = PACK * (lo % BANK)
             weights[lo] = spare[lo // BANK][:, first : first + PACK * n].rearrange("p (t n) -> p t n", t=PACK)
 
-        staged = {0: ringed([P, PACK * WIDTHS[0]], F32, "table_then_stage", 1)}
+        out_banks = [5, 2, 6, 0, 7, 4, 1, 3] * 2
+        stage = [wide_tile(1), wide_tile(3)]
+        filled = []
+
+        def finish(x):
+            lo, n = ranges[x]
+            staged = stage[lo // BANK][:, PACK * (lo % BANK) : PACK * (lo % BANK + n)]
+            per_bank = PACK // 2 if x == len(ranges) - 1 else BANK // n
+            for first, bank in zip(range(0, PACK, per_bank), back_project(lo, n, per_bank)):
+                filled.append((lo, n, first, per_bank, bank, staged))
+
+        def store(copy):
+            lo, n, first, per_bank, bank, staged = filled.pop(0)
+            part = staged[:, first * n : (first + per_bank) * n]
+            copy(part, bank[:, 0 : per_bank * n])
+            nc.sync.dma_start(out_v[:, first : first + per_bank, lo : lo + n], part.rearrange("p (j c) -> p j c", c=n))
+
         for lo, n in ranges[:AHEAD]:
             weight(1, lo, n, weights[lo])
-        waiting = []
-        for x, (lo, n) in enumerate(ranges):
-            if x > 0:
-                staged[lo] = held([P, PACK * n], F32, f"staged{lo}")
-            if x == len(ranges) - 1:
-                weigh(0, lo, n, chain[0][:, :, lo : lo + n])
-            weigh(1, lo, n, weights[lo])
-            for part in waiting:
-                store(*part, range(2), nc.scalar.copy)
-            if x == 1:
-                for later in ranges[AHEAD:]:
-                    weight(1, *later, weights[later[0]])
-            waiting = [(lo, n, back_project(lo, n, parked_bank if x % 2 == 0 else stream_bank))]
-        store(*waiting[0], [0], nc.vector.tensor_copy)
-        store(*waiting[0], [1], nc.scalar.copy)
+        units = [(0, 0, BANK)] + [(0, lo, n) for lo, n in ranges[2:-1]] + [(1, lo, n) for lo, n in ranges[:-1]]
+        units = units + [(b, *ranges[-1]) for b in range(R_PASSES)]
+        rounded = None
+        done = 0
+        for b, lo, n in units + [(None, None, None)]:
+            previous = rounded
+            if b is not None:
+                rounded = (b, weigh(b, lo, n, weights[lo] if b else chain[0][:, :, lo : lo + n]))
+            if previous is not None:
+                quantize(*previous[1])
+                if previous[0] == 1:
+                    finish(done)
+                    done = done + 1
+                    if done == 1:
+                        store(nc.scalar.copy)
+                        for later in ranges[AHEAD:]:
+                            weight(1, *later, weights[later[0]])
+        while len(filled) > 2:
+            store(nc.scalar.copy)
+        store(nc.vector.tensor_copy)
+        store(nc.scalar.copy)

@@ -32,6 +32,7 @@ ALIGN = 64
 WIDE_BUFS = 4
 ROUNDED_BUFS = 5
 BANKS = 8
+LATE_B = 3
 AHEAD = 3
 LAST = ROW_TILES - 1
 WIDTHS = (256, 256, 256, 128, 128)
@@ -98,11 +99,7 @@ def tile_list_submap_robust_gradient_kernel(
         page = [wide_tile(j) for j in range(PACK)]
         scan = [ringed([P, S], F32, "scan", PACK - 1) for j in range(PACK - 1)]
         scan.append(ringed([P, S], F32, "scan_then_wr", 1))
-        pairs = ringed([P, T * PACK], BF16, "pairs_then_resid", 1)
-        first_w = ringed([P, PACK * BANK], F32, "w_then_resid", 1)
-        w_raw = [
-            values.rearrange("p (j r) -> p j r", j=PACK) for values in (first_w[:], pairs[:, 2 * T :].bitcast(F32))
-        ]
+        w_raw = [ringed([P, PACK, BANK], F32, tag, 1)[:] for tag in ("w_then_resid", "w_pairs_resid")]
 
         def scan_parts(j):
             return [(0, S // 4), (S // 4, S)] if j == 0 else [(0, S)]
@@ -135,13 +132,13 @@ def tile_list_submap_robust_gradient_kernel(
                 prec[b * BANK : (b + 1) * BANK].rearrange("(s t u) -> t s u", t=PACK, u=RUN),
             )
         load_w(0)
-        load_plane(2)
-        load_scan(2, 0)
+        load_plane(1)
+        load_scan(1, 0)
+        load_w(1)
         load_scale_rows(wc_s_raw, wc_scales[0])
         nc.sync.dma_start(wc_w_raw[:], wc_words[0].bitcast(I32))
-        load_w(1)
         nc.sync.dma_start(tab_w[:], tab_words[0].rearrange("p t i -> p (t i)").bitcast(I32))
-        for j in (1, 3):
+        for j in (2, 3):
             load_plane(j)
             load_scan(j, 0)
         nc.sync.dma_start(list_pair[:], offs3)
@@ -155,10 +152,7 @@ def tile_list_submap_robust_gradient_kernel(
             slots = pairs[:].rearrange("p (h n e) -> p h n e", h=2, e=2)[:, j // 2, first * BANK : last * BANK, j % 2]
             copy(slots, page[j][:, first * BANK : last * BANK])
 
-        def round_on_gpsimd(rounded, values):
-            nc.gpsimd.tensor_scalar(rounded, values, 1.0, 0.0, ALU.mult, ALU.add)
-
-        wk_all = ringed([P, H * PACK], BF16, "w_then_wc", 1)
+        wk_all = held([P, H * PACK], BF16, "wk_bf")
         wk_bf = [wk_all[:, b * BANK * PACK : (b + 1) * BANK * PACK] for b in range(R_PASSES)]
         wk_c = held([P, H], U32, "wk_c")
         wk_s = held([P, H], U8, "wk_s")
@@ -184,7 +178,7 @@ def tile_list_submap_robust_gradient_kernel(
 
         v_c = held([P, NP], U32, "v_c")
         v_s = held([P, NP], U8, "v_s")
-        wc_w = ringed([P, H // 2], I32, "w_then_wc", 1)
+        wc_w = held([P, H // 2], I32, "wc_w")
         wc_s = held([P, H], U8, "wc_s")
         wc_codes = wc_w[:].bitcast(U8)
         chain = [held([P, PACK, NP], F32, f"chain{b}") for b in range(R_PASSES)]
@@ -221,10 +215,6 @@ def tile_list_submap_robust_gradient_kernel(
                 )
                 copy(b_rows(i, lo, BANK), bank[:])
 
-        def gather_words(lo):
-            entries = list_tab[:, lo // PER_COL : (lo + BANK) // PER_COL]
-            nc.vector.tensor_copy(v_c[:, lo : lo + BANK], tab_w[:].bitcast(U32).indirect(entries))
-
         prec_col = held([P, ROW_TILES], F32, "prec_col")
         prec_log = held([P, ROW_TILES], F32, "prec_log")
         prec_bank = bank_at(3)
@@ -236,13 +226,13 @@ def tile_list_submap_robust_gradient_kernel(
         round_w(0)
         wr_bf = [rounded_tile(BANK)]
         turn_w(0, wr_bf[0], nc.scalar.copy, (6, 7))
-        scatter(2)
+        quantize(wk_c[:, 0:BANK], wk_s[:, 0:BANK], wk_bf[0])
+        scatter(1)
         round_w(1)
         wr_bf.append(rounded_tile(BANK))
         turn_w(1, wr_bf[1], nc.scalar.copy, (4, 5))
-        quantize(wk_c[:], wk_s[:], wk_all[:])
-        gather_words(0)
-        gather_words(BANK)
+        quantize(wk_c[:, BANK:], wk_s[:, BANK:], wk_bf[1])
+        nc.vector.tensor_copy(v_c[:], tab_w[:].bitcast(U32).indirect(list_tab[:]))
         nc.gpsimd.tensor_copy(
             wc_w[:].rearrange("p (b t s x) -> p b t s x", b=R_PASSES, t=PACK, x=RUN // 2),
             wc_w_raw[:].rearrange("p (b s t x) -> p b t s x", b=R_PASSES, t=PACK, x=RUN // 2),
@@ -251,11 +241,13 @@ def tile_list_submap_robust_gradient_kernel(
             wc_s[:].bitcast(I32).rearrange("p (b t s x) -> p b t s x", b=R_PASSES, t=PACK, x=RUN // 4),
             wc_s_raw[:].bitcast(I32).rearrange("p (b s t x) -> p b t s x", b=R_PASSES, t=PACK, x=RUN // 4),
         )
-        round_plane(0, 0, CHUNKS, round_on_gpsimd)
+        pairs = ringed([P, T * PACK], BF16, "w_pairs_resid", 1)
+        round_plane(0, 0, CHUNKS, nc.scalar.copy)
+        round_plane(1, 0, CHUNKS, nc.scalar.copy)
+        scatter(2)
+        banks_of_b = [(i, lo) for i in range(ROW_TILES) for lo in range(0, NP, BANK)]
+        map_side(banks_of_b[:-LATE_B], nc.scalar.copy)
         round_plane(2, 0, CHUNKS, nc.scalar.copy)
-        scatter(1)
-        round_plane(1, 0, CHUNKS, round_on_gpsimd)
-        map_side([(i, lo) for lo in range(0, NP, BANK) for i in range(ROW_TILES)], nc.scalar.copy)
         scatter(3)
         wr_c = ringed([P, R_PASSES * BANK], U32, "scan_then_wr", 1)
         wr_s = held([P, R_PASSES * BANK], U8, "wr_s")
@@ -264,6 +256,7 @@ def tile_list_submap_robust_gradient_kernel(
             quantize(wr_c[:, cols], wr_s[:, cols], wr_bf[b][:])
         for c in range(CHUNKS):
             round_plane(3, c, c + 1, nc.scalar.copy)
+        map_side(banks_of_b[-LATE_B:], nc.scalar.copy)
 
         page_c = [held([P, BANK], U32, f"page_c{c}") for c in range(CHUNKS)]
         page_s = [held([P, BANK], U8, f"page_s{c}") for c in range(CHUNKS)]
@@ -284,7 +277,7 @@ def tile_list_submap_robust_gradient_kernel(
             quantize(page_c[c][:], page_s[c][:], woven[c][:])
 
         a_sb = {}
-        resid = [ringed([P, PACK, NP], F32, "w_then_resid", 1), ringed([P, PACK, NP], F32, "pairs_then_resid", 1)]
+        resid = [ringed([P, PACK, NP], F32, "w_then_resid", 1), ringed([P, PACK, NP], F32, "w_pairs_resid", 1)]
         g_c = [held([P, NP], U32, f"g_c{b}") for b in range(R_PASSES)]
         g_s = [held([P, NP], U8, f"g_s{b}") for b in range(R_PASSES)]
 
@@ -298,7 +291,7 @@ def tile_list_submap_robust_gradient_kernel(
                 elif i - 2 in early_b:
                     a_sb[i] = ringed([P, T], F32, f"b{i - 2}_then_a", 1)
                 else:
-                    a_sb[i] = wide_tile({0: 0, 2: 2, 3: 1, 4: 3}[i])
+                    a_sb[i] = wide_tile({0: 0, 2: 1, 3: 2, 4: 3}[i])
             bank = bank_at(x)
             nc.tensor.matmul_mx(
                 out=bank[:],
@@ -349,13 +342,17 @@ def tile_list_submap_robust_gradient_kernel(
 
         def weigh(b, lo, n, weights):
             g_bf = rounded_tile(n)
-            nc.vector.tensor_tensor(
-                g_bf[:].rearrange("p (c i t) -> p c t i", i=LINE, t=PACK),
-                resid[b][:, :, lo : lo + n].rearrange("p t (c i) -> p c t i", i=LINE),
-                weights.rearrange("p t (c i) -> p c t i", i=LINE),
-                ALU.mult,
-            )
-            return g_c[b][:, lo : lo + n], g_s[b][:, lo : lo + n], g_bf[:]
+            halves = [(0, n // 2), (n // 2, n)]
+            for first, last in halves:
+                nc.vector.tensor_tensor(
+                    g_bf[:, first * PACK : last * PACK].rearrange("p (c i t) -> p c t i", i=LINE, t=PACK),
+                    resid[b][:, :, lo + first : lo + last].rearrange("p t (c i) -> p c t i", i=LINE),
+                    weights[:, :, first:last].rearrange("p t (c i) -> p c t i", i=LINE),
+                    ALU.mult,
+                )
+            for first, last in halves:
+                cols = slice(lo + first, lo + last)
+                quantize(g_c[b][:, cols], g_s[b][:, cols], g_bf[:, first * PACK : last * PACK])
 
         def back_project(lo, n, per_bank):
             banks = [bank_at(out_banks.pop(0)) for x in range(PACK // per_bank)]
@@ -386,23 +383,22 @@ def tile_list_submap_robust_gradient_kernel(
         project(1, 0, True, 3)
         project(1, 1, True, 4)
         project(0, 2, False, 0)
-        project(1, 2, True, 5)
         project(0, 3, False, 1)
         residual(0, 0, NP)
-        for i, c, x in ((1, 3, 2), (2, 3, 6), (2, 1, 0), (2, 2, 3)):
+        for i, c, x in ((1, 3, 2), (2, 3, 5), (1, 2, 0), (2, 1, 3), (2, 2, 4)):
             project(i, c, False, x)
         square(0, 0, NP, nc.scalar)
         residual(1, 0, NP)
-        for c, x in ((3, 7), (0, 4), (1, 1), (2, 5)):
+        for c, x in ((3, 6), (0, 1), (1, 2), (2, 5)):
             project(3, c, False, x)
         log_denominator(0, 0, NP)
         residual(2, 0, NP)
-        project_chunks(4, False, (2, 6, 0, 3))
+        project_chunks(4, False, (0, 3, 4, 7))
         square(1, 0, NP, nc.scalar)
         square(2, 0, NP, nc.scalar)
         residual(3, 0, NP)
         square(3, 0, NP, nc.gpsimd)
-        project_chunks(5, True, (5, 2, 6, 0))
+        project_chunks(5, True, (5, 0, 3, 4))
         for i in (1, 2, 3):
             log_denominator(i, 0, NP)
         weight(0, 0, NP, chain[0][:])
@@ -410,7 +406,7 @@ def tile_list_submap_robust_gradient_kernel(
             residual(i, 0, half)
             residual(i, half, half)
             square(i, 0, NP, nc.gpsimd)
-            project_chunks(i + 2, True, (7, 4, 1, 3))
+            project_chunks(i + 2, True, (6, 1, 2, 7))
         residual(6, 0, NP)
         residual(7, 0, half)
         residual(7, half, half)
@@ -428,20 +424,20 @@ def tile_list_submap_robust_gradient_kernel(
             ranges.append((lo, n))
             lo = lo + n
 
-        spare = [wide_tile(x) for x in (0, 2)]
+        spare = [wide_tile(x) for x in (0, 1)]
         weights = {}
         for lo, n in ranges:
             first = PACK * (lo % BANK)
             weights[lo] = spare[lo // BANK][:, first : first + PACK * n].rearrange("p (t n) -> p t n", t=PACK)
 
-        out_banks = [5, 2, 6, 0, 7, 4, 1, 3] * 2
-        stage = [wide_tile(1), wide_tile(3)]
+        out_banks = [5, 0, 3, 4, 6, 1, 2, 7] * 2
+        stage = [wide_tile(2), wide_tile(3)]
         filled = []
 
         def finish(x):
             lo, n = ranges[x]
             staged = stage[lo // BANK][:, PACK * (lo % BANK) : PACK * (lo % BANK + n)]
-            per_bank = PACK // 2 if x == len(ranges) - 1 else BANK // n
+            per_bank = PACK // 2
             for first, bank in zip(range(0, PACK, per_bank), back_project(lo, n, per_bank)):
                 filled.append((lo, n, first, per_bank, bank, staged))
 
@@ -451,26 +447,19 @@ def tile_list_submap_robust_gradient_kernel(
             copy(part, bank[:, 0 : per_bank * n])
             nc.sync.dma_start(out_v[:, first : first + per_bank, lo : lo + n], part.rearrange("p (j c) -> p j c", c=n))
 
+        for lo, n in [(0, BANK)] + ranges[2:-1]:
+            weigh(0, lo, n, chain[0][:, :, lo : lo + n])
         for lo, n in ranges[:AHEAD]:
             weight(1, lo, n, weights[lo])
-        units = [(0, 0, BANK)] + [(0, lo, n) for lo, n in ranges[2:-1]] + [(1, lo, n) for lo, n in ranges[:-1]]
-        units = units + [(b, *ranges[-1]) for b in range(R_PASSES)]
-        rounded = None
-        done = 0
-        for b, lo, n in units + [(None, None, None)]:
-            previous = rounded
-            if b is not None:
-                rounded = (b, weigh(b, lo, n, weights[lo] if b else chain[0][:, :, lo : lo + n]))
-            if previous is not None:
-                quantize(*previous[1])
-                if previous[0] == 1:
-                    finish(done)
-                    done = done + 1
-                    if done == 1:
-                        store(nc.scalar.copy)
-                        for later in ranges[AHEAD:]:
-                            weight(1, *later, weights[later[0]])
-        while len(filled) > 2:
-            store(nc.scalar.copy)
+        for x, (lo, n) in enumerate(ranges):
+            if x == len(ranges) - 1:
+                weigh(0, lo, n, chain[0][:, :, lo : lo + n])
+            weigh(1, lo, n, weights[lo])
+            while filled:
+                store(nc.scalar.copy)
+            if x == 1:
+                for later in ranges[AHEAD:]:
+                    weight(1, *later, weights[later[0]])
+            finish(x)
         store(nc.vector.tensor_copy)
         store(nc.scalar.copy)

@@ -34,6 +34,7 @@ ROUNDED_BUFS = 5
 BANKS = 8
 LATE_B = 3
 AHEAD = 3
+OWN = 128
 LAST = ROW_TILES - 1
 WIDTHS = (256, 256, 256, 128, 128)
 
@@ -154,14 +155,19 @@ def tile_list_submap_robust_gradient_kernel(
 
         wk_all = held([P, H * PACK], BF16, "wk_bf")
         wk_bf = [wk_all[:, b * BANK * PACK : (b + 1) * BANK * PACK] for b in range(R_PASSES)]
-        wk_c = held([P, H], U32, "wk_c")
+        wk_c = held([P, LAST * P], U32, "wk_c")
         wk_s = held([P, H], U8, "wk_s")
+        late_c = []
+
+        def wk_codes(i):
+            return late_c[0][:, H:] if i == LAST else wk_c[:, i * P : (i + 1) * P]
 
         def round_w(b):
             rounded = wk_bf[b].rearrange("p (t s u j) -> p s t j u", t=PACK, u=RUN, j=PACK)
             values = w_raw[b].rearrange("p j (s t u) -> p s t j u", t=PACK, u=RUN)
-            for first in range(0, 2 * RUN, RUN):
-                nc.scalar.copy(rounded[:, first : first + RUN], values[:, first : first + RUN])
+            nc.scalar.copy(rounded[:, 0:RUN], values[:, 0:RUN])
+            for tiles in (slice(0, 2), slice(2, PACK)) if b == 0 else (slice(0, PACK),):
+                nc.scalar.copy(rounded[:, RUN:, tiles], values[:, RUN:, tiles])
 
         def turn_w(b, turned, copy, banks):
             words = wk_bf[b].bitcast(F32)
@@ -197,7 +203,7 @@ def tile_list_submap_robust_gradient_kernel(
                 bank = new_bank()
                 nc.tensor.matmul_mx(
                     out=bank[:],
-                    lhsT=wk_c[:, i * P : (i + 1) * P].bitcast(FP8X4),
+                    lhsT=wk_codes(i).bitcast(FP8X4),
                     lhsT_scale=wk_s[:, i * P : (i + 1) * P],
                     rhs=v_c[:, cols].bitcast(FP8X4),
                     rhs_scale=v_s[:, cols],
@@ -231,7 +237,7 @@ def tile_list_submap_robust_gradient_kernel(
         round_w(1)
         wr_bf.append(rounded_tile(BANK))
         turn_w(1, wr_bf[1], nc.scalar.copy, (4, 5))
-        quantize(wk_c[:, BANK:], wk_s[:, BANK:], wk_bf[1])
+        quantize(wk_c[:, BANK:], wk_s[:, BANK : LAST * P], wk_all[:, BANK * PACK : LAST * P * PACK])
         nc.vector.tensor_copy(v_c[:], tab_w[:].bitcast(U32).indirect(list_tab[:]))
         nc.gpsimd.tensor_copy(
             wc_w[:].rearrange("p (b t s x) -> p b t s x", b=R_PASSES, t=PACK, x=RUN // 2),
@@ -249,7 +255,9 @@ def tile_list_submap_robust_gradient_kernel(
         map_side(banks_of_b[:-LATE_B], nc.scalar.copy)
         round_plane(2, 0, CHUNKS, nc.scalar.copy)
         scatter(3)
-        wr_c = ringed([P, R_PASSES * BANK], U32, "scan_then_wr", 1)
+        late_c.append(ringed([P, H + P], U32, "scan_then_wr", 1))
+        wr_c = late_c[0][:, 0:H]
+        quantize(wk_codes(LAST), wk_s[:, LAST * P :], wk_all[:, LAST * P * PACK :])
         wr_s = held([P, R_PASSES * BANK], U8, "wr_s")
         for b in range(R_PASSES):
             cols = slice(b * BANK, (b + 1) * BANK)
@@ -263,7 +271,7 @@ def tile_list_submap_robust_gradient_kernel(
         woven = []
 
         def weave(c, copy):
-            last = c == CHUNKS - 1
+            last = c == CHUNKS - 2
             woven.append(ringed([P, BANK * PACK], BF16, "woven_then_a", 1) if last else rounded_tile(BANK))
             copy(
                 woven[c][:].bitcast(F32).rearrange("p (n h) -> p n h", h=2),
@@ -295,7 +303,7 @@ def tile_list_submap_robust_gradient_kernel(
             bank = bank_at(x)
             nc.tensor.matmul_mx(
                 out=bank[:],
-                lhsT=wk_c[:, i * P : (i + 1) * P].bitcast(FP8X4),
+                lhsT=wk_codes(i).bitcast(FP8X4),
                 lhsT_scale=wk_s[:, i * P : (i + 1) * P],
                 rhs=page_c[c][:].bitcast(FP8X4),
                 rhs_scale=page_s[c][:],
@@ -340,19 +348,26 @@ def tile_list_submap_robust_gradient_kernel(
                     dst[:, t, :], chain[b][:, t, lo : lo + n], ACT.Exp, bias=prec_log[:, i : i + 1], scale=-2.0
                 )
 
-        def weigh(b, lo, n, weights):
+        def product(b, lo, n, weights):
             g_bf = rounded_tile(n)
-            halves = [(0, n // 2), (n // 2, n)]
-            for first, last in halves:
-                nc.vector.tensor_tensor(
-                    g_bf[:, first * PACK : last * PACK].rearrange("p (c i t) -> p c t i", i=LINE, t=PACK),
-                    resid[b][:, :, lo + first : lo + last].rearrange("p t (c i) -> p c t i", i=LINE),
-                    weights[:, :, first:last].rearrange("p t (c i) -> p c t i", i=LINE),
-                    ALU.mult,
-                )
-            for first, last in halves:
-                cols = slice(lo + first, lo + last)
-                quantize(g_c[b][:, cols], g_s[b][:, cols], g_bf[:, first * PACK : last * PACK])
+            nc.vector.tensor_tensor(
+                g_bf[:].rearrange("p (c i t) -> p c t i", i=LINE, t=PACK),
+                resid[b][:, :, lo : lo + n].rearrange("p t (c i) -> p c t i", i=LINE),
+                weights.rearrange("p t (c i) -> p c t i", i=LINE),
+                ALU.mult,
+            )
+            return g_c[b][:, lo : lo + n], g_s[b][:, lo : lo + n], g_bf[:]
+
+        def weigh(parts):
+            for operands in [product(*part) for part in parts]:
+                quantize(*operands)
+
+        def first_part(lo, n):
+            return 0, lo, n, chain[0][:, :, lo : lo + n]
+
+        def second_parts(lo, n, pieces):
+            width = n // pieces
+            return [(1, lo + x, width, weights[lo][:, :, x : x + width]) for x in range(0, n, width)]
 
         def back_project(lo, n, per_bank):
             banks = [bank_at(out_banks.pop(0)) for x in range(PACK // per_bank)]
@@ -377,6 +392,15 @@ def tile_list_submap_robust_gradient_kernel(
                 project(i, c, on_vector, banks[c - CHUNKS])
 
         half = NP // 2
+
+        def window(i, banks):
+            residual(i, 0, half)
+            residual(i, half, half)
+            square(i, 0, OWN, nc.vector)
+            square(i, OWN, NP - OWN, nc.gpsimd)
+            project_chunks(i + 2, True, banks)
+
+
         project(0, 0, False, 0)
         project(2, 0, False, 1)
         project(0, 1, False, 2)
@@ -396,17 +420,12 @@ def tile_list_submap_robust_gradient_kernel(
         project_chunks(4, False, (0, 3, 4, 7))
         square(1, 0, NP, nc.scalar)
         square(2, 0, NP, nc.scalar)
-        residual(3, 0, NP)
-        square(3, 0, NP, nc.gpsimd)
-        project_chunks(5, True, (5, 0, 3, 4))
+        window(3, (5, 0, 3, 4))
         for i in (1, 2, 3):
             log_denominator(i, 0, NP)
         weight(0, 0, NP, chain[0][:])
         for i in (4, 5):
-            residual(i, 0, half)
-            residual(i, half, half)
-            square(i, 0, NP, nc.gpsimd)
-            project_chunks(i + 2, True, (6, 1, 2, 7))
+            window(i, (6, 1, 2, 7))
         residual(6, 0, NP)
         residual(7, 0, half)
         residual(7, half, half)
@@ -447,14 +466,18 @@ def tile_list_submap_robust_gradient_kernel(
             copy(part, bank[:, 0 : per_bank * n])
             nc.sync.dma_start(out_v[:, first : first + per_bank, lo : lo + n], part.rearrange("p (j c) -> p j c", c=n))
 
-        for lo, n in [(0, BANK)] + ranges[2:-1]:
-            weigh(0, lo, n, chain[0][:, :, lo : lo + n])
+        behind = []
+        for lo, n in ranges[:-1]:
+            behind.append(product(*first_part(lo, n)))
+            if len(behind) == 2:
+                quantize(*behind.pop(0))
+        quantize(*behind.pop(0))
         for lo, n in ranges[:AHEAD]:
             weight(1, lo, n, weights[lo])
         for x, (lo, n) in enumerate(ranges):
             if x == len(ranges) - 1:
-                weigh(0, lo, n, chain[0][:, :, lo : lo + n])
-            weigh(1, lo, n, weights[lo])
+                weigh([first_part(lo, n // 2), first_part(lo + n // 2, n // 2)])
+            weigh(second_parts(lo, n, 2))
             while filled:
                 store(nc.scalar.copy)
             if x == 1:

@@ -24,6 +24,7 @@ QUADRANT = 32
 BANK = 512
 R_PASSES = H // (P * PACK)
 ROW_TILES = R_PASSES * PACK
+SCALE_ROWS = P // RUN
 CHUNKS = T // BANK
 PER_COL = 16
 LINE = 4
@@ -72,9 +73,9 @@ def tile_list_submap_robust_gradient_kernel(
         def quantize(codes, scales, rounded):
             nc.vector.quantize_mx(out=codes.bitcast(FP8X4), scales=scales, in_=rounded)
 
-        def load_scale_rows(tile, rows):
+        def load_scale_rows(tile, rows, queue):
             for q in range(P // QUADRANT):
-                nc.sync.dma_start(
+                queue.dma_start(
                     tile[QUADRANT * q : QUADRANT * q + PACK, :].bitcast(I32),
                     rows[PACK * q : PACK * (q + 1), :].bitcast(I32),
                 )
@@ -122,7 +123,7 @@ def tile_list_submap_robust_gradient_kernel(
         wc_w_raw = held([P, H // 2], I32, "wc_w_raw")
 
         nc.sync.dma_start(list_tab[:], offs)
-        load_scale_rows(tab_s, tab_scales[0])
+        nc.sync.dma_start(tab_s[0:SCALE_ROWS, :].bitcast(I32), tab_scales[0].bitcast(I32))
         nc.sync.dma_start(list_page[:], offs2)
         load_plane(0)
         load_scan(0, 0)
@@ -136,7 +137,7 @@ def tile_list_submap_robust_gradient_kernel(
         load_plane(1)
         load_scan(1, 0)
         load_w(1)
-        load_scale_rows(wc_s_raw, wc_scales[0])
+        load_scale_rows(wc_s_raw, wc_scales[0], nc.sync)
         nc.sync.dma_start(wc_w_raw[:], wc_words[0].bitcast(I32))
         nc.sync.dma_start(tab_w[:], tab_words[0].rearrange("p t i -> p (t i)").bitcast(I32))
         for j in (2, 3):
@@ -227,7 +228,10 @@ def tile_list_submap_robust_gradient_kernel(
         nc.tensor.transpose(prec_bank[:, 0:P], prec_rows[:], ident[:])
         nc.scalar.activation(prec_log[:], prec_bank[:, 0:ROW_TILES], ACT.Ln)
         nc.scalar.copy(prec_col[:], prec_bank[:, 0:ROW_TILES])
-        nc.vector.tensor_copy(v_s[:], tab_s[:].indirect(list_tab[:]))
+        v_rows = held([P, NP], U8, "v_rows")
+        nc.gpsimd.memset(v_s[:].bitcast(I32), 0)
+        nc.vector.tensor_copy(v_rows[:], tab_s[:].indirect(list_tab[:]))
+        load_scale_rows(v_s, v_rows, nc.gpsimd)
         scatter(0)
         round_w(0)
         wr_bf = [rounded_tile(BANK)]

@@ -324,8 +324,10 @@ def tile_list_submap_robust_gradient_kernel(
                 resid[b][:, t, lo : lo + n], a_sb[i][:].indirect(entries), b_rows(i, lo, n), ALU.subtract
             )
 
+        apart = ringed([P, NP], F32, "squares_then_roots", 1)
+
         def square_rows(i):
-            return chain[i // PACK][:, i % PACK, :]
+            return apart[:] if i == PACK - 1 else chain[i // PACK][:, i % PACK, :]
 
         def square(i, lo, n, engine):
             b, t = divmod(i, PACK)
@@ -337,19 +339,18 @@ def tile_list_submap_robust_gradient_kernel(
 
         def log_denominator(i, lo, n):
             b, t = divmod(i, PACK)
+            bias, scale = (1.0, prec_col[:, i : i + 1]) if b == 0 else (roots[1][:, t : t + 1], roots[0][:, t : t + 1])
             nc.scalar.activation(
-                chain[b][:, t, lo : lo + n],
-                square_rows(i)[:, lo : lo + n],
-                ACT.Ln,
-                bias=1.0,
-                scale=prec_col[:, i : i + 1],
+                chain[b][:, t, lo : lo + n], square_rows(i)[:, lo : lo + n], ACT.Ln, bias=bias, scale=scale
             )
 
-        def weight(b, lo, n, dst):
-            for t in range(PACK):
-                i = b * PACK + t
+        def weight(b, lo, n, dst, tiles=range(PACK)):
+            if b == 1:
+                nc.scalar.activation(dst, chain[b][:, :, lo : lo + n], ACT.Exp, scale=-2.0)
+                return
+            for t in tiles:
                 nc.scalar.activation(
-                    dst[:, t, :], chain[b][:, t, lo : lo + n], ACT.Exp, bias=prec_log[:, i : i + 1], scale=-2.0
+                    dst[:, t, :], chain[b][:, t, lo : lo + n], ACT.Exp, bias=prec_log[:, t : t + 1], scale=-2.0
                 )
 
         def product(b, lo, n, weights):
@@ -369,9 +370,9 @@ def tile_list_submap_robust_gradient_kernel(
         def first_part(lo, n):
             return 0, lo, n, chain[0][:, :, lo : lo + n]
 
-        def second_parts(lo, n, pieces):
-            width = n // pieces
-            return [(1, lo + x, width, weights[lo][:, :, x : x + width]) for x in range(0, n, width)]
+        def second_parts(lo, n):
+            width = n // 2
+            return [(1, x, width, weights[x]) for x in (lo, lo + width)]
 
         def back_project(lo, n, per_bank):
             banks = [bank_at(out_banks.pop(0)) for x in range(PACK // per_bank)]
@@ -427,9 +428,14 @@ def tile_list_submap_robust_gradient_kernel(
         window(3, (5, 0, 3, 4))
         for i in (1, 2, 3):
             log_denominator(i, 0, NP)
-        weight(0, 0, NP, chain[0][:])
         for i in (4, 5):
             window(i, (6, 1, 2, 7))
+        weight(0, 0, NP, chain[0][:], (0,))
+        both = ringed([P, 2, PACK], F32, "squares_then_roots", 1)
+        roots = [both[:, 0, :], both[:, 1, :]]
+        for root, power in zip(roots, (0.5, -0.5)):
+            nc.scalar.activation(root, prec_log[:, PACK:], ACT.Exp, scale=power)
+        weight(0, 0, NP, chain[0][:], (1, 2, 3))
         residual(6, 0, NP)
         residual(7, 0, half)
         residual(7, half, half)
@@ -451,7 +457,13 @@ def tile_list_submap_robust_gradient_kernel(
         weights = {}
         for lo, n in ranges:
             first = PACK * (lo % BANK)
-            weights[lo] = spare[lo // BANK][:, first : first + PACK * n].rearrange("p (t n) -> p t n", t=PACK)
+            block = spare[lo // BANK][:, first : first + PACK * n]
+            if lo == 0:
+                halves = block.rearrange("p (h t n) -> p h t n", h=2, t=PACK)
+                weights[lo], weights[lo + n // 2] = halves[:, 0], halves[:, 1]
+            else:
+                whole = block.rearrange("p (t n) -> p t n", t=PACK)
+                weights[lo, n], weights[lo], weights[lo + n // 2] = whole, whole[:, :, : n // 2], whole[:, :, n // 2 :]
 
         out_banks = [5, 0, 3, 4, 6, 1, 2, 7] * 2
         stage = [wide_tile(2), wide_tile(3)]
@@ -476,17 +488,18 @@ def tile_list_submap_robust_gradient_kernel(
             if len(behind) == 2:
                 quantize(*behind.pop(0))
         quantize(*behind.pop(0))
-        for lo, n in ranges[:AHEAD]:
-            weight(1, lo, n, weights[lo])
+        for lo in (0, WIDTHS[0] // 2):
+            weight(1, lo, WIDTHS[0] // 2, weights[lo])
+        for lo, n in ranges[1:AHEAD]:
+            weight(1, lo, n, weights[lo, n])
         for x, (lo, n) in enumerate(ranges):
             if x == len(ranges) - 1:
                 weigh([first_part(lo, n // 2), first_part(lo + n // 2, n // 2)])
-            weigh(second_parts(lo, n, 2))
+            weigh(second_parts(lo, n))
             while filled:
                 store(nc.scalar.copy)
-            if x == 1:
-                for later in ranges[AHEAD:]:
-                    weight(1, *later, weights[later[0]])
+            if x in (1, 2):
+                weight(1, *ranges[x + 2], weights[ranges[x + 2]])
             finish(x)
-        store(nc.vector.tensor_copy)
         store(nc.scalar.copy)
+        store(nc.vector.tensor_copy)

@@ -34,7 +34,7 @@ WIDE_BUFS = 4
 ROUNDED_BUFS = 5
 BANKS = 8
 LATE_B = 3
-AHEAD = 3
+AHEAD = 4
 OWN = 128
 LAST = ROW_TILES - 1
 WIDTHS = (256, 256, 256, 128, 128)
@@ -222,12 +222,12 @@ def tile_list_submap_robust_gradient_kernel(
                 )
                 copy(b_rows(i, lo, BANK), bank[:])
 
-        prec_col = held([P, ROW_TILES], F32, "prec_col")
+        prec_col = held([P, PACK], F32, "prec_col")
         prec_log = held([P, ROW_TILES], F32, "prec_log")
         prec_bank = bank_at(3)
         nc.tensor.transpose(prec_bank[:, 0:P], prec_rows[:], ident[:])
         nc.scalar.activation(prec_log[:], prec_bank[:, 0:ROW_TILES], ACT.Ln)
-        nc.scalar.copy(prec_col[:], prec_bank[:, 0:ROW_TILES])
+        nc.scalar.copy(prec_col[:], prec_bank[:, 0:PACK])
         v_rows = held([P, NP], U8, "v_rows")
         nc.gpsimd.memset(v_s[:].bitcast(I32), 0)
         nc.vector.tensor_copy(v_rows[:], tab_s[:].indirect(list_tab[:]))
@@ -493,13 +493,11 @@ def tile_list_submap_robust_gradient_kernel(
         for lo, n in ranges[1:AHEAD]:
             weight(1, lo, n, weights[lo, n])
         for x, (lo, n) in enumerate(ranges):
-            if x == len(ranges) - 1:
-                weigh([first_part(lo, n // 2), first_part(lo + n // 2, n // 2)])
-            weigh(second_parts(lo, n))
+            weigh(([first_part(lo, n)] if x == len(ranges) - 1 else []) + second_parts(lo, n))
             while filled:
                 store(nc.scalar.copy)
-            if x in (1, 2):
-                weight(1, *ranges[x + 2], weights[ranges[x + 2]])
+            if x == 1:
+                weight(1, *ranges[AHEAD], weights[ranges[AHEAD]])
             finish(x)
         store(nc.scalar.copy)
         store(nc.vector.tensor_copy)

from contextlib import ExitStack

import concourse.mybir as mybir
from concourse.masks import make_identity

K, H, T, S, NP = 512, 1024, 2048, 1024, 1024
FLOPS = 2 * K * H * T + 2 * 2 * K * H * NP + 2 * H * K * NP

F32 = mybir.dt.float32
BF16 = mybir.dt.bfloat16
I32 = mybir.dt.int32
U32 = mybir.dt.uint32
U16 = mybir.dt.uint16
U8 = mybir.dt.uint8
FP8X4 = mybir.dt.float8_e4m3fn_x4
FP4X4 = mybir.dt.float4_e2m1fn_x4
ACT = mybir.ActivationFunctionType
ALU = mybir.AluOpType

P = 128
PACK = 4
RUN = 8
QUADRANT = 32
BANK = 512
R_PASSES = H // (P * PACK)
ROW_TILES = R_PASSES * PACK
SCALE_ROWS = P // RUN
CHUNKS = T // BANK
PER_COL = 16
LINE = 4
ALIGN = 64

WIDE_BUFS = 4
ROUNDED_BUFS = 5
BANKS = 8
LATE_B = 3
AHEAD = 4
OWN = 128
LAST = ROW_TILES - 1
WIDTHS = (256, 256, 256, 128, 128)


def tile_list_submap_robust_gradient_kernel(
    tc, tab_words, tab_scales, offs, offs2, offs3, xs, base, w, wc_words, wc_scales, prec, out
):
    nc = tc.nc
    with ExitStack() as ctx:
        keep = ctx.enter_context(tc.tile_pool(name="keep", bufs=1))
        ring = ctx.enter_context(tc.tile_pool(name="ring", bufs=1))
        psum = ctx.enter_context(tc.psum_pool(name="psum", bufs=1))

        def held(shape, dtype, name):
            return keep.tile(shape, dtype, name=name, align_bytes=ALIGN)

        def ringed(shape, dtype, tag, bufs):
            return ring.tile(shape, dtype, name=tag, tag=tag, bufs=bufs, align_bytes=ALIGN)

        def wide_tile(x):
            return ringed([P, T], F32, f"wide{x}", 1)

        def rounded_tile(columns):
            return ringed([P, columns * PACK], BF16, "rounded", ROUNDED_BUFS)

        turn = [BANKS - 1]

        def bank_at(x):
            return psum.tile([P, BANK], F32, name=f"bank{x}", tag=f"bank{x}", bufs=1)

        def new_bank():
            turn.append((turn[-1] + 1) % BANKS)
            return bank_at(turn[-1])

        def quantize(codes, scales, rounded):
            nc.vector.quantize_mx(out=codes.bitcast(FP8X4), scales=scales, in_=rounded)

        def load_scale_rows(tile, rows, queue):
            for q in range(P // QUADRANT):
                queue.dma_start(
                    tile[QUADRANT * q : QUADRANT * q + PACK, :].bitcast(I32),
                    rows[PACK * q : PACK * (q + 1), :].bitcast(I32),
                )

        list_tab = held([P, NP // PER_COL], U16, "list_tab")
        list_page = held([P, S // PER_COL], U16, "list_page")
        list_pair = held([P, NP // PER_COL], U16, "list_pair")

        tab_s = held([P, T], U8, "tab_s")
        wc_s_raw = held([P, H], U8, "wc_s_raw")
        prec_rows = held([P, P], F32, "prec_rows")
        ident = held([P, P], F32, "ident")
        nc.gpsimd.memset(tab_s[:].bitcast(I32), 0)
        nc.gpsimd.memset(wc_s_raw[:].bitcast(I32), 0)
        nc.gpsimd.memset(prec_rows[:], 0.0)
        make_identity(nc, ident[:])

        base_v = base.rearrange("(p j) t -> p j t", j=PACK)
        xs_v = xs.rearrange("(p j) m -> p j m", j=PACK)
        w_v = w.rearrange("(p j) r -> p j r", j=PACK)
        out_v = out.rearrange("(p j) c -> p j c", j=PACK)

        page = [wide_tile(j) for j in range(PACK)]
        scan = [ringed([P, S], F32, "scan", PACK - 1) for j in range(PACK - 1)]
        scan.append(ringed([P, S], F32, "scan_then_wr", 1))
        w_raw = [ringed([P, PACK, BANK], F32, tag, 1)[:] for tag in ("w_then_resid", "w_pairs_resid")]

        def scan_parts(j):
            return [(0, S // 4), (S // 4, S)] if j == 0 else [(0, S)]

        def load_plane(j):
            nc.sync.dma_start(page[j][:], base_v[:, j, :])

        def load_scan(j, part):
            lo, hi = scan_parts(j)[part]
            nc.sync.dma_start(scan[j][:, lo:hi], xs_v[:, j, lo:hi])

        def load_w(b):
            for lo in range(0, BANK, BANK // 2):
                nc.sync.dma_start(
                    w_raw[b][:, :, lo : lo + BANK // 2], w_v[:, :, b * BANK + lo : b * BANK + lo + BANK // 2]
                )

        tab_w = ringed([P, T], I32, "table_then_a", 1)
        wc_w_raw = held([P, H // 2], I32, "wc_w_raw")

        nc.sync.dma_start(list_tab[:], offs)
        nc.sync.dma_start(tab_s[0:SCALE_ROWS, :].bitcast(I32), tab_scales[0].bitcast(I32))
        nc.sync.dma_start(list_page[:], offs2)
        load_plane(0)
        load_scan(0, 0)
        load_scan(0, 1)
        for b in range(R_PASSES):
            nc.sync.dma_start(
                prec_rows[PACK * b : PACK * (b + 1), :].rearrange("t (s u) -> t s u", u=RUN),
                prec[b * BANK : (b + 1) * BANK].rearrange("(s t u) -> t s u", t=PACK, u=RUN),
            )
        load_w(0)
        load_plane(1)
        load_scan(1, 0)
        load_w(1)
        load_scale_rows(wc_s_raw, wc_scales[0], nc.sync)
        nc.sync.dma_start(wc_w_raw[:], wc_words[0].bitcast(I32))
        nc.sync.dma_start(tab_w[:], tab_words[0].rearrange("p t i -> p (t i)").bitcast(I32))
        for j in (2, 3):
            load_plane(j)
            load_scan(j, 0)
        nc.sync.dma_start(list_pair[:], offs3)

        def scatter(j):
            for lo, hi in scan_parts(j):
                entries = list_page[:, lo // PER_COL : hi // PER_COL]
                nc.vector.tensor_copy(page[j][:].indirect(entries), scan[j][:, lo:hi])

        def round_plane(j, first, last, copy):
            slots = pairs[:].rearrange("p (h n e) -> p h n e", h=2, e=2)[:, j // 2, first * BANK : last * BANK, j % 2]
            copy(slots, page[j][:, first * BANK : last * BANK])

        wk_all = held([P, H * PACK], BF16, "wk_bf")
        wk_bf = [wk_all[:, b * BANK * PACK : (b + 1) * BANK * PACK] for b in range(R_PASSES)]
        wk_c = held([P, LAST * P], U32, "wk_c")
        wk_s = held([P, H], U8, "wk_s")
        late_c = []

        def wk_codes(i):
            return late_c[0][:, H:] if i == LAST else wk_c[:, i * P : (i + 1) * P]

        def round_w(b):
            rounded = wk_bf[b].rearrange("p (t s u j) -> p s t j u", t=PACK, u=RUN, j=PACK)
            values = w_raw[b].rearrange("p j (s t u) -> p s t j u", t=PACK, u=RUN)
            nc.scalar.copy(rounded[:, 0:RUN], values[:, 0:RUN])
            for tiles in (slice(0, 2), slice(2, PACK)) if b == 0 else (slice(0, PACK),):
                nc.scalar.copy(rounded[:, RUN:, tiles], values[:, RUN:, tiles])

        def turn_w(b, turned, copy, banks):
            words = wk_bf[b].bitcast(F32)
            for h in range(2):
                bank = bank_at(banks[h])
                for t in range(PACK):
                    nc.tensor.transpose(
                        bank[:, t * P : (t + 1) * P], words[:, 2 * P * t + h : 2 * P * (t + 1) : 2], ident[:]
                    )
                copy(
                    turned[:, h * 2 * BANK : (h + 1) * 2 * BANK].rearrange("m (e p t) -> m e p t", e=2, t=PACK),
                    bank[:].bitcast(BF16).rearrange("m (t p e) -> m e p t", t=PACK, e=2),
                )

        v_c = held([P, NP], U32, "v_c")
        v_s = held([P, NP], U8, "v_s")
        wc_w = held([P, H // 2], I32, "wc_w")
        wc_s = held([P, H], U8, "wc_s")
        wc_codes = wc_w[:].bitcast(U8)
        chain = [held([P, PACK, NP], F32, f"chain{b}") for b in range(R_PASSES)]

        early_b = {i: ringed([P, BANK], F32, f"b{i}_then_a", 1) for i in (4, 5)}

        def b_rows(i, lo, n):
            if i in early_b and lo == 0:
                return early_b[i][:]
            return chain[i // PACK][:, i % PACK, lo : lo + n]

        def map_side(banks, copy):
            for i, lo in banks:
                b, t = divmod(i, PACK)
                cols = slice(lo, lo + BANK)
                bank = new_bank()
                nc.tensor.matmul_mx(
                    out=bank[:],
                    lhsT=wk_codes(i).bitcast(FP8X4),
                    lhsT_scale=wk_s[:, i * P : (i + 1) * P],
                    rhs=v_c[:, cols].bitcast(FP8X4),
                    rhs_scale=v_s[:, cols],
                    start=True,
                    stop=False,
                )
                nc.tensor.matmul_mx(
                    out=bank[:],
                    lhsT=wc_codes[:, 2 * P * i : 2 * P * (i + 1)].bitcast(FP4X4),
                    lhsT_scale=wc_s[:, P * i : P * (i + 1)],
                    rhs=v_c[:, cols].bitcast(FP8X4),
                    rhs_scale=v_s[:, cols],
                    start=False,
                    stop=True,
                )
                copy(b_rows(i, lo, BANK), bank[:])

        prec_col = held([P, PACK], F32, "prec_col")
        prec_log = held([P, ROW_TILES], F32, "prec_log")
        prec_bank = bank_at(3)
        nc.tensor.transpose(prec_bank[:, 0:P], prec_rows[:], ident[:])
        nc.scalar.activation(prec_log[:], prec_bank[:, 0:ROW_TILES], ACT.Ln)
        nc.scalar.copy(prec_col[:], prec_bank[:, 0:PACK])
        v_rows = held([P, NP], U8, "v_rows")
        nc.gpsimd.memset(v_s[:].bitcast(I32), 0)
        nc.vector.tensor_copy(v_rows[:], tab_s[:].indirect(list_tab[:]))
        load_scale_rows(v_s, v_rows, nc.gpsimd)
        scatter(0)
        round_w(0)
        wr_bf = [rounded_tile(BANK)]
        turn_w(0, wr_bf[0], nc.scalar.copy, (6, 7))
        quantize(wk_c[:, 0:BANK], wk_s[:, 0:BANK], wk_bf[0])
        scatter(1)
        round_w(1)
        wr_bf.append(rounded_tile(BANK))
        turn_w(1, wr_bf[1], nc.scalar.copy, (4, 5))
        quantize(wk_c[:, BANK:], wk_s[:, BANK : LAST * P], wk_all[:, BANK * PACK : LAST * P * PACK])
        nc.vector.tensor_copy(v_c[:], tab_w[:].bitcast(U32).indirect(list_tab[:]))
        nc.gpsimd.tensor_copy(
            wc_w[:].rearrange("p (b t s x) -> p b t s x", b=R_PASSES, t=PACK, x=RUN // 2),
            wc_w_raw[:].rearrange("p (b s t x) -> p b t s x", b=R_PASSES, t=PACK, x=RUN // 2),
        )
        nc.gpsimd.tensor_copy(
            wc_s[:].bitcast(I32).rearrange("p (b t s x) -> p b t s x", b=R_PASSES, t=PACK, x=RUN // 4),
            wc_s_raw[:].bitcast(I32).rearrange("p (b s t x) -> p b t s x", b=R_PASSES, t=PACK, x=RUN // 4),
        )
        pairs = ringed([P, T * PACK], BF16, "w_pairs_resid", 1)
        round_plane(0, 0, CHUNKS, nc.scalar.copy)
        round_plane(1, 0, CHUNKS, nc.scalar.copy)
        scatter(2)
        banks_of_b = [(i, lo) for i in range(ROW_TILES) for lo in range(0, NP, BANK)]
        map_side(banks_of_b[:-LATE_B], nc.scalar.copy)
        round_plane(2, 0, CHUNKS, nc.scalar.copy)
        scatter(3)
        late_c.append(ringed([P, H + P], U32, "scan_then_wr", 1))
        wr_c = late_c[0][:, 0:H]
        quantize(wk_codes(LAST), wk_s[:, LAST * P :], wk_all[:, LAST * P * PACK :])
        wr_s = held([P, R_PASSES * BANK], U8, "wr_s")
        for b in range(R_PASSES):
            cols = slice(b * BANK, (b + 1) * BANK)
            quantize(wr_c[:, cols], wr_s[:, cols], wr_bf[b][:])
        for c in range(CHUNKS):
            round_plane(3, c, c + 1, nc.scalar.copy)
        map_side(banks_of_b[-LATE_B:], nc.scalar.copy)

        page_c = [held([P, BANK], U32, f"page_c{c}") for c in range(CHUNKS)]
        page_s = [held([P, BANK], U8, f"page_s{c}") for c in range(CHUNKS)]
        woven = []

        def weave(c, copy):
            last = c == CHUNKS - 2
            woven.append(ringed([P, BANK * PACK], BF16, "woven_then_a", 1) if last else rounded_tile(BANK))
            copy(
                woven[c][:].bitcast(F32).rearrange("p (n h) -> p n h", h=2),
                pairs[:].bitcast(F32).rearrange("p (h n) -> p n h", h=2)[:, c * BANK : (c + 1) * BANK],
            )

        weave(0, nc.vector.tensor_copy)
        for c in range(CHUNKS):
            if c + 1 < CHUNKS:
                weave(c + 1, nc.vector.tensor_copy)
            quantize(page_c[c][:], page_s[c][:], woven[c][:])

        a_sb = {}
        resid = [ringed([P, PACK, NP], F32, "w_then_resid", 1), ringed([P, PACK, NP], F32, "w_pairs_resid", 1)]
        g_c = [held([P, NP], U32, f"g_c{b}") for b in range(R_PASSES)]
        g_s = [held([P, NP], U8, f"g_s{b}") for b in range(R_PASSES)]

        def project(i, c, on_vector, x):
            b, t = divmod(i, PACK)
            if i not in a_sb:
                if i == 1:
                    a_sb[i] = ringed([P, T], F32, "woven_then_a", 1)
                elif i == 5:
                    a_sb[i] = ringed([P, T], F32, "table_then_a", 1)
                elif i - 2 in early_b:
                    a_sb[i] = ringed([P, T], F32, f"b{i - 2}_then_a", 1)
                else:
                    a_sb[i] = wide_tile({0: 0, 2: 1, 3: 2, 4: 3}[i])
            bank = bank_at(x)
            nc.tensor.matmul_mx(
                out=bank[:],
                lhsT=wk_codes(i).bitcast(FP8X4),
                lhsT_scale=wk_s[:, i * P : (i + 1) * P],
                rhs=page_c[c][:].bitcast(FP8X4),
                rhs_scale=page_s[c][:],
                start=True,
                stop=True,
            )
            copy = nc.vector.tensor_copy if on_vector else nc.scalar.copy
            copy(a_sb[i][:, c * BANK : (c + 1) * BANK], bank[:])

        def residual(i, lo, n):
            b, t = divmod(i, PACK)
            entries = list_pair[:, lo // PER_COL : (lo + n) // PER_COL]
            nc.vector.tensor_tensor(
                resid[b][:, t, lo : lo + n], a_sb[i][:].indirect(entries), b_rows(i, lo, n), ALU.subtract
            )

        apart = ringed([P, NP], F32, "squares_then_roots", 1)

        def square_rows(i):
            return apart[:] if i == PACK - 1 else chain[i // PACK][:, i % PACK, :]

        def square(i, lo, n, engine):
            b, t = divmod(i, PACK)
            e = resid[b][:, t, lo : lo + n]
            if engine == nc.scalar:
                nc.scalar.activation(square_rows(i)[:, lo : lo + n], e, ACT.Square)
            else:
                engine.tensor_tensor(square_rows(i)[:, lo : lo + n], e, e, ALU.mult)

        def log_denominator(i, lo, n):
            b, t = divmod(i, PACK)
            bias, scale = (1.0, prec_col[:, i : i + 1]) if b == 0 else (roots[1][:, t : t + 1], roots[0][:, t : t + 1])
            nc.scalar.activation(
                chain[b][:, t, lo : lo + n], square_rows(i)[:, lo : lo + n], ACT.Ln, bias=bias, scale=scale
            )

        def weight(b, lo, n, dst, tiles=range(PACK)):
            if b == 1:
                nc.scalar.activation(dst, chain[b][:, :, lo : lo + n], ACT.Exp, scale=-2.0)
                return
            for t in tiles:
                nc.scalar.activation(
                    dst[:, t, :], chain[b][:, t, lo : lo + n], ACT.Exp, bias=prec_log[:, t : t + 1], scale=-2.0
                )

        def product(b, lo, n, weights):
            g_bf = rounded_tile(n)
            nc.vector.tensor_tensor(
                g_bf[:].rearrange("p (c i t) -> p c t i", i=LINE, t=PACK),
                resid[b][:, :, lo : lo + n].rearrange("p t (c i) -> p c t i", i=LINE),
                weights.rearrange("p t (c i) -> p c t i", i=LINE),
                ALU.mult,
            )
            return g_c[b][:, lo : lo + n], g_s[b][:, lo : lo + n], g_bf[:]

        def weigh(parts):
            for operands in [product(*part) for part in parts]:
                quantize(*operands)

        def first_part(lo, n):
            return 0, lo, n, chain[0][:, :, lo : lo + n]

        def second_parts(lo, n):
            width = n // 2
            return [(1, x, width, weights[x]) for x in (lo, lo + width)]

        def back_project(lo, n, per_bank):
            banks = [bank_at(out_banks.pop(0)) for x in range(PACK // per_bank)]
            cols = slice(lo, lo + n)
            for b in range(R_PASSES):
                for j in range(PACK):
                    place = j % per_bank
                    rows = slice(b * BANK + j * P, b * BANK + (j + 1) * P)
                    nc.tensor.matmul_mx(
                        out=banks[j // per_bank][:, place * n : (place + 1) * n],
                        lhsT=wr_c[:, rows].bitcast(FP8X4),
                        lhsT_scale=wr_s[:, rows],
                        rhs=g_c[b][:, cols].bitcast(FP8X4),
                        rhs_scale=g_s[b][:, cols],
                        start=(b == 0 and place == 0),
                        stop=(b == R_PASSES - 1 and place == per_bank - 1),
                    )
            return banks

        def project_chunks(i, on_vector, banks):
            for c in range(CHUNKS - len(banks), CHUNKS):
                project(i, c, on_vector, banks[c - CHUNKS])

        half = NP // 2

        def window(i, banks):
            residual(i, 0, half)
            residual(i, half, half)
            square(i, 0, OWN, nc.vector)
            square(i, OWN, NP - OWN, nc.gpsimd)
            project_chunks(i + 2, True, banks)


        project(0, 0, False, 0)
        project(2, 0, False, 1)
        project(0, 1, False, 2)
        project(1, 0, True, 3)
        project(1, 1, True, 4)
        project(0, 2, False, 0)
        project(0, 3, False, 1)
        residual(0, 0, NP)
        for i, c, x in ((1, 3, 2), (2, 3, 5), (1, 2, 0), (2, 1, 3), (2, 2, 4)):
            project(i, c, False, x)
        square(0, 0, NP, nc.scalar)
        residual(1, 0, NP)
        for c, x in ((3, 6), (0, 1), (1, 2), (2, 5)):
            project(3, c, False, x)
        log_denominator(0, 0, NP)
        residual(2, 0, NP)
        project_chunks(4, False, (0, 3, 4, 7))
        square(1, 0, NP, nc.scalar)
        square(2, 0, NP, nc.scalar)
        window(3, (5, 0, 3, 4))
        for i in (1, 2, 3):
            log_denominator(i, 0, NP)
        for i in (4, 5):
            window(i, (6, 1, 2, 7))
        weight(0, 0, NP, chain[0][:], (0,))
        both = ringed([P, 2, PACK], F32, "squares_then_roots", 1)
        roots = [both[:, 0, :], both[:, 1, :]]
        for root, power in zip(roots, (0.5, -0.5)):
            nc.scalar.activation(root, prec_log[:, PACK:], ACT.Exp, scale=power)
        weight(0, 0, NP, chain[0][:], (1, 2, 3))
        residual(6, 0, NP)
        residual(7, 0, half)
        residual(7, half, half)
        log_denominator(4, 0, NP)
        square(6, 0, NP, nc.scalar)
        log_denominator(5, 0, NP)
        square(7, 0, half, nc.vector)
        square(7, half, half, nc.vector)
        log_denominator(6, 0, NP)
        log_denominator(7, 0, NP)

        ranges = []
        lo = 0
        for n in WIDTHS:
            ranges.append((lo, n))
            lo = lo + n

        spare = [wide_tile(x) for x in (0, 1)]
        weights = {}
        for lo, n in ranges:
            first = PACK * (lo % BANK)
            block = spare[lo // BANK][:, first : first + PACK * n]
            if lo == 0:
                halves = block.rearrange("p (h t n) -> p h t n", h=2, t=PACK)
                weights[lo], weights[lo + n // 2] = halves[:, 0], halves[:, 1]
            else:
                whole = block.rearrange("p (t n) -> p t n", t=PACK)
                weights[lo, n], weights[lo], weights[lo + n // 2] = whole, whole[:, :, : n // 2], whole[:, :, n // 2 :]

        out_banks = [5, 0, 3, 4, 6, 1, 2, 7] * 2
        stage = [wide_tile(2), wide_tile(3)]
        filled = []

        def finish(x):
            lo, n = ranges[x]
            staged = stage[lo // BANK][:, PACK * (lo % BANK) : PACK * (lo % BANK + n)]
            per_bank = PACK // 2
            for first, bank in zip(range(0, PACK, per_bank), back_project(lo, n, per_bank)):
                filled.append((lo, n, first, per_bank, bank, staged))

        def store(copy):
            lo, n, first, per_bank, bank, staged = filled.pop(0)
            part = staged[:, first * n : (first + per_bank) * n]
            copy(part, bank[:, 0 : per_bank * n])
            nc.sync.dma_start(out_v[:, first : first + per_bank, lo : lo + n], part.rearrange("p (j c) -> p j c", c=n))

        behind = []
        for lo, n in ranges[:-1]:
            behind.append(product(*first_part(lo, n)))
            if len(behind) == 2:
                quantize(*behind.pop(0))
        quantize(*behind.pop(0))
        for lo in (0, WIDTHS[0] // 2):
            weight(1, lo, WIDTHS[0] // 2, weights[lo])
        for lo, n in ranges[1:AHEAD]:
            weight(1, lo, n, weights[lo, n])
        for x, (lo, n) in enumerate(ranges):
            weigh(([first_part(lo, n)] if x == len(ranges) - 1 else []) + second_parts(lo, n))
            while filled:
                store(nc.scalar.copy)
            if x == 1:
                weight(1, *ranges[AHEAD], weights[ranges[AHEAD]])
            finish(x)
        store(nc.scalar.copy)
        store(nc.vector.tensor_copy)
